import numpy as np
import ml_dtypes


def mxq(x, axis, fmt="e4m3"):
    dtype, down = {"e4m3": (ml_dtypes.float8_e4m3fn, 7), "e5m2": (ml_dtypes.float8_e5m2, 14)}[fmt]
    v = np.moveaxis(np.asarray(x, np.float32).astype(ml_dtypes.bfloat16).astype(np.float64), axis, -1)
    blocks = v.reshape(v.shape[:-1] + (-1, 32))
    amax = np.abs(blocks).max(-1, keepdims=True)
    byte = np.maximum(np.where(amax > 0, np.frexp(amax)[1] - 1 + 127, 0) - down, 1)
    scale = np.exp2(byte - 127.0)
    codes = (blocks / scale).astype(np.float32).astype(dtype).astype(np.float64)
    return np.moveaxis((codes * scale).reshape(v.shape), -1, axis)


WIDE = False


def mx_kscale(k):
    if not WIDE:
        return np.ones(k)
    levels = np.array([30, -30])
    if k % 512:
        return np.exp2(np.random.permutation(np.resize(levels, k // 32))).repeat(32)
    a = np.empty((k // 512, 16))
    for p in range(k // 512):
        a[p, :8] = np.random.permutation(np.resize(levels, 8))
        for g in range(8):
            far = levels[np.abs(levels - a[p, g]) >= 10]
            a[p, g + 8] = far[np.random.randint(len(far))]
    return np.exp2(a.ravel()).repeat(32)


def f64(x):
    return np.asarray(x).astype(np.float64)


def striped(idx):
    return np.tile(idx.reshape(-1, 16).T, (8, 1)).astype(np.uint16)


def unstriped(offs):
    return offs[:16].T.reshape(-1).astype(np.int64)


def bf(x):
    return np.asarray(x, np.float32).astype(ml_dtypes.bfloat16)


E2M1 = np.array([0.0, 0.5, 1.0, 1.5, 2.0, 3.0, 4.0, 6.0, -0.0, -0.5, -1.0, -1.5, -2.0, -3.0, -4.0, -6.0])


def pack_weight(w, fmt):
    k, n = w.shape
    w = f64(bf(w)).reshape(k // 32, 32, n)
    amax = np.abs(w).max(1)
    if fmt in ("e4m3", "e5m2"):
        byte = np.frexp(amax)[1] - 1 + 127 - (7 if fmt == "e4m3" else 14)
    else:
        mant, ex = np.frexp(amax / 6.0)
        byte = np.where(mant > 0.5, ex, ex - 1) + 127
    byte = np.clip(np.where(amax > 0, byte, 1), 1, 254)
    scaled = (w * np.exp2(127.0 - byte)[:, None, :]).reshape(k, n).astype(np.float32)
    by_word = np.ascontiguousarray(scaled.reshape(k // 512, 128, 4, n).transpose(0, 1, 3, 2))
    if fmt in ("e4m3", "e5m2"):
        words = by_word.astype(ml_dtypes.float8_e4m3fn if fmt == "e4m3" else ml_dtypes.float8_e5m2).view(np.uint8)
    else:
        c = by_word.astype(ml_dtypes.float4_e2m1fn).view(np.uint8) & 0xF
        words = c[..., 0::2] | (c[..., 1::2] << 4)
    return np.ascontiguousarray(words), np.ascontiguousarray(byte.astype(np.uint8).reshape(k // 512, 16, n))


def unpack_weight(words, scales, fmt):
    g, p, n, _ = words.shape
    if fmt in ("e4m3", "e5m2"):
        vals = np.ascontiguousarray(words).view(ml_dtypes.float8_e4m3fn if fmt == "e4m3" else ml_dtypes.float8_e5m2).astype(np.float64)
    else:
        nib = np.empty((g, p, n, 4), np.uint8)
        nib[..., 0::2] = words & 0xF
        nib[..., 1::2] = words >> 4
        vals = E2M1[nib]
    vals = vals * np.repeat(np.exp2(scales.astype(np.float64) - 127.0), 8, axis=1)[..., None]
    return vals.transpose(0, 1, 3, 2).reshape(g * 512, n)


K, H, N, T, S, T2 = 1024, 1536, 512, 2048, 1024, 2048


def setup_inputs():
    n = np.random.standard_normal
    s = mx_kscale(K)[:, None]
    u = mx_kscale(H)[:, None]
    grads = n((K, T)) * np.exp(1.0 * n((1, T))) * s
    tab_words, tab_scales = pack_weight(grads, "e5m2")
    w1 = (n((K, H)) / np.sqrt(K) / s * u.T).astype(np.float32)
    w2_words, w2_scales = pack_weight(1.5 * n((H, N)) / np.sqrt(H) / u, "e4m3")
    return {
        "tab_words": tab_words, "tab_scales": tab_scales,
        "w1": w1,
        "w2_words": w2_words, "w2_scales": w2_scales,
        "sT": (1.2 * n((H, T))).astype(np.float32),
        "wgo": np.exp(0.3 * n((128, S))).astype(np.float32),
        "offs": striped(np.random.permutation(T)[:S]),
        "offs2": striped(np.random.permutation(T2)[:S]),
    }


def reference(tab_words, tab_scales, w1, w2_words, w2_scales, sT, wgo, offs, offs2):
    v = unpack_weight(tab_words, tab_scales, "e5m2")[:, unstriped(offs)]
    s_ = f64(sT)[:, unstriped(offs)]
    h = mxq(f64(w1), 0, "e4m3").T @ v
    sig = 1.0 / (1.0 + np.exp(-s_))
    d = sig * (1.0 + s_ * (1.0 - sig))
    z = h * d
    w2 = unpack_weight(w2_words, w2_scales, "e4m3")
    y = w2.T @ mxq(z, 0, "e4m3")
    out = np.zeros((N, T2))
    out[:, unstriped(offs2)] = np.tile(f64(wgo), (N // 128, 1)) * y
    return out

@@ -1,0 +1,211 @@
+from contextlib import ExitStack
+
+import concourse.mybir as mybir
+
+K, H, N, T, S, T2 = 1024, 1536, 512, 2048, 1024, 2048
+FLOPS = 2 * K * H * S + 2 * H * N * S
+
+F32 = mybir.dt.float32
+BF16 = mybir.dt.bfloat16
+I32 = mybir.dt.int32
+U32 = mybir.dt.uint32
+U16 = mybir.dt.uint16
+U8 = mybir.dt.uint8
+E4M3X4 = mybir.dt.float8_e4m3fn_x4
+E5M2X4 = mybir.dt.float8_e5m2_x4
+ACT = mybir.ActivationFunctionType
+ALU = mybir.AluOpType
+
+P = 128
+PACK = 4
+PASS = P * PACK
+HALF = 512
+K_PASSES = K // PASS
+H_PASSES = H // PASS
+HALVES = S // HALF
+N_TILES = N // P
+LIST_COLS = HALF // 16
+
+
+def tile_list_nack_silu_backward_kernel(tc, tab_words, tab_scales, w1, w2_words, w2_scales, sT, wgo, offs, offs2, out):
+    nc = tc.nc
+    with ExitStack() as ctx:
+        keep = ctx.enter_context(tc.tile_pool(name="keep", bufs=1))
+        stream = ctx.enter_context(tc.tile_pool(name="stream", bufs=8))
+        work = ctx.enter_context(tc.tile_pool(name="work", bufs=2))
+        h_psum = ctx.enter_context(tc.psum_pool(name="h_psum", bufs=6))
+        y_psum = ctx.enter_context(tc.psum_pool(name="y_psum", bufs=2))
+
+        idx = keep.tile([P, S // 16], U16, name="idx")
+        nc.sync.dma_start(idx[:], offs)
+
+        tab_planes = keep.tile([P, T], U8, name="tab_planes", align_bytes=64)
+        v_planes = [keep.tile([P, S], U8, name=f"v_plane{g}", align_bytes=64) for g in range(K_PASSES)]
+        w2_planes = keep.tile([P, N], U8, name="w2_planes", align_bytes=64)
+        nc.vector.memset(tab_planes[:].bitcast(I32), 0)
+        nc.vector.memset(w2_planes[:].bitcast(I32), 0)
+        nc.vector.memset(v_planes[1][:].bitcast(I32), 0)
+        pages = [keep.tile([P, T2], F32, name=f"page{n}") for n in range(N_TILES)]
+        for page in pages:
+            nc.vector.memset(page[:], 0.0)
+
+        v_words = [keep.tile([P, S], U32, name=f"v_words{g}", align_bytes=64) for g in range(K_PASSES)]
+        for g in range(K_PASSES):
+            words = stream.tile([P, T], I32, name="words", tag="load", align_bytes=64)
+            nc.sync.dma_start(out=words[:], in_=tab_words[g].rearrange("p t i -> p (t i)").bitcast(I32))
+            if g == 0:
+                for q in range(4):
+                    nc.sync.dma_start(
+                        out=tab_planes[32 * q : 32 * q + 4 * K_PASSES, :].bitcast(I32),
+                        in_=tab_scales[:, 4 * q : 4 * q + 4, :].bitcast(I32),
+                    )
+            nc.vector.tensor_copy(v_words[g][:], words[:].bitcast(U32).indirect(idx[:]))
+            if g == 0:
+                nc.vector.tensor_copy(v_planes[0][:], tab_planes[:].indirect(idx[:]))
+                nc.scalar.dma_start(out=v_planes[1][0 : P - 4, :].bitcast(I32), in_=v_planes[0][4:P, :].bitcast(I32))
+        for q in range(4):
+            nc.gpsimd.dma_start(
+                out=w2_planes[32 * q : 32 * q + 4 * H_PASSES, :].bitcast(I32),
+                in_=w2_scales[:, 4 * q : 4 * q + 4, :].bitcast(I32),
+            )
+
+        w1_codes = {}
+        w1_planes = {}
+        picked = {}
+        neg_sig = {}
+        z_bf = {}
+        z_codes = {}
+        z_planes = {}
+
+        def prepare_w1(g, a):
+            raw = stream.tile([P, PACK, PASS], F32, name="raw", tag="load", align_bytes=64)
+            nc.sync.dma_start(
+                out=raw[:],
+                in_=w1[g * PASS : (g + 1) * PASS, a * PASS : (a + 1) * PASS].rearrange("(p j) c -> p j c", j=PACK),
+            )
+            grouped = work.tile([P, PACK * PASS], BF16, name="grouped", align_bytes=64)
+            nc.scalar.activation(
+                out=grouped[:].rearrange("p (t m j) -> p m t j", t=PACK, j=PACK),
+                in_=raw[:].rearrange("p j (m t) -> p m t j", t=PACK),
+                func=ACT.Copy,
+            )
+            w1_codes[g, a] = keep.tile([P, PASS], U32, name=f"w1_codes{g}_{a}", align_bytes=64)
+            w1_planes[g, a] = keep.tile([P, PASS], U8, name=f"w1_plane{g}_{a}", align_bytes=64)
+            nc.vector.quantize_mx(out=w1_codes[g, a][:].bitcast(E4M3X4), scales=w1_planes[g, a][:], in_=grouped[:])
+
+        def gather_s(a, t):
+            rows = stream.tile([P, T], F32, name="rows", tag="load", align_bytes=64)
+            nc.sync.dma_start(out=rows[:], in_=sT[a * PASS : (a + 1) * PASS, :].rearrange("(p t) n -> p t n", t=PACK)[:, t, :])
+            for half in range(HALVES):
+                if t == 0:
+                    picked[a, half] = keep.tile([P, PACK, HALF], F32, name=f"picked{a}_{half}")
+                nc.vector.tensor_copy(
+                    picked[a, half][:, t, :], rows[:].indirect(idx[:, half * LIST_COLS : (half + 1) * LIST_COLS])
+                )
+
+        def activations(a, half, t):
+            if t == 0:
+                neg_sig[a, half] = work.tile([P, PACK, HALF], F32, name="neg_sig")
+            s = picked[a, half][:, t, :]
+            nc.scalar.activation(out=neg_sig[a, half][:, t, :], in_=s, func=ACT.Tanh, scale=0.5)
+            nc.scalar.activation(out=s, in_=s, func=ACT.Silu, scale=-1.0)
+            if t == PACK - 1:
+                nc.scalar.activation(out=neg_sig[a, half][:], in_=neg_sig[a, half][:], func=ACT.Copy, scale=-0.5, bias=-0.5)
+
+        def first_product(a, half, t):
+            cols = slice(half * HALF, (half + 1) * HALF)
+            h = h_psum.tile([P, HALF], F32, name="h")
+            for g in range(K_PASSES):
+                nc.tensor.matmul_mx(
+                    out=h[:],
+                    lhsT=w1_codes[g, a][:, t * P : (t + 1) * P].bitcast(E4M3X4),
+                    lhsT_scale=w1_planes[g, a][:, t * P : (t + 1) * P],
+                    rhs=v_words[g][:, cols].bitcast(E5M2X4),
+                    rhs_scale=v_planes[g][:, cols],
+                    start=(g == 0),
+                    stop=(g == K_PASSES - 1),
+                )
+            n = picked[a, half][:, t, :]
+            nc.vector.scalar_tensor_tensor(out=n, in0=n, scalar=1.0, in1=h[:], op0=ALU.subtract, op1=ALU.mult)
+
+        def finish_z(a, half):
+            z_bf[a, half] = work.tile([P, HALF * PACK], BF16, name="z_bf", align_bytes=64)
+            nc.vector.tensor_tensor(
+                out=z_bf[a, half][:].rearrange("p (c i t) -> p c t i", i=2, t=PACK),
+                in0=picked[a, half][:].rearrange("p t (c i) -> p c t i", i=2),
+                in1=neg_sig[a, half][:].rearrange("p t (c i) -> p c t i", i=2),
+                op=ALU.mult,
+            )
+
+        def quantize_z(a, half):
+            z_codes[a, half] = work.tile([P, HALF], U32, name="z_codes", bufs=4, align_bytes=64)
+            z_planes[a, half] = work.tile([P, HALF], U8, name="z_plane", bufs=4, align_bytes=64)
+            nc.vector.quantize_mx(out=z_codes[a, half][:].bitcast(E4M3X4), scales=z_planes[a, half][:], in_=z_bf[a, half][:])
+
+        def second_product(n, half):
+            y = y_psum.tile([P, HALF], F32, name="y")
+            for a in range(H_PASSES):
+                nc.tensor.matmul_mx(
+                    out=y[:],
+                    lhsT=w2_codes[:, a, n * P : (n + 1) * P].bitcast(E4M3X4),
+                    lhsT_scale=w2_planes[4 * a : P, n * P : (n + 1) * P],
+                    rhs=z_codes[a, half][:].bitcast(E4M3X4),
+                    rhs_scale=z_planes[a, half][:],
+                    start=(a == 0),
+                    stop=(a == H_PASSES - 1),
+                )
+            y_sb = work.tile([P, HALF], F32, name="y_sb", bufs=3)
+            nc.scalar.activation(out=y_sb[:], in_=y[:], func=ACT.Copy)
+            nc.vector.tensor_tensor(
+                pages[n][:].indirect(idx2[:, half * LIST_COLS : (half + 1) * LIST_COLS]),
+                y_sb[:],
+                weights[:, half * HALF : (half + 1) * HALF],
+                ALU.mult,
+            )
+            if half == HALVES - 1:
+                nc.sync.dma_start(out=out[n * P : (n + 1) * P, :], in_=pages[n][:])
+
+        for a in range(H_PASSES):
+            for t in range(PACK):
+                gather_s(a, t)
+                if t < K_PASSES:
+                    prepare_w1(t, a)
+                activations(a, 0, t)
+                if a > 0 and t == 0:
+                    for u in range(PACK):
+                        first_product(a - 1, 0, u)
+                if a > 0 and t == 1:
+                    finish_z(a - 1, 0)
+                if a > 0 and t == 2:
+                    quantize_z(a - 1, 0)
+
+        w2_codes = stream.tile([P, H_PASSES, N], I32, name="w2_codes", tag="load", align_bytes=64)
+        nc.sync.dma_start(out=w2_codes[:], in_=w2_words.rearrange("a p c i -> p a (c i)").bitcast(I32))
+        weights = stream.tile([P, S], F32, name="weights", tag="load", align_bytes=64)
+        nc.sync.dma_start(out=weights[:], in_=wgo)
+        idx2 = keep.tile([P, S // 16], U16, name="idx2")
+        nc.sync.dma_start(idx2[:], offs2)
+
+        last = H_PASSES - 1
+        for t in range(PACK):
+            activations(0, 1, t)
+        for t in range(PACK):
+            first_product(last, 0, t)
+        finish_z(last, 0)
+        for t in range(PACK):
+            first_product(0, 1, t)
+        quantize_z(last, 0)
+        finish_z(0, 1)
+        for a in range(1, H_PASSES):
+            for t in range(PACK):
+                activations(a, 1, t)
+            second_product(a - 1, 0)
+            quantize_z(a - 1, 1)
+            for t in range(PACK):
+                first_product(a, 1, t)
+            finish_z(a, 1)
+        second_product(2, 0)
+        quantize_z(last, 1)
+        second_product(3, 0)
+        for n in range(N_TILES):
+            second_product(n, 1)

@@ -39,35 +39,29 @@ def tile_list_nack_silu_backward_kernel(tc, tab_words, tab_scales, w1, w2_words,
         idx = keep.tile([P, S // 16], U16, name="idx")
         nc.sync.dma_start(idx[:], offs)
 
-        tab_planes = keep.tile([P, T], U8, name="tab_planes", align_bytes=64)
+        tab_planes = keep.tile([P, K_PASSES * T], U8, name="tab_planes", align_bytes=64)
         v_planes = [keep.tile([P, S], U8, name=f"v_plane{g}", align_bytes=64) for g in range(K_PASSES)]
         w2_planes = keep.tile([P, N], U8, name="w2_planes", align_bytes=64)
-        nc.vector.memset(tab_planes[:].bitcast(I32), 0)
-        nc.vector.memset(w2_planes[:].bitcast(I32), 0)
-        nc.vector.memset(v_planes[1][:].bitcast(I32), 0)
+        nc.gpsimd.memset(tab_planes[:].bitcast(I32), 0)
+        nc.gpsimd.memset(w2_planes[:].bitcast(I32), 0)
         pages = [keep.tile([P, T2], F32, name=f"page{n}") for n in range(N_TILES)]
         for page in pages:
-            nc.vector.memset(page[:], 0.0)
+            nc.gpsimd.memset(page[:], 0.0)
 
         v_words = [keep.tile([P, S], U32, name=f"v_words{g}", align_bytes=64) for g in range(K_PASSES)]
+        for q in range(4):
+            nc.sync.dma_start(
+                out=tab_planes[32 * q : 32 * q + 4, :].bitcast(I32).rearrange("r (g n) -> r g n", g=K_PASSES),
+                in_=tab_scales[:, 4 * q : 4 * q + 4, :].bitcast(I32).rearrange("g r n -> r g n"),
+            )
         for g in range(K_PASSES):
+            nc.vector.tensor_copy(v_planes[g][:], tab_planes[:, g * T : (g + 1) * T].indirect(idx[:]))
+
+        def gather_table(g):
             words = stream.tile([P, T], I32, name="words", tag="load", align_bytes=64)
             nc.sync.dma_start(out=words[:], in_=tab_words[g].rearrange("p t i -> p (t i)").bitcast(I32))
-            if g == 0:
-                for q in range(4):
-                    nc.sync.dma_start(
-                        out=tab_planes[32 * q : 32 * q + 4 * K_PASSES, :].bitcast(I32),
-                        in_=tab_scales[:, 4 * q : 4 * q + 4, :].bitcast(I32),
-                    )
             nc.vector.tensor_copy(v_words[g][:], words[:].bitcast(U32).indirect(idx[:]))
-            if g == 0:
-                nc.vector.tensor_copy(v_planes[0][:], tab_planes[:].indirect(idx[:]))
-                nc.scalar.dma_start(out=v_planes[1][0 : P - 4, :].bitcast(I32), in_=v_planes[0][4:P, :].bitcast(I32))
-        for q in range(4):
-            nc.gpsimd.dma_start(
-                out=w2_planes[32 * q : 32 * q + 4 * H_PASSES, :].bitcast(I32),
-                in_=w2_scales[:, 4 * q : 4 * q + 4, :].bitcast(I32),
-            )
+
 
         w1_codes = {}
         w1_planes = {}
@@ -105,7 +99,7 @@ def tile_list_nack_silu_backward_kernel(tc, tab_words, tab_scales, w1, w2_words,
 
         def activations(a, half, t):
             if t == 0:
-                neg_sig[a, half] = work.tile([P, PACK, HALF], F32, name="neg_sig")
+                neg_sig[a, half] = work.tile([P, PACK, HALF], F32, name="neg_sig", bufs=3)
             s = picked[a, half][:, t, :]
             nc.scalar.activation(out=neg_sig[a, half][:, t, :], in_=s, func=ACT.Tanh, scale=0.5)
             nc.scalar.activation(out=s, in_=s, func=ACT.Silu, scale=-1.0)
@@ -130,16 +124,19 @@ def tile_list_nack_silu_backward_kernel(tc, tab_words, tab_scales, w1, w2_words,
 
         def finish_z(a, half):
             z_bf[a, half] = work.tile([P, HALF * PACK], BF16, name="z_bf", align_bytes=64)
-            nc.vector.tensor_tensor(
-                out=z_bf[a, half][:].rearrange("p (c i t) -> p c t i", i=2, t=PACK),
-                in0=picked[a, half][:].rearrange("p t (c i) -> p c t i", i=2),
-                in1=neg_sig[a, half][:].rearrange("p t (c i) -> p c t i", i=2),
-                op=ALU.mult,
-            )
+            on_gpsimd = False
+            PIECE = 128 if on_gpsimd else HALF
+            for c0 in range(0, HALF, PIECE):
+                (nc.gpsimd if on_gpsimd else nc.vector).tensor_tensor(
+                    out=z_bf[a, half][:, PACK * c0 : PACK * (c0 + PIECE)].rearrange("p (c i t) -> p c t i", i=2, t=PACK),
+                    in0=picked[a, half][:, :, c0 : c0 + PIECE].rearrange("p t (c i) -> p c t i", i=2),
+                    in1=neg_sig[a, half][:, :, c0 : c0 + PIECE].rearrange("p t (c i) -> p c t i", i=2),
+                    op=ALU.mult,
+                )
 
         def quantize_z(a, half):
-            z_codes[a, half] = work.tile([P, HALF], U32, name="z_codes", bufs=4, align_bytes=64)
-            z_planes[a, half] = work.tile([P, HALF], U8, name="z_plane", bufs=4, align_bytes=64)
+            z_codes[a, half] = work.tile([P, HALF], U32, name="z_codes", bufs=6, align_bytes=64)
+            z_planes[a, half] = work.tile([P, HALF], U8, name="z_plane", bufs=6, align_bytes=64)
             nc.vector.quantize_mx(out=z_codes[a, half][:].bitcast(E4M3X4), scales=z_planes[a, half][:], in_=z_bf[a, half][:])
 
         def second_product(n, half):
@@ -154,58 +151,54 @@ def tile_list_nack_silu_backward_kernel(tc, tab_words, tab_scales, w1, w2_words,
                     start=(a == 0),
                     stop=(a == H_PASSES - 1),
                 )
-            y_sb = work.tile([P, HALF], F32, name="y_sb", bufs=3)
+            y_sb = work.tile([P, HALF], F32, name="y_sb", bufs=4)
             nc.scalar.activation(out=y_sb[:], in_=y[:], func=ACT.Copy)
-            nc.vector.tensor_tensor(
-                pages[n][:].indirect(idx2[:, half * LIST_COLS : (half + 1) * LIST_COLS]),
-                y_sb[:],
-                weights[:, half * HALF : (half + 1) * HALF],
-                ALU.mult,
-            )
+            places = pages[n][:].indirect(idx2[:, half * LIST_COLS : (half + 1) * LIST_COLS])
+            w = weights[:, half * HALF : (half + 1) * HALF]
+            nc.vector.tensor_tensor(places, y_sb[:], w, ALU.mult)
             if half == HALVES - 1:
                 nc.sync.dma_start(out=out[n * P : (n + 1) * P, :], in_=pages[n][:])
 
+        for g in range(K_PASSES):
+            gather_table(g)
+            prepare_w1(g, 0)
         for a in range(H_PASSES):
+            halves = range(HALVES) if a < 3 else range(1)
             for t in range(PACK):
                 gather_s(a, t)
-                if t < K_PASSES:
+                if a > 0 and t < 2:
                     prepare_w1(t, a)
-                activations(a, 0, t)
-                if a > 0 and t == 0:
-                    for u in range(PACK):
-                        first_product(a - 1, 0, u)
-                if a > 0 and t == 1:
-                    finish_z(a - 1, 0)
-                if a > 0 and t == 2:
-                    quantize_z(a - 1, 0)
+                for half in halves:
+                    activations(a, half, t)
+            for half in halves:
+                for t in range(PACK):
+                    first_product(a, half, t)
+                finish_z(a, half)
+                quantize_z(a, half)
 
         w2_codes = stream.tile([P, H_PASSES, N], I32, name="w2_codes", tag="load", align_bytes=64)
         nc.sync.dma_start(out=w2_codes[:], in_=w2_words.rearrange("a p c i -> p a (c i)").bitcast(I32))
+        for q in range(4):
+            nc.sync.dma_start(
+                out=w2_planes[32 * q : 32 * q + 4 * H_PASSES, :].bitcast(I32),
+                in_=w2_scales[:, 4 * q : 4 * q + 4, :].bitcast(I32),
+            )
         weights = stream.tile([P, S], F32, name="weights", tag="load", align_bytes=64)
         nc.sync.dma_start(out=weights[:], in_=wgo)
         idx2 = keep.tile([P, S // 16], U16, name="idx2")
         nc.sync.dma_start(idx2[:], offs2)
 
-        last = H_PASSES - 1
-        for t in range(PACK):
-            activations(0, 1, t)
-        for t in range(PACK):
-            first_product(last, 0, t)
-        finish_z(last, 0)
-        for t in range(PACK):
-            first_product(0, 1, t)
-        quantize_z(last, 0)
-        finish_z(0, 1)
-        for a in range(1, H_PASSES):
+        done = 0
+        for a in range(3, H_PASSES):
             for t in range(PACK):
                 activations(a, 1, t)
-            second_product(a - 1, 0)
-            quantize_z(a - 1, 1)
-            for t in range(PACK):
                 first_product(a, 1, t)
             finish_z(a, 1)
-        second_product(2, 0)
-        quantize_z(last, 1)
-        second_product(3, 0)
+            if a >= 0:
+                second_product(done, 0)
+                done = done + 1
+            quantize_z(a, 1)
+        for n in range(done, N_TILES):
+            second_product(n, 0)
         for n in range(N_TILES):
             second_product(n, 1)

@@ -83,8 +83,8 @@ def tile_list_nack_silu_backward_kernel(tc, tab_words, tab_scales, w1, w2_words,
                 in_=raw[:].rearrange("p j (m t) -> p m t j", t=PACK),
                 func=ACT.Copy,
             )
-            w1_codes[g, a] = keep.tile([P, PASS], U32, name=f"w1_codes{g}_{a}", align_bytes=64)
-            w1_planes[g, a] = keep.tile([P, PASS], U8, name=f"w1_plane{g}_{a}", align_bytes=64)
+            w1_codes[g, a] = keep.tile([P, PASS], U32, name="w1_codes", tag=f"codes{g}_{a}", align_bytes=64)
+            w1_planes[g, a] = keep.tile([P, PASS], U8, name="w1_plane", tag=f"plane{g}_{a}", align_bytes=64)
             nc.vector.quantize_mx(out=w1_codes[g, a][:].bitcast(E4M3X4), scales=w1_planes[g, a][:], in_=grouped[:])
 
         def gather_s(a, t):
@@ -99,7 +99,7 @@ def tile_list_nack_silu_backward_kernel(tc, tab_words, tab_scales, w1, w2_words,
 
         def activations(a, half, t):
             if t == 0:
-                neg_sig[a, half] = work.tile([P, PACK, HALF], F32, name="neg_sig", bufs=3)
+                neg_sig[a, half] = work.tile([P, PACK, HALF], F32, name="neg_sig", bufs=4)
             s = picked[a, half][:, t, :]
             nc.scalar.activation(out=neg_sig[a, half][:, t, :], in_=s, func=ACT.Tanh, scale=0.5)
             nc.scalar.activation(out=s, in_=s, func=ACT.Silu, scale=-1.0)
@@ -123,8 +123,8 @@ def tile_list_nack_silu_backward_kernel(tc, tab_words, tab_scales, w1, w2_words,
             nc.vector.scalar_tensor_tensor(out=n, in0=n, scalar=1.0, in1=h[:], op0=ALU.subtract, op1=ALU.mult)
 
         def finish_z(a, half):
-            z_bf[a, half] = work.tile([P, HALF * PACK], BF16, name="z_bf", align_bytes=64)
-            on_gpsimd = False
+            z_bf[a, half] = work.tile([P, HALF * PACK], BF16, name="z_bf", bufs=4, align_bytes=64)
+            on_gpsimd = a < 2
             PIECE = 128 if on_gpsimd else HALF
             for c0 in range(0, HALF, PIECE):
                 (nc.gpsimd if on_gpsimd else nc.vector).tensor_tensor(
@@ -135,8 +135,8 @@ def tile_list_nack_silu_backward_kernel(tc, tab_words, tab_scales, w1, w2_words,
                 )
 
         def quantize_z(a, half):
-            z_codes[a, half] = work.tile([P, HALF], U32, name="z_codes", bufs=6, align_bytes=64)
-            z_planes[a, half] = work.tile([P, HALF], U8, name="z_plane", bufs=6, align_bytes=64)
+            z_codes[a, half] = keep.tile([P, HALF], U32, name="z_codes", tag=f"codes{half}_{(a + 1) % H_PASSES}", align_bytes=64)
+            z_planes[a, half] = keep.tile([P, HALF], U8, name="z_plane", tag=f"plane{half}_{(a + 1) % H_PASSES}", align_bytes=64)
             nc.vector.quantize_mx(out=z_codes[a, half][:].bitcast(E4M3X4), scales=z_planes[a, half][:], in_=z_bf[a, half][:])
 
         def second_product(n, half):
@@ -174,7 +174,11 @@ def tile_list_nack_silu_backward_kernel(tc, tab_words, tab_scales, w1, w2_words,
                 for t in range(PACK):
                     first_product(a, half, t)
                 finish_z(a, half)
-                quantize_z(a, half)
+            for half in halves:
+                if a > 0:
+                    quantize_z(a - 1, half)
+        for half in range(HALVES):
+            quantize_z(H_PASSES - 1, half)
 
         w2_codes = stream.tile([P, H_PASSES, N], I32, name="w2_codes", tag="load", align_bytes=64)
         nc.sync.dma_start(out=w2_codes[:], in_=w2_words.rearrange("a p c i -> p a (c i)").bitcast(I32))

@@ -19,22 +19,32 @@ ALU = mybir.AluOpType
 P = 128
 PACK = 4
 PASS = P * PACK
+QUADRANTS = 4
 HALF = 512
 K_PASSES = K // PASS
 H_PASSES = H // PASS
 HALVES = S // HALF
 N_TILES = N // P
 LIST_COLS = HALF // 16
+LAST = H_PASSES - 1
+
+LOAD_BUFS = 8
+H_BANKS = 6
+SIG_BUFS = 4
+Z_BUFS = 4
+Y_BUFS = 4
+GPSIMD_PIECE = 128
+ODD_SPLIT = T2 // 2 + 1
 
 
 def tile_list_nack_silu_backward_kernel(tc, tab_words, tab_scales, w1, w2_words, w2_scales, sT, wgo, offs, offs2, out):
     nc = tc.nc
     with ExitStack() as ctx:
         keep = ctx.enter_context(tc.tile_pool(name="keep", bufs=1))
-        stream = ctx.enter_context(tc.tile_pool(name="stream", bufs=8))
+        stream = ctx.enter_context(tc.tile_pool(name="stream", bufs=LOAD_BUFS))
         work = ctx.enter_context(tc.tile_pool(name="work", bufs=2))
-        h_psum = ctx.enter_context(tc.psum_pool(name="h_psum", bufs=6))
-        y_psum = ctx.enter_context(tc.psum_pool(name="y_psum", bufs=2))
+        h_psum = ctx.enter_context(tc.psum_pool(name="h_psum", bufs=H_BANKS))
+        y_psum = ctx.enter_context(tc.psum_pool(name="y_psum", bufs=8 - H_BANKS))
 
         idx = keep.tile([P, S // 16], U16, name="idx")
         nc.sync.dma_start(idx[:], offs)
@@ -44,24 +54,22 @@ def tile_list_nack_silu_backward_kernel(tc, tab_words, tab_scales, w1, w2_words,
         w2_planes = keep.tile([P, N], U8, name="w2_planes", align_bytes=64)
         nc.gpsimd.memset(tab_planes[:].bitcast(I32), 0)
         nc.gpsimd.memset(w2_planes[:].bitcast(I32), 0)
+
         pages = [keep.tile([P, T2], F32, name=f"page{n}") for n in range(N_TILES)]
-        for page in pages:
+        for page in pages[: N_TILES // 2]:
             nc.gpsimd.memset(page[:], 0.0)
+        for page in pages[N_TILES // 2 :]:
+            nc.vector.memset(page[:, :ODD_SPLIT], 0.0)
+            nc.vector.memset(page[:, ODD_SPLIT:], 0.0)
 
         v_words = [keep.tile([P, S], U32, name=f"v_words{g}", align_bytes=64) for g in range(K_PASSES)]
-        for q in range(4):
+        for q in range(QUADRANTS):
             nc.sync.dma_start(
                 out=tab_planes[32 * q : 32 * q + 4, :].bitcast(I32).rearrange("r (g n) -> r g n", g=K_PASSES),
                 in_=tab_scales[:, 4 * q : 4 * q + 4, :].bitcast(I32).rearrange("g r n -> r g n"),
             )
         for g in range(K_PASSES):
             nc.vector.tensor_copy(v_planes[g][:], tab_planes[:, g * T : (g + 1) * T].indirect(idx[:]))
-
-        def gather_table(g):
-            words = stream.tile([P, T], I32, name="words", tag="load", align_bytes=64)
-            nc.sync.dma_start(out=words[:], in_=tab_words[g].rearrange("p t i -> p (t i)").bitcast(I32))
-            nc.vector.tensor_copy(v_words[g][:], words[:].bitcast(U32).indirect(idx[:]))
-
 
         w1_codes = {}
         w1_planes = {}
@@ -70,6 +78,11 @@ def tile_list_nack_silu_backward_kernel(tc, tab_words, tab_scales, w1, w2_words,
         z_bf = {}
         z_codes = {}
         z_planes = {}
+
+        def gather_table(g):
+            words = stream.tile([P, T], I32, name="words", tag="load", align_bytes=64)
+            nc.sync.dma_start(out=words[:], in_=tab_words[g].rearrange("p t i -> p (t i)").bitcast(I32))
+            nc.vector.tensor_copy(v_words[g][:], words[:].bitcast(U32).indirect(idx[:]))
 
         def prepare_w1(g, a):
             raw = stream.tile([P, PACK, PASS], F32, name="raw", tag="load", align_bytes=64)
@@ -99,7 +112,7 @@ def tile_list_nack_silu_backward_kernel(tc, tab_words, tab_scales, w1, w2_words,
 
         def activations(a, half, t):
             if t == 0:
-                neg_sig[a, half] = work.tile([P, PACK, HALF], F32, name="neg_sig", bufs=4)
+                neg_sig[a, half] = work.tile([P, PACK, HALF], F32, name="neg_sig", bufs=SIG_BUFS)
             s = picked[a, half][:, t, :]
             nc.scalar.activation(out=neg_sig[a, half][:, t, :], in_=s, func=ACT.Tanh, scale=0.5)
             nc.scalar.activation(out=s, in_=s, func=ACT.Silu, scale=-1.0)
@@ -119,24 +132,24 @@ def tile_list_nack_silu_backward_kernel(tc, tab_words, tab_scales, w1, w2_words,
                     start=(g == 0),
                     stop=(g == K_PASSES - 1),
                 )
-            n = picked[a, half][:, t, :]
-            nc.vector.scalar_tensor_tensor(out=n, in0=n, scalar=1.0, in1=h[:], op0=ALU.subtract, op1=ALU.mult)
+            silu_neg = picked[a, half][:, t, :]
+            nc.vector.scalar_tensor_tensor(out=silu_neg, in0=silu_neg, scalar=1.0, in1=h[:], op0=ALU.subtract, op1=ALU.mult)
 
         def finish_z(a, half):
-            z_bf[a, half] = work.tile([P, HALF * PACK], BF16, name="z_bf", bufs=4, align_bytes=64)
-            on_gpsimd = a < 2
-            PIECE = 128 if on_gpsimd else HALF
-            for c0 in range(0, HALF, PIECE):
-                (nc.gpsimd if on_gpsimd else nc.vector).tensor_tensor(
-                    out=z_bf[a, half][:, PACK * c0 : PACK * (c0 + PIECE)].rearrange("p (c i t) -> p c t i", i=2, t=PACK),
-                    in0=picked[a, half][:, :, c0 : c0 + PIECE].rearrange("p t (c i) -> p c t i", i=2),
-                    in1=neg_sig[a, half][:, :, c0 : c0 + PIECE].rearrange("p t (c i) -> p c t i", i=2),
+            z_bf[a, half] = work.tile([P, HALF * PACK], BF16, name="z_bf", bufs=Z_BUFS, align_bytes=64)
+            engine, piece = (nc.gpsimd, GPSIMD_PIECE) if a < LAST else (nc.vector, HALF)
+            for c0 in range(0, HALF, piece):
+                engine.tensor_tensor(
+                    out=z_bf[a, half][:, PACK * c0 : PACK * (c0 + piece)].rearrange("p (c i t) -> p c t i", i=2, t=PACK),
+                    in0=picked[a, half][:, :, c0 : c0 + piece].rearrange("p t (c i) -> p c t i", i=2),
+                    in1=neg_sig[a, half][:, :, c0 : c0 + piece].rearrange("p t (c i) -> p c t i", i=2),
                     op=ALU.mult,
                 )
 
         def quantize_z(a, half):
-            z_codes[a, half] = keep.tile([P, HALF], U32, name="z_codes", tag=f"codes{half}_{(a + 1) % H_PASSES}", align_bytes=64)
-            z_planes[a, half] = keep.tile([P, HALF], U8, name="z_plane", tag=f"plane{half}_{(a + 1) % H_PASSES}", align_bytes=64)
+            tenant = f"{half}_{(a + 1) % H_PASSES}"
+            z_codes[a, half] = keep.tile([P, HALF], U32, name="z_codes", tag="codes" + tenant, align_bytes=64)
+            z_planes[a, half] = keep.tile([P, HALF], U8, name="z_plane", tag="plane" + tenant, align_bytes=64)
             nc.vector.quantize_mx(out=z_codes[a, half][:].bitcast(E4M3X4), scales=z_planes[a, half][:], in_=z_bf[a, half][:])
 
         def second_product(n, half):
@@ -149,13 +162,12 @@ def tile_list_nack_silu_backward_kernel(tc, tab_words, tab_scales, w1, w2_words,
                     rhs=z_codes[a, half][:].bitcast(E4M3X4),
                     rhs_scale=z_planes[a, half][:],
                     start=(a == 0),
-                    stop=(a == H_PASSES - 1),
+                    stop=(a == LAST),
                 )
-            y_sb = work.tile([P, HALF], F32, name="y_sb", bufs=4)
+            y_sb = work.tile([P, HALF], F32, name="y_sb", bufs=Y_BUFS)
             nc.scalar.activation(out=y_sb[:], in_=y[:], func=ACT.Copy)
             places = pages[n][:].indirect(idx2[:, half * LIST_COLS : (half + 1) * LIST_COLS])
-            w = weights[:, half * HALF : (half + 1) * HALF]
-            nc.vector.tensor_tensor(places, y_sb[:], w, ALU.mult)
+            nc.vector.tensor_tensor(places, y_sb[:], weights[:, half * HALF : (half + 1) * HALF], ALU.mult)
             if half == HALVES - 1:
                 nc.sync.dma_start(out=out[n * P : (n + 1) * P, :], in_=pages[n][:])
 
@@ -163,26 +175,25 @@ def tile_list_nack_silu_backward_kernel(tc, tab_words, tab_scales, w1, w2_words,
             gather_table(g)
             prepare_w1(g, 0)
         for a in range(H_PASSES):
-            halves = range(HALVES) if a < 3 else range(1)
             for t in range(PACK):
                 gather_s(a, t)
-                if a > 0 and t < 2:
+                if a > 0 and t < K_PASSES:
                     prepare_w1(t, a)
-                for half in halves:
+                for half in range(HALVES):
                     activations(a, half, t)
-            for half in halves:
+            for half in range(HALVES):
                 for t in range(PACK):
                     first_product(a, half, t)
                 finish_z(a, half)
-            for half in halves:
-                if a > 0:
+            if a > 0:
+                for half in range(HALVES):
                     quantize_z(a - 1, half)
         for half in range(HALVES):
-            quantize_z(H_PASSES - 1, half)
+            quantize_z(LAST, half)
 
         w2_codes = stream.tile([P, H_PASSES, N], I32, name="w2_codes", tag="load", align_bytes=64)
         nc.sync.dma_start(out=w2_codes[:], in_=w2_words.rearrange("a p c i -> p a (c i)").bitcast(I32))
-        for q in range(4):
+        for q in range(QUADRANTS):
             nc.sync.dma_start(
                 out=w2_planes[32 * q : 32 * q + 4 * H_PASSES, :].bitcast(I32),
                 in_=w2_scales[:, 4 * q : 4 * q + 4, :].bitcast(I32),
@@ -192,17 +203,6 @@ def tile_list_nack_silu_backward_kernel(tc, tab_words, tab_scales, w1, w2_words,
         idx2 = keep.tile([P, S // 16], U16, name="idx2")
         nc.sync.dma_start(idx2[:], offs2)
 
-        done = 0
-        for a in range(3, H_PASSES):
-            for t in range(PACK):
-                activations(a, 1, t)
-                first_product(a, 1, t)
-            finish_z(a, 1)
-            if a >= 0:
-                second_product(done, 0)
-                done = done + 1
-            quantize_z(a, 1)
-        for n in range(done, N_TILES):
-            second_product(n, 0)
-        for n in range(N_TILES):
-            second_product(n, 1)
+        for half in range(HALVES):
+            for n in range(N_TILES):
+                second_product(n, half)

@@ -28,13 +28,16 @@ N_TILES = N // P
 LIST_COLS = HALF // 16
 LAST = H_PASSES - 1
 
-LOAD_BUFS = 8
-H_BANKS = 6
-SIG_BUFS = 4
-Z_BUFS = 4
-Y_BUFS = 4
-GPSIMD_PIECE = 128
-ODD_SPLIT = T2 // 2 + 1
+SLICES = H // P
+PAIR = 2
+PAIRS = SLICES // PAIR
+LOAD_BUFS = 6
+H_BANKS = 4
+PICKED_BUFS = 4
+TANH_BUFS = 3
+GPSIMD_PIECE = 256
+ROW_TAGS = (0, 1, 2, 3, 4, 5, 6, 7, 0, 1, 3, 5)
+GPSIMD_SHIFTS = (0, 1, 2, 4, 6)
 
 
 def tile_list_nack_silu_backward_kernel(tc, tab_words, tab_scales, w1, w2_words, w2_scales, sT, wgo, offs, offs2, out):
@@ -42,7 +45,7 @@ def tile_list_nack_silu_backward_kernel(tc, tab_words, tab_scales, w1, w2_words,
     with ExitStack() as ctx:
         keep = ctx.enter_context(tc.tile_pool(name="keep", bufs=1))
         stream = ctx.enter_context(tc.tile_pool(name="stream", bufs=LOAD_BUFS))
-        work = ctx.enter_context(tc.tile_pool(name="work", bufs=2))
+        work = ctx.enter_context(tc.tile_pool(name="work", bufs=TANH_BUFS))
         h_psum = ctx.enter_context(tc.psum_pool(name="h_psum", bufs=H_BANKS))
         y_psum = ctx.enter_context(tc.psum_pool(name="y_psum", bufs=8 - H_BANKS))
 
@@ -56,11 +59,8 @@ def tile_list_nack_silu_backward_kernel(tc, tab_words, tab_scales, w1, w2_words,
         nc.gpsimd.memset(w2_planes[:].bitcast(I32), 0)
 
         pages = [keep.tile([P, T2], F32, name=f"page{n}") for n in range(N_TILES)]
-        for page in pages[: N_TILES // 2]:
+        for page in pages:
             nc.gpsimd.memset(page[:], 0.0)
-        for page in pages[N_TILES // 2 :]:
-            nc.vector.memset(page[:, :ODD_SPLIT], 0.0)
-            nc.vector.memset(page[:, ODD_SPLIT:], 0.0)
 
         v_words = [keep.tile([P, S], U32, name=f"v_words{g}", align_bytes=64) for g in range(K_PASSES)]
         for q in range(QUADRANTS):
@@ -68,137 +68,182 @@ def tile_list_nack_silu_backward_kernel(tc, tab_words, tab_scales, w1, w2_words,
                 out=tab_planes[32 * q : 32 * q + 4, :].bitcast(I32).rearrange("r (g n) -> r g n", g=K_PASSES),
                 in_=tab_scales[:, 4 * q : 4 * q + 4, :].bitcast(I32).rearrange("g r n -> r g n"),
             )
-        for g in range(K_PASSES):
-            nc.vector.tensor_copy(v_planes[g][:], tab_planes[:, g * T : (g + 1) * T].indirect(idx[:]))
 
+        grouped = {}
         w1_codes = {}
         w1_planes = {}
         picked = {}
-        neg_sig = {}
+        neg_tanh = {}
+        scaled_h = {}
         z_bf = {}
+        z_pairs = {}
         z_codes = {}
         z_planes = {}
+
+        def row_tag(i):
+            return f"rows{ROW_TAGS[i]}"
+
+        def picked_tag(i):
+            return f"picked{i % PICKED_BUFS}"
 
         def gather_table(g):
             words = stream.tile([P, T], I32, name="words", tag="load", align_bytes=64)
             nc.sync.dma_start(out=words[:], in_=tab_words[g].rearrange("p t i -> p (t i)").bitcast(I32))
             nc.vector.tensor_copy(v_words[g][:], words[:].bitcast(U32).indirect(idx[:]))
 
-        def prepare_w1(g, a):
+        def round_w1(g, a):
             raw = stream.tile([P, PACK, PASS], F32, name="raw", tag="load", align_bytes=64)
             nc.sync.dma_start(
                 out=raw[:],
                 in_=w1[g * PASS : (g + 1) * PASS, a * PASS : (a + 1) * PASS].rearrange("(p j) c -> p j c", j=PACK),
             )
-            grouped = work.tile([P, PACK * PASS], BF16, name="grouped", align_bytes=64)
+            if g == 0:
+                grouped[a] = keep.tile([P, K_PASSES * PACK * PASS], BF16, name="grouped", tag="grouped", align_bytes=64)
             nc.scalar.activation(
-                out=grouped[:].rearrange("p (t m j) -> p m t j", t=PACK, j=PACK),
-                in_=raw[:].rearrange("p j (m t) -> p m t j", t=PACK),
+                out=grouped[a][:, g * PACK * PASS : (g + 1) * PACK * PASS].rearrange("p (t m j) -> p m j t", t=PACK, j=PACK),
+                in_=raw[:].rearrange("p j (m t) -> p m j t", t=PACK),
                 func=ACT.Copy,
             )
-            w1_codes[g, a] = keep.tile([P, PASS], U32, name="w1_codes", tag=f"codes{g}_{a}", align_bytes=64)
-            w1_planes[g, a] = keep.tile([P, PASS], U8, name="w1_plane", tag=f"plane{g}_{a}", align_bytes=64)
-            nc.vector.quantize_mx(out=w1_codes[g, a][:].bitcast(E4M3X4), scales=w1_planes[g, a][:], in_=grouped[:])
 
-        def gather_s(a, t):
-            rows = stream.tile([P, T], F32, name="rows", tag="load", align_bytes=64)
+        def quantize_w1(a):
+            tag = row_tag(PACK * a) if a > 0 else "codes"
+            w1_codes[a] = keep.tile([P, K_PASSES * PASS], U32, name="w1_codes", tag=tag, align_bytes=64)
+            w1_planes[a] = keep.tile([P, K_PASSES * PASS], U8, name="w1_plane", tag=f"plane{a}", align_bytes=64)
+            nc.vector.quantize_mx(out=w1_codes[a][:].bitcast(E4M3X4), scales=w1_planes[a][:], in_=grouped[a][:])
+
+        def gather_s(i):
+            a, t = divmod(i, PACK)
+            u, e = divmod(i, PAIR)
+            rows = keep.tile([P, T], F32, name="rows", tag=row_tag(i), align_bytes=64)
             nc.sync.dma_start(out=rows[:], in_=sT[a * PASS : (a + 1) * PASS, :].rearrange("(p t) n -> p t n", t=PACK)[:, t, :])
-            for half in range(HALVES):
-                if t == 0:
-                    picked[a, half] = keep.tile([P, PACK, HALF], F32, name=f"picked{a}_{half}")
-                nc.vector.tensor_copy(
-                    picked[a, half][:, t, :], rows[:].indirect(idx[:, half * LIST_COLS : (half + 1) * LIST_COLS])
-                )
-
-        def activations(a, half, t):
-            if t == 0:
-                neg_sig[a, half] = work.tile([P, PACK, HALF], F32, name="neg_sig", bufs=SIG_BUFS)
-            s = picked[a, half][:, t, :]
-            nc.scalar.activation(out=neg_sig[a, half][:, t, :], in_=s, func=ACT.Tanh, scale=0.5)
+            if e == 0:
+                neg_tanh[u] = work.tile([P, PAIR, S], F32, name="neg_tanh", tag="tanh", align_bytes=64)
+            picked[i] = keep.tile([P, S], F32, name="picked", tag=picked_tag(i), align_bytes=64)
+            s = picked[i][:]
+            nc.vector.tensor_copy(s, rows[:].indirect(idx[:]))
+            nc.scalar.activation(out=neg_tanh[u][:, e, :], in_=s, func=ACT.Tanh, scale=-0.5)
             nc.scalar.activation(out=s, in_=s, func=ACT.Silu, scale=-1.0)
-            if t == PACK - 1:
-                nc.scalar.activation(out=neg_sig[a, half][:], in_=neg_sig[a, half][:], func=ACT.Copy, scale=-0.5, bias=-0.5)
+            if i in GPSIMD_SHIFTS:
+                nc.gpsimd.tensor_scalar(neg_tanh[u][:, e, :], neg_tanh[u][:, e, :], 1.0, -1.0, ALU.mult, ALU.add)
+            elif u < PAIRS - 1:
+                nc.scalar.activation(out=neg_tanh[u][:, e, :], in_=neg_tanh[u][:, e, :], func=ACT.Copy, bias=-1.0)
 
-        def first_product(a, half, t):
-            cols = slice(half * HALF, (half + 1) * HALF)
-            h = h_psum.tile([P, HALF], F32, name="h")
-            for g in range(K_PASSES):
-                nc.tensor.matmul_mx(
-                    out=h[:],
-                    lhsT=w1_codes[g, a][:, t * P : (t + 1) * P].bitcast(E4M3X4),
-                    lhsT_scale=w1_planes[g, a][:, t * P : (t + 1) * P],
-                    rhs=v_words[g][:, cols].bitcast(E5M2X4),
-                    rhs_scale=v_planes[g][:, cols],
-                    start=(g == 0),
-                    stop=(g == K_PASSES - 1),
+        def first_product(i):
+            a, t = divmod(i, PACK)
+            u, e = divmod(i, PAIR)
+            if e == 0:
+                tag = "grouped" if a < LAST and t > 0 else row_tag(min(i + PAIR, SLICES - 1))
+                scaled_h[u] = keep.tile([P, PAIR, S], F32, name="scaled_h", tag=tag, align_bytes=64)
+            for half in range(HALVES):
+                cols = slice(half * HALF, (half + 1) * HALF)
+                h = h_psum.tile([P, HALF], F32, name="h")
+                for g in range(K_PASSES):
+                    w_cols = slice(g * PASS + t * P, g * PASS + (t + 1) * P)
+                    nc.tensor.matmul_mx(
+                        out=h[:],
+                        lhsT=w1_codes[a][:, w_cols].bitcast(E4M3X4),
+                        lhsT_scale=w1_planes[a][:, w_cols],
+                        rhs=v_words[g][:, cols].bitcast(E5M2X4),
+                        rhs_scale=v_planes[g][:, cols],
+                        start=(g == 0),
+                        stop=(g == K_PASSES - 1),
+                    )
+                nc.vector.scalar_tensor_tensor(
+                    out=scaled_h[u][:, e, cols], in0=picked[i][:, cols], scalar=1.0, in1=h[:], op0=ALU.subtract, op1=ALU.mult
                 )
-            silu_neg = picked[a, half][:, t, :]
-            nc.vector.scalar_tensor_tensor(out=silu_neg, in0=silu_neg, scalar=1.0, in1=h[:], op0=ALU.subtract, op1=ALU.mult)
 
-        def finish_z(a, half):
-            z_bf[a, half] = work.tile([P, HALF * PACK], BF16, name="z_bf", bufs=Z_BUFS, align_bytes=64)
-            engine, piece = (nc.gpsimd, GPSIMD_PIECE) if a < LAST else (nc.vector, HALF)
-            for c0 in range(0, HALF, piece):
-                engine.tensor_tensor(
-                    out=z_bf[a, half][:, PACK * c0 : PACK * (c0 + piece)].rearrange("p (c i t) -> p c t i", i=2, t=PACK),
-                    in0=picked[a, half][:, :, c0 : c0 + piece].rearrange("p t (c i) -> p c t i", i=2),
-                    in1=neg_sig[a, half][:, :, c0 : c0 + piece].rearrange("p t (c i) -> p c t i", i=2),
-                    op=ALU.mult,
-                )
+        def finish_pair(u):
+            a, w = divmod(u, PACK // PAIR)
+            if a < LAST and w == 0:
+                z_bf[a] = keep.tile([P, S * PACK], BF16, name=f"z_bf{a}", align_bytes=64)
+            if a == LAST and w == 0:
+                for half in range(HALVES):
+                    z_pairs[half] = keep.tile([P, PACK // PAIR, HALF * PAIR], BF16, name=f"z_pairs{half}", align_bytes=64)
+            piece = GPSIMD_PIECE if u < PAIRS - 1 else HALF
+            for c0 in range(0, S, piece):
+                if a < LAST:
+                    z = z_bf[a][:].rearrange("p (c t) -> p c t", t=PACK)[:, c0 : c0 + piece, PAIR * w : PAIR * (w + 1)]
+                else:
+                    half, c1 = divmod(c0, HALF)
+                    z = z_pairs[half][:, w, PAIR * c1 : PAIR * (c1 + piece)].rearrange("p (c e) -> p c e", e=PAIR)
+                left = neg_tanh[u][:, :, c0 : c0 + piece].rearrange("p e c -> p c e")
+                right = scaled_h[u][:, :, c0 : c0 + piece].rearrange("p e c -> p c e")
+                if u < PAIRS - 1:
+                    nc.gpsimd.tensor_tensor(out=z, in0=left, in1=right, op=ALU.mult)
+                else:
+                    nc.vector.scalar_tensor_tensor(out=z, in0=left, scalar=1.0, in1=right, op0=ALU.subtract, op1=ALU.mult)
 
-        def quantize_z(a, half):
-            tenant = f"{half}_{(a + 1) % H_PASSES}"
-            z_codes[a, half] = keep.tile([P, HALF], U32, name="z_codes", tag="codes" + tenant, align_bytes=64)
-            z_planes[a, half] = keep.tile([P, HALF], U8, name="z_plane", tag="plane" + tenant, align_bytes=64)
-            nc.vector.quantize_mx(out=z_codes[a, half][:].bitcast(E4M3X4), scales=z_planes[a, half][:], in_=z_bf[a, half][:])
+        def quantize_z(a, c0, c1):
+            nc.vector.quantize_mx(
+                out=z_codes[a][:, c0:c1].bitcast(E4M3X4), scales=z_planes[a][:, c0:c1], in_=z_bf[a][:, PACK * c0 : PACK * c1]
+            )
 
         def second_product(n, half):
+            cols = slice(half * HALF, (half + 1) * HALF)
             y = y_psum.tile([P, HALF], F32, name="y")
             for a in range(H_PASSES):
                 nc.tensor.matmul_mx(
                     out=y[:],
                     lhsT=w2_codes[:, a, n * P : (n + 1) * P].bitcast(E4M3X4),
                     lhsT_scale=w2_planes[4 * a : P, n * P : (n + 1) * P],
-                    rhs=z_codes[a, half][:].bitcast(E4M3X4),
-                    rhs_scale=z_planes[a, half][:],
+                    rhs=z_codes[a][:, cols].bitcast(E4M3X4),
+                    rhs_scale=z_planes[a][:, cols],
                     start=(a == 0),
                     stop=(a == LAST),
                 )
-            y_sb = work.tile([P, HALF], F32, name="y_sb", bufs=Y_BUFS)
-            nc.scalar.activation(out=y_sb[:], in_=y[:], func=ACT.Copy)
+            y_sb = work.tile([P, HALF], F32, name="y_sb", tag="tanh", align_bytes=64)
+            nc.scalar.activation(out=y_sb[:], in_=y[:], func=ACT.Copy, scale=0.5)
             places = pages[n][:].indirect(idx2[:, half * LIST_COLS : (half + 1) * LIST_COLS])
-            nc.vector.tensor_tensor(places, y_sb[:], weights[:, half * HALF : (half + 1) * HALF], ALU.mult)
+            nc.vector.tensor_tensor(places, y_sb[:], weights[:, cols], ALU.mult)
             if half == HALVES - 1:
                 nc.sync.dma_start(out=out[n * P : (n + 1) * P, :], in_=pages[n][:])
 
+        gather_s(0)
         for g in range(K_PASSES):
+            nc.vector.tensor_copy(v_planes[g][:], tab_planes[:, g * T : (g + 1) * T].indirect(idx[:]))
+        for g in range(K_PASSES):
+            round_w1(g, 0)
+            if g == K_PASSES - 1:
+                quantize_w1(0)
             gather_table(g)
-            prepare_w1(g, 0)
-        for a in range(H_PASSES):
-            for t in range(PACK):
-                gather_s(a, t)
-                if a > 0 and t < K_PASSES:
-                    prepare_w1(t, a)
-                for half in range(HALVES):
-                    activations(a, half, t)
-            for half in range(HALVES):
-                for t in range(PACK):
-                    first_product(a, half, t)
-                finish_z(a, half)
-            if a > 0:
-                for half in range(HALVES):
-                    quantize_z(a - 1, half)
-        for half in range(HALVES):
-            quantize_z(LAST, half)
+        for i in range(1, SLICES):
+            a, t = divmod(i, PACK)
+            if a < LAST and t == PACK - 1:
+                for g in range(K_PASSES):
+                    round_w1(g, a + 1)
+            gather_s(i)
+            if a > 0 and t == 0:
+                quantize_w1(a)
+            if i % PAIR == 0:
+                for j in range(i - PAIR, i):
+                    first_product(j)
+                finish_pair(i // PAIR - 1)
+        for j in range(SLICES - PAIR, SLICES):
+            first_product(j)
+        finish_pair(PAIRS - 1)
 
-        w2_codes = stream.tile([P, H_PASSES, N], I32, name="w2_codes", tag="load", align_bytes=64)
+        tags = (picked_tag(SLICES - PAIR), row_tag(SLICES - 1), "codes")
+        for a in range(H_PASSES):
+            z_codes[a] = keep.tile([P, S], U32, name="z_codes", tag=tags[a], align_bytes=64)
+            z_planes[a] = keep.tile([P, S], U8, name="z_plane", tag=f"plane{a}", align_bytes=64)
+        for a in range(LAST):
+            quantize_z(a, 0, S)
+        z_bf[LAST] = keep.tile([P, S * PACK], BF16, name="z_bf", tag="grouped", align_bytes=64)
+        for half in range(HALVES):
+            nc.scalar.copy(
+                out=z_bf[LAST][:, half * HALF * PACK : (half + 1) * HALF * PACK].bitcast(U32).rearrange("p (c w) -> p c w", w=PACK // PAIR),
+                in_=z_pairs[half][:].bitcast(U32).rearrange("p w c -> p c w"),
+            )
+            quantize_z(LAST, half * HALF, (half + 1) * HALF)
+
+        w2_codes = keep.tile([P, H_PASSES, N], I32, name="w2_codes", tag=row_tag(SLICES - 3), align_bytes=64)
         nc.sync.dma_start(out=w2_codes[:], in_=w2_words.rearrange("a p c i -> p a (c i)").bitcast(I32))
         for q in range(QUADRANTS):
             nc.sync.dma_start(
                 out=w2_planes[32 * q : 32 * q + 4 * H_PASSES, :].bitcast(I32),
                 in_=w2_scales[:, 4 * q : 4 * q + 4, :].bitcast(I32),
             )
-        weights = stream.tile([P, S], F32, name="weights", tag="load", align_bytes=64)
+        weights = keep.tile([P, S], F32, name="weights", tag=row_tag(SLICES - 5), align_bytes=64)
         nc.sync.dma_start(out=weights[:], in_=wgo)
         idx2 = keep.tile([P, S // 16], U16, name="idx2")
         nc.sync.dma_start(idx2[:], offs2)

@@ -31,13 +31,11 @@ LAST = H_PASSES - 1
 SLICES = H // P
 PAIR = 2
 PAIRS = SLICES // PAIR
-LOAD_BUFS = 6
+LOAD_BUFS = 5
 H_BANKS = 4
-PICKED_BUFS = 4
+PICKED_TAGS = (0, 1, 2, 3, 0, 1, 2, 3, 0, 4, 2, 3)
 TANH_BUFS = 3
-GPSIMD_PIECE = 256
 ROW_TAGS = (0, 1, 2, 3, 4, 5, 6, 7, 0, 1, 3, 5)
-GPSIMD_SHIFTS = (0, 1, 2, 4, 6)
 
 
 def tile_list_nack_silu_backward_kernel(tc, tab_words, tab_scales, w1, w2_words, w2_scales, sT, wgo, offs, offs2, out):
@@ -73,6 +71,7 @@ def tile_list_nack_silu_backward_kernel(tc, tab_words, tab_scales, w1, w2_words,
         w1_codes = {}
         w1_planes = {}
         picked = {}
+        silu_neg = {}
         neg_tanh = {}
         scaled_h = {}
         z_bf = {}
@@ -84,7 +83,7 @@ def tile_list_nack_silu_backward_kernel(tc, tab_words, tab_scales, w1, w2_words,
             return f"rows{ROW_TAGS[i]}"
 
         def picked_tag(i):
-            return f"picked{i % PICKED_BUFS}"
+            return f"picked{PICKED_TAGS[i]}"
 
         def gather_table(g):
             words = stream.tile([P, T], I32, name="words", tag="load", align_bytes=64)
@@ -121,18 +120,21 @@ def tile_list_nack_silu_backward_kernel(tc, tab_words, tab_scales, w1, w2_words,
             picked[i] = keep.tile([P, S], F32, name="picked", tag=picked_tag(i), align_bytes=64)
             s = picked[i][:]
             nc.vector.tensor_copy(s, rows[:].indirect(idx[:]))
-            nc.scalar.activation(out=neg_tanh[u][:, e, :], in_=s, func=ACT.Tanh, scale=-0.5)
-            nc.scalar.activation(out=s, in_=s, func=ACT.Silu, scale=-1.0)
-            if i in GPSIMD_SHIFTS:
-                nc.gpsimd.tensor_scalar(neg_tanh[u][:, e, :], neg_tanh[u][:, e, :], 1.0, -1.0, ALU.mult, ALU.add)
-            elif u < PAIRS - 1:
-                nc.scalar.activation(out=neg_tanh[u][:, e, :], in_=neg_tanh[u][:, e, :], func=ACT.Copy, bias=-1.0)
+            if i < SLICES - 1:
+                silu_neg[i] = s
+                nc.scalar.activation(out=neg_tanh[u][:, e, :], in_=s, func=ACT.Tanh, scale=-0.5)
+                nc.scalar.activation(out=s, in_=s, func=ACT.Silu, scale=-1.0)
+            else:
+                scaled_h[u] = keep.tile([P, PAIR, S], F32, name="scaled_h", tag=row_tag(i), align_bytes=64)
+                silu_neg[i] = scaled_h[u][:, e, :]
+                nc.scalar.activation(out=silu_neg[i], in_=s, func=ACT.Silu, scale=-1.0)
+                nc.scalar.activation(out=neg_tanh[u][:, e, :], in_=s, func=ACT.Tanh, scale=-0.5)
 
         def first_product(i):
             a, t = divmod(i, PACK)
             u, e = divmod(i, PAIR)
-            if e == 0:
-                tag = "grouped" if a < LAST and t > 0 else row_tag(min(i + PAIR, SLICES - 1))
+            if e == 0 and u < PAIRS - 1:
+                tag = "grouped" if a < LAST and t > 0 else row_tag(i + PAIR)
                 scaled_h[u] = keep.tile([P, PAIR, S], F32, name="scaled_h", tag=tag, align_bytes=64)
             for half in range(HALVES):
                 cols = slice(half * HALF, (half + 1) * HALF)
@@ -149,29 +151,34 @@ def tile_list_nack_silu_backward_kernel(tc, tab_words, tab_scales, w1, w2_words,
                         stop=(g == K_PASSES - 1),
                     )
                 nc.vector.scalar_tensor_tensor(
-                    out=scaled_h[u][:, e, cols], in0=picked[i][:, cols], scalar=1.0, in1=h[:], op0=ALU.subtract, op1=ALU.mult
+                    out=scaled_h[u][:, e, cols], in0=silu_neg[i][:, cols], scalar=1.0, in1=h[:], op0=ALU.subtract, op1=ALU.mult
                 )
 
         def finish_pair(u):
             a, w = divmod(u, PACK // PAIR)
-            if a < LAST and w == 0:
-                z_bf[a] = keep.tile([P, S * PACK], BF16, name=f"z_bf{a}", align_bytes=64)
-            if a == LAST and w == 0:
-                for half in range(HALVES):
-                    z_pairs[half] = keep.tile([P, PACK // PAIR, HALF * PAIR], BF16, name=f"z_pairs{half}", align_bytes=64)
-            piece = GPSIMD_PIECE if u < PAIRS - 1 else HALF
-            for c0 in range(0, S, piece):
-                if a < LAST:
-                    z = z_bf[a][:].rearrange("p (c t) -> p c t", t=PACK)[:, c0 : c0 + piece, PAIR * w : PAIR * (w + 1)]
-                else:
-                    half, c1 = divmod(c0, HALF)
-                    z = z_pairs[half][:, w, PAIR * c1 : PAIR * (c1 + piece)].rearrange("p (c e) -> p c e", e=PAIR)
-                left = neg_tanh[u][:, :, c0 : c0 + piece].rearrange("p e c -> p c e")
-                right = scaled_h[u][:, :, c0 : c0 + piece].rearrange("p e c -> p c e")
-                if u < PAIRS - 1:
-                    nc.gpsimd.tensor_tensor(out=z, in0=left, in1=right, op=ALU.mult)
-                else:
-                    nc.vector.scalar_tensor_tensor(out=z, in0=left, scalar=1.0, in1=right, op0=ALU.subtract, op1=ALU.mult)
+            for half in range(HALVES):
+                if w == 0:
+                    z_pairs[a, half] = keep.tile(
+                        [P, PACK // PAIR, HALF * PAIR], BF16, name="z_pairs", tag=f"pairs{a % 2}_{half}", align_bytes=64
+                    )
+                cols = slice(half * HALF, (half + 1) * HALF)
+                nc.vector.scalar_tensor_tensor(
+                    out=z_pairs[a, half][:, w, :].rearrange("p (c e) -> p c e", e=PAIR),
+                    in0=neg_tanh[u][:, :, cols].rearrange("p e c -> p c e"),
+                    scalar=1.0,
+                    in1=scaled_h[u][:, :, cols].rearrange("p e c -> p c e"),
+                    op0=ALU.subtract,
+                    op1=ALU.mult,
+                )
+
+        def join_pairs(a, half):
+            if half == 0:
+                tag = picked_tag(PACK * (a + 1) + 1) if a < LAST else "grouped"
+                z_bf[a] = keep.tile([P, S * PACK], BF16, name="z_bf", tag=tag, align_bytes=64)
+            nc.scalar.copy(
+                out=z_bf[a][:, half * HALF * PACK : (half + 1) * HALF * PACK].bitcast(U32).rearrange("p (c w) -> p c w", w=PACK // PAIR),
+                in_=z_pairs[a, half][:].bitcast(U32).rearrange("p w c -> p c w"),
+            )
 
         def quantize_z(a, c0, c1):
             nc.vector.quantize_mx(
@@ -218,6 +225,9 @@ def tile_list_nack_silu_backward_kernel(tc, tab_words, tab_scales, w1, w2_words,
                 for j in range(i - PAIR, i):
                     first_product(j)
                 finish_pair(i // PAIR - 1)
+            if a > 0 and t == PAIR:
+                for half in range(HALVES):
+                    join_pairs(a - 1, half)
         for j in range(SLICES - PAIR, SLICES):
             first_product(j)
         finish_pair(PAIRS - 1)
@@ -228,12 +238,8 @@ def tile_list_nack_silu_backward_kernel(tc, tab_words, tab_scales, w1, w2_words,
             z_planes[a] = keep.tile([P, S], U8, name="z_plane", tag=f"plane{a}", align_bytes=64)
         for a in range(LAST):
             quantize_z(a, 0, S)
-        z_bf[LAST] = keep.tile([P, S * PACK], BF16, name="z_bf", tag="grouped", align_bytes=64)
         for half in range(HALVES):
-            nc.scalar.copy(
-                out=z_bf[LAST][:, half * HALF * PACK : (half + 1) * HALF * PACK].bitcast(U32).rearrange("p (c w) -> p c w", w=PACK // PAIR),
-                in_=z_pairs[half][:].bitcast(U32).rearrange("p w c -> p c w"),
-            )
+            join_pairs(LAST, half)
             quantize_z(LAST, half * HALF, (half + 1) * HALF)
 
         w2_codes = keep.tile([P, H_PASSES, N], I32, name="w2_codes", tag=row_tag(SLICES - 3), align_bytes=64)

@@ -33,9 +33,12 @@ PAIR = 2
 PAIRS = SLICES // PAIR
 LOAD_BUFS = 5
 H_BANKS = 4
-PICKED_TAGS = (0, 1, 2, 3, 0, 1, 2, 3, 0, 4, 2, 3)
 TANH_BUFS = 3
-ROW_TAGS = (0, 1, 2, 3, 4, 5, 6, 7, 0, 1, 3, 5)
+SPLIT = 576
+KIB = 1024
+AREA_KIB = (8, 9, 12, 9, 8, 12, 8, 12)
+ROW_AREAS = (0, 1, 2, 3, 4, 5, 6, 7, 0, 1, 3, 2)
+SHIFTED_BYTES = 4 * PAIR * SPLIT
 
 
 def tile_list_nack_silu_backward_kernel(tc, tab_words, tab_scales, w1, w2_words, w2_scales, sT, wgo, offs, offs2, out):
@@ -44,6 +47,7 @@ def tile_list_nack_silu_backward_kernel(tc, tab_words, tab_scales, w1, w2_words,
         keep = ctx.enter_context(tc.tile_pool(name="keep", bufs=1))
         stream = ctx.enter_context(tc.tile_pool(name="stream", bufs=LOAD_BUFS))
         work = ctx.enter_context(tc.tile_pool(name="work", bufs=TANH_BUFS))
+        arena = ctx.enter_context(tc.tile_pool(name="arena", bufs=1))
         h_psum = ctx.enter_context(tc.psum_pool(name="h_psum", bufs=H_BANKS))
         y_psum = ctx.enter_context(tc.psum_pool(name="y_psum", bufs=8 - H_BANKS))
 
@@ -79,11 +83,9 @@ def tile_list_nack_silu_backward_kernel(tc, tab_words, tab_scales, w1, w2_words,
         z_codes = {}
         z_planes = {}
 
-        def row_tag(i):
-            return f"rows{ROW_TAGS[i]}"
-
-        def picked_tag(i):
-            return f"picked{PICKED_TAGS[i]}"
+        def placed(name, shape, dtype, i, start=0):
+            offset = KIB * sum(AREA_KIB[: ROW_AREAS[i]]) + start
+            return arena.tile(shape, dtype, name=name, offset=offset, align_bytes=64)
 
         def gather_table(g):
             words = stream.tile([P, T], I32, name="words", tag="load", align_bytes=64)
@@ -105,27 +107,34 @@ def tile_list_nack_silu_backward_kernel(tc, tab_words, tab_scales, w1, w2_words,
             )
 
         def quantize_w1(a):
-            tag = row_tag(PACK * a) if a > 0 else "codes"
-            w1_codes[a] = keep.tile([P, K_PASSES * PASS], U32, name="w1_codes", tag=tag, align_bytes=64)
+            if a < LAST:
+                w1_codes[a] = keep.tile([P, K_PASSES * PASS], U32, name="w1_codes", tag=("codes", "picked2")[a], align_bytes=64)
+            else:
+                w1_codes[a] = placed("w1_codes_last", [P, K_PASSES * PASS], U32, 5, 8 * KIB)
             w1_planes[a] = keep.tile([P, K_PASSES * PASS], U8, name="w1_plane", tag=f"plane{a}", align_bytes=64)
             nc.vector.quantize_mx(out=w1_codes[a][:].bitcast(E4M3X4), scales=w1_planes[a][:], in_=grouped[a][:])
 
         def gather_s(i):
             a, t = divmod(i, PACK)
-            u, e = divmod(i, PAIR)
-            rows = keep.tile([P, T], F32, name="rows", tag=row_tag(i), align_bytes=64)
+            rows = placed(f"rows{i}", [P, T], F32, i)
             nc.sync.dma_start(out=rows[:], in_=sT[a * PASS : (a + 1) * PASS, :].rearrange("(p t) n -> p t n", t=PACK)[:, t, :])
+            if i % PAIR == 0 and i > PAIR:
+                picked[i] = placed(f"picked{i}", [P, S], F32, i - 1, SHIFTED_BYTES)
+            else:
+                picked[i] = keep.tile([P, S], F32, name="picked", tag="picked1" if i % PAIR else f"picked{i}", align_bytes=64)
+            nc.vector.tensor_copy(picked[i][:], rows[:].indirect(idx[:]))
+
+        def activations(i):
+            u, e = divmod(i, PAIR)
             if e == 0:
                 neg_tanh[u] = work.tile([P, PAIR, S], F32, name="neg_tanh", tag="tanh", align_bytes=64)
-            picked[i] = keep.tile([P, S], F32, name="picked", tag=picked_tag(i), align_bytes=64)
             s = picked[i][:]
-            nc.vector.tensor_copy(s, rows[:].indirect(idx[:]))
             if i < SLICES - 1:
                 silu_neg[i] = s
                 nc.scalar.activation(out=neg_tanh[u][:, e, :], in_=s, func=ACT.Tanh, scale=-0.5)
                 nc.scalar.activation(out=s, in_=s, func=ACT.Silu, scale=-1.0)
             else:
-                scaled_h[u] = keep.tile([P, PAIR, S], F32, name="scaled_h", tag=row_tag(i), align_bytes=64)
+                scaled_h[u] = placed("scaled_h_last", [P, PAIR, S], F32, i, 4 * KIB)
                 silu_neg[i] = scaled_h[u][:, e, :]
                 nc.scalar.activation(out=silu_neg[i], in_=s, func=ACT.Silu, scale=-1.0)
                 nc.scalar.activation(out=neg_tanh[u][:, e, :], in_=s, func=ACT.Tanh, scale=-0.5)
@@ -134,8 +143,7 @@ def tile_list_nack_silu_backward_kernel(tc, tab_words, tab_scales, w1, w2_words,
             a, t = divmod(i, PACK)
             u, e = divmod(i, PAIR)
             if e == 0 and u < PAIRS - 1:
-                tag = "grouped" if a < LAST and t > 0 else row_tag(i + PAIR)
-                scaled_h[u] = keep.tile([P, PAIR, S], F32, name="scaled_h", tag=tag, align_bytes=64)
+                scaled_h[u] = placed(f"scaled_h{u}", [P, PAIR, S], F32, i + PAIR)
             for half in range(HALVES):
                 cols = slice(half * HALF, (half + 1) * HALF)
                 h = h_psum.tile([P, HALF], F32, name="h")
@@ -154,31 +162,58 @@ def tile_list_nack_silu_backward_kernel(tc, tab_words, tab_scales, w1, w2_words,
                     out=scaled_h[u][:, e, cols], in0=silu_neg[i][:, cols], scalar=1.0, in1=h[:], op0=ALU.subtract, op1=ALU.mult
                 )
 
-        def finish_pair(u):
+        def pair_out(u, c0, c1):
             a, w = divmod(u, PACK // PAIR)
-            for half in range(HALVES):
-                if w == 0:
-                    z_pairs[a, half] = keep.tile(
-                        [P, PACK // PAIR, HALF * PAIR], BF16, name="z_pairs", tag=f"pairs{a % 2}_{half}", align_bytes=64
-                    )
-                cols = slice(half * HALF, (half + 1) * HALF)
-                nc.vector.scalar_tensor_tensor(
-                    out=z_pairs[a, half][:, w, :].rearrange("p (c e) -> p c e", e=PAIR),
-                    in0=neg_tanh[u][:, :, cols].rearrange("p e c -> p c e"),
-                    scalar=1.0,
-                    in1=scaled_h[u][:, :, cols].rearrange("p e c -> p c e"),
-                    op0=ALU.subtract,
-                    op1=ALU.mult,
-                )
+            if a < LAST:
+                if a not in z_pairs:
+                    z_pairs[a] = keep.tile([P, PACK // PAIR, S * PAIR], BF16, name=f"z_pairs{a}", align_bytes=64)
+                return z_pairs[a][:, w, PAIR * c0 : PAIR * c1].rearrange("p (c e) -> p c e", e=PAIR)
+            half = c0 // HALF
+            if w == 0 and half == 0:
+                z_pairs[a, half] = placed("last_pairs", [P, PACK // PAIR, HALF * PAIR], BF16, SLICES - 1)
+            elif w == 0:
+                z_pairs[a, half] = keep.tile([P, PACK // PAIR, HALF * PAIR], BF16, name="last_pairs1", tag="z_pairs0", align_bytes=64)
+            return z_pairs[a, half][:, w, :].rearrange("p (c e) -> p c e", e=PAIR)
+
+        def finish_on_vector(u, half):
+            cols = slice(half * HALF, (half + 1) * HALF)
+            nc.vector.scalar_tensor_tensor(
+                out=pair_out(u, half * HALF, (half + 1) * HALF),
+                in0=neg_tanh[u][:, :, cols].rearrange("p e c -> p c e"),
+                scalar=1.0,
+                in1=scaled_h[u][:, :, cols].rearrange("p e c -> p c e"),
+                op0=ALU.subtract,
+                op1=ALU.mult,
+            )
+
+        def shift_on_scalar(u, c0):
+            nc.scalar.activation(out=neg_tanh[u][:, :, c0:], in_=neg_tanh[u][:, :, c0:], func=ACT.Copy, bias=-1.0)
+
+        def finish_on_gpsimd(u, c0, c1, factor):
+            nc.gpsimd.tensor_tensor(
+                out=pair_out(u, c0, c1),
+                in0=factor.rearrange("p e c -> p c e"),
+                in1=scaled_h[u][:, :, c0:c1].rearrange("p e c -> p c e"),
+                op=ALU.mult,
+            )
 
         def join_pairs(a, half):
-            if half == 0:
-                tag = picked_tag(PACK * (a + 1) + 1) if a < LAST else "grouped"
-                z_bf[a] = keep.tile([P, S * PACK], BF16, name="z_bf", tag=tag, align_bytes=64)
+            if half == 0 and a < LAST:
+                z_bf[a] = placed(f"z_bf{a}", [P, S * PACK], BF16, 5 + 2 * a)
+            elif half == 0:
+                z_bf[a] = keep.tile([P, S * PACK], BF16, name="z_bf", tag="grouped", align_bytes=64)
+            pairs = z_pairs[a][:, :, half * HALF * PAIR : (half + 1) * HALF * PAIR] if a < LAST else z_pairs[a, half][:]
             nc.scalar.copy(
                 out=z_bf[a][:, half * HALF * PACK : (half + 1) * HALF * PACK].bitcast(U32).rearrange("p (c w) -> p c w", w=PACK // PAIR),
-                in_=z_pairs[a, half][:].bitcast(U32).rearrange("p w c -> p c w"),
+                in_=pairs.bitcast(U32).rearrange("p w c -> p c w"),
             )
+
+        def z_tiles(a):
+            if a < LAST:
+                z_codes[a] = placed(f"z_codes{a}", [P, S], U32, (7, SLICES - 1)[a], 8 * KIB)
+            else:
+                z_codes[a] = keep.tile([P, S], U32, name="z_codes", tag="codes", align_bytes=64)
+            z_planes[a] = keep.tile([P, S], U8, name="z_plane", tag=f"plane{a}", align_bytes=64)
 
         def quantize_z(a, c0, c1):
             nc.vector.quantize_mx(
@@ -206,6 +241,7 @@ def tile_list_nack_silu_backward_kernel(tc, tab_words, tab_scales, w1, w2_words,
                 nc.sync.dma_start(out=out[n * P : (n + 1) * P, :], in_=pages[n][:])
 
         gather_s(0)
+        activations(0)
         for g in range(K_PASSES):
             nc.vector.tensor_copy(v_planes[g][:], tab_planes[:, g * T : (g + 1) * T].indirect(idx[:]))
         for g in range(K_PASSES):
@@ -215,41 +251,52 @@ def tile_list_nack_silu_backward_kernel(tc, tab_words, tab_scales, w1, w2_words,
             gather_table(g)
         for i in range(1, SLICES):
             a, t = divmod(i, PACK)
-            if a < LAST and t == PACK - 1:
-                for g in range(K_PASSES):
-                    round_w1(g, a + 1)
+            if a < LAST and t % PAIR == 1:
+                round_w1(t // PAIR, a + 1)
             gather_s(i)
-            if a > 0 and t == 0:
-                quantize_w1(a)
+            u = i // PAIR
+            if i % PAIR == 1 and PAIR < i < SLICES - 1:
+                shifted = placed(f"shifted{i}", [P, PAIR, SPLIT], F32, i)
+                nc.gpsimd.tensor_scalar(shifted[:], neg_tanh[u - 1][:, :, :SPLIT], 1.0, -1.0, ALU.mult, ALU.add)
+                finish_on_gpsimd(u - 1, 0, SPLIT, shifted[:])
+            if i == SLICES - 1:
+                finish_on_gpsimd(u - 1, 0, HALF, neg_tanh[u - 1][:, :, :HALF])
+            activations(i)
+            if i % PAIR == 1 and i < SLICES - 1:
+                shift_on_scalar(u, SPLIT if u < PAIRS - 2 else 0)
             if i % PAIR == 0:
-                for j in range(i - PAIR, i):
-                    first_product(j)
-                finish_pair(i // PAIR - 1)
-            if a > 0 and t == PAIR:
+                first_product(i - 2)
+                if a > 0 and t == 0:
+                    quantize_w1(a)
+                if i == SLICES - 2:
+                    z_tiles(0)
+                    quantize_z(0, 0, S)
+                first_product(i - 1)
+                c0 = SPLIT if u - 1 < PAIRS - 2 else HALF
+                finish_on_gpsimd(u - 1, c0, S, neg_tanh[u - 1][:, :, c0:])
+            if i in (SLICES - 4, SLICES - 2):
+                done = (i - SLICES + 4) // PAIR
                 for half in range(HALVES):
-                    join_pairs(a - 1, half)
+                    join_pairs(done, half)
         for j in range(SLICES - PAIR, SLICES):
             first_product(j)
-        finish_pair(PAIRS - 1)
-
-        tags = (picked_tag(SLICES - PAIR), row_tag(SLICES - 1), "codes")
-        for a in range(H_PASSES):
-            z_codes[a] = keep.tile([P, S], U32, name="z_codes", tag=tags[a], align_bytes=64)
-            z_planes[a] = keep.tile([P, S], U8, name="z_plane", tag=f"plane{a}", align_bytes=64)
-        for a in range(LAST):
-            quantize_z(a, 0, S)
+        for half in range(HALVES):
+            finish_on_vector(PAIRS - 1, half)
+        z_tiles(1)
+        z_tiles(LAST)
         for half in range(HALVES):
             join_pairs(LAST, half)
-            quantize_z(LAST, half * HALF, (half + 1) * HALF)
+            for a in range(1, H_PASSES):
+                quantize_z(a, half * HALF, (half + 1) * HALF)
 
-        w2_codes = keep.tile([P, H_PASSES, N], I32, name="w2_codes", tag=row_tag(SLICES - 3), align_bytes=64)
+        w2_codes = placed("w2_codes", [P, H_PASSES, N], I32, 6)
         nc.sync.dma_start(out=w2_codes[:], in_=w2_words.rearrange("a p c i -> p a (c i)").bitcast(I32))
         for q in range(QUADRANTS):
             nc.sync.dma_start(
                 out=w2_planes[32 * q : 32 * q + 4 * H_PASSES, :].bitcast(I32),
                 in_=w2_scales[:, 4 * q : 4 * q + 4, :].bitcast(I32),
             )
-        weights = keep.tile([P, S], F32, name="weights", tag=row_tag(SLICES - 5), align_bytes=64)
+        weights = placed("weights", [P, S], F32, 8)
         nc.sync.dma_start(out=weights[:], in_=wgo)
         idx2 = keep.tile([P, S // 16], U16, name="idx2")
         nc.sync.dma_start(idx2[:], offs2)

@@ -31,14 +31,14 @@ LAST = H_PASSES - 1
 SLICES = H // P
 PAIR = 2
 PAIRS = SLICES // PAIR
-LOAD_BUFS = 5
+LOAD_BUFS = 4
 H_BANKS = 4
 TANH_BUFS = 3
 SPLIT = 576
+ODD_SPLIT = T2 // 2 + 1
 KIB = 1024
-AREA_KIB = (8, 9, 12, 9, 8, 12, 8, 12)
-ROW_AREAS = (0, 1, 2, 3, 4, 5, 6, 7, 0, 1, 3, 2)
-SHIFTED_BYTES = 4 * PAIR * SPLIT
+AREA_KIB = (8, 12, 12, 12, 8, 14, 8, 14, 6)
+ROW_AREAS = (0, 1, 2, 3, 4, 5, 6, 7, 0, 1, 3, 2, 8)
 
 
 def tile_list_nack_silu_backward_kernel(tc, tab_words, tab_scales, w1, w2_words, w2_scales, sT, wgo, offs, offs2, out):
@@ -56,13 +56,14 @@ def tile_list_nack_silu_backward_kernel(tc, tab_words, tab_scales, w1, w2_words,
 
         tab_planes = keep.tile([P, K_PASSES * T], U8, name="tab_planes", align_bytes=64)
         v_planes = [keep.tile([P, S], U8, name=f"v_plane{g}", align_bytes=64) for g in range(K_PASSES)]
-        w2_planes = keep.tile([P, N], U8, name="w2_planes", align_bytes=64)
         nc.gpsimd.memset(tab_planes[:].bitcast(I32), 0)
-        nc.gpsimd.memset(w2_planes[:].bitcast(I32), 0)
 
         pages = [keep.tile([P, T2], F32, name=f"page{n}") for n in range(N_TILES)]
-        for page in pages:
+        for page in pages[: N_TILES // 2]:
             nc.gpsimd.memset(page[:], 0.0)
+        for page in pages[N_TILES // 2 :]:
+            nc.vector.memset(page[:, :ODD_SPLIT], 0.0)
+            nc.vector.memset(page[:, ODD_SPLIT:], 0.0)
 
         v_words = [keep.tile([P, S], U32, name=f"v_words{g}", align_bytes=64) for g in range(K_PASSES)]
         for q in range(QUADRANTS):
@@ -110,7 +111,7 @@ def tile_list_nack_silu_backward_kernel(tc, tab_words, tab_scales, w1, w2_words,
             if a < LAST:
                 w1_codes[a] = keep.tile([P, K_PASSES * PASS], U32, name="w1_codes", tag=("codes", "picked2")[a], align_bytes=64)
             else:
-                w1_codes[a] = placed("w1_codes_last", [P, K_PASSES * PASS], U32, 5, 8 * KIB)
+                w1_codes[a] = placed("w1_codes_last", [P, K_PASSES * PASS], U32, 5, 10 * KIB)
             w1_planes[a] = keep.tile([P, K_PASSES * PASS], U8, name="w1_plane", tag=f"plane{a}", align_bytes=64)
             nc.vector.quantize_mx(out=w1_codes[a][:].bitcast(E4M3X4), scales=w1_planes[a][:], in_=grouped[a][:])
 
@@ -119,9 +120,11 @@ def tile_list_nack_silu_backward_kernel(tc, tab_words, tab_scales, w1, w2_words,
             rows = placed(f"rows{i}", [P, T], F32, i)
             nc.sync.dma_start(out=rows[:], in_=sT[a * PASS : (a + 1) * PASS, :].rearrange("(p t) n -> p t n", t=PACK)[:, t, :])
             if i % PAIR == 0 and i > PAIR:
-                picked[i] = placed(f"picked{i}", [P, S], F32, i - 1, SHIFTED_BYTES)
+                picked[i] = placed(f"picked{i}", [P, S], F32, i - 1, 8 * KIB)
+            elif i % PAIR == 0:
+                picked[i] = keep.tile([P, S], F32, name="picked", tag=f"picked{i}", align_bytes=64)
             else:
-                picked[i] = keep.tile([P, S], F32, name="picked", tag="picked1" if i % PAIR else f"picked{i}", align_bytes=64)
+                picked[i] = placed(f"picked{i}", [P, S], F32, SLICES, 2 * KIB * (i // PAIR % 2))
             nc.vector.tensor_copy(picked[i][:], rows[:].indirect(idx[:]))
 
         def activations(i):
@@ -130,13 +133,25 @@ def tile_list_nack_silu_backward_kernel(tc, tab_words, tab_scales, w1, w2_words,
                 neg_tanh[u] = work.tile([P, PAIR, S], F32, name="neg_tanh", tag="tanh", align_bytes=64)
             s = picked[i][:]
             if i < SLICES - 1:
-                silu_neg[i] = s
                 nc.scalar.activation(out=neg_tanh[u][:, e, :], in_=s, func=ACT.Tanh, scale=-0.5)
+            if e == 0:
                 nc.scalar.activation(out=s, in_=s, func=ACT.Silu, scale=-1.0)
+                for half in range(HALVES):
+                    silu_neg[i, half] = s[:, half * HALF : (half + 1) * HALF]
+            elif i < SLICES - 1:
+                first = placed(f"silu_first{i}", [P, HALF], F32, SLICES, 4 * KIB * (1 - u % 2))
+                if i < SLICES - 3:
+                    second = placed(f"silu_second{i}", [P, HALF], F32, i + 2, 8 * KIB)
+                else:
+                    second = keep.tile([P, HALF], F32, name="silu_second", tag="picked0", align_bytes=64)
+                for half, tile in enumerate((first, second)):
+                    silu_neg[i, half] = tile[:]
+                    nc.scalar.activation(out=tile[:], in_=s[:, half * HALF : (half + 1) * HALF], func=ACT.Silu, scale=-1.0)
             else:
                 scaled_h[u] = placed("scaled_h_last", [P, PAIR, S], F32, i, 4 * KIB)
-                silu_neg[i] = scaled_h[u][:, e, :]
-                nc.scalar.activation(out=silu_neg[i], in_=s, func=ACT.Silu, scale=-1.0)
+                for half in range(HALVES):
+                    silu_neg[i, half] = scaled_h[u][:, e, half * HALF : (half + 1) * HALF]
+                nc.scalar.activation(out=scaled_h[u][:, e, :], in_=s, func=ACT.Silu, scale=-1.0)
                 nc.scalar.activation(out=neg_tanh[u][:, e, :], in_=s, func=ACT.Tanh, scale=-0.5)
 
         def first_product(i):
@@ -159,7 +174,7 @@ def tile_list_nack_silu_backward_kernel(tc, tab_words, tab_scales, w1, w2_words,
                         stop=(g == K_PASSES - 1),
                     )
                 nc.vector.scalar_tensor_tensor(
-                    out=scaled_h[u][:, e, cols], in0=silu_neg[i][:, cols], scalar=1.0, in1=h[:], op0=ALU.subtract, op1=ALU.mult
+                    out=scaled_h[u][:, e, cols], in0=silu_neg[i, half], scalar=1.0, in1=h[:], op0=ALU.subtract, op1=ALU.mult
                 )
 
         def pair_out(u, c0, c1):
@@ -199,7 +214,7 @@ def tile_list_nack_silu_backward_kernel(tc, tab_words, tab_scales, w1, w2_words,
 
         def join_pairs(a, half):
             if half == 0 and a < LAST:
-                z_bf[a] = placed(f"z_bf{a}", [P, S * PACK], BF16, 5 + 2 * a)
+                z_bf[a] = placed(f"z_bf{a}", [P, S * PACK], BF16, 5 + 2 * a, 2 * KIB)
             elif half == 0:
                 z_bf[a] = keep.tile([P, S * PACK], BF16, name="z_bf", tag="grouped", align_bytes=64)
             pairs = z_pairs[a][:, :, half * HALF * PAIR : (half + 1) * HALF * PAIR] if a < LAST else z_pairs[a, half][:]
@@ -210,7 +225,7 @@ def tile_list_nack_silu_backward_kernel(tc, tab_words, tab_scales, w1, w2_words,
 
         def z_tiles(a):
             if a < LAST:
-                z_codes[a] = placed(f"z_codes{a}", [P, S], U32, (7, SLICES - 1)[a], 8 * KIB)
+                z_codes[a] = placed(f"z_codes{a}", [P, S], U32, (7, SLICES - 1)[a], (10, 8)[a] * KIB)
             else:
                 z_codes[a] = keep.tile([P, S], U32, name="z_codes", tag="codes", align_bytes=64)
             z_planes[a] = keep.tile([P, S], U8, name="z_plane", tag=f"plane{a}", align_bytes=64)
@@ -227,7 +242,7 @@ def tile_list_nack_silu_backward_kernel(tc, tab_words, tab_scales, w1, w2_words,
                 nc.tensor.matmul_mx(
                     out=y[:],
                     lhsT=w2_codes[:, a, n * P : (n + 1) * P].bitcast(E4M3X4),
-                    lhsT_scale=w2_planes[4 * a : P, n * P : (n + 1) * P],
+                    lhsT_scale=w2_planes[:, a * N + n * P : a * N + (n + 1) * P],
                     rhs=z_codes[a][:, cols].bitcast(E4M3X4),
                     rhs_scale=z_planes[a][:, cols],
                     start=(a == 0),
@@ -291,10 +306,12 @@ def tile_list_nack_silu_backward_kernel(tc, tab_words, tab_scales, w1, w2_words,
 
         w2_codes = placed("w2_codes", [P, H_PASSES, N], I32, 6)
         nc.sync.dma_start(out=w2_codes[:], in_=w2_words.rearrange("a p c i -> p a (c i)").bitcast(I32))
+        w2_planes = placed("w2_planes", [P, H_PASSES * N], U8, 6, 6 * KIB)
+        nc.gpsimd.memset(w2_planes[:].bitcast(I32), 0)
         for q in range(QUADRANTS):
             nc.sync.dma_start(
-                out=w2_planes[32 * q : 32 * q + 4 * H_PASSES, :].bitcast(I32),
-                in_=w2_scales[:, 4 * q : 4 * q + 4, :].bitcast(I32),
+                out=w2_planes[32 * q : 32 * q + 4, :].bitcast(I32).rearrange("r (a n) -> r a n", a=H_PASSES),
+                in_=w2_scales[:, 4 * q : 4 * q + 4, :].bitcast(I32).rearrange("a r n -> r a n"),
             )
         weights = placed("weights", [P, S], F32, 8)
         nc.sync.dma_start(out=weights[:], in_=wgo)

@@ -36,6 +36,7 @@ H_BANKS = 4
 TANH_BUFS = 3
 SPLIT = 576
 ODD_SPLIT = T2 // 2 + 1
+RUN = 4
 KIB = 1024
 AREA_KIB = (8, 12, 12, 12, 8, 14, 8, 14, 6)
 ROW_AREAS = (0, 1, 2, 3, 4, 5, 6, 7, 0, 1, 3, 2, 8)
@@ -182,18 +183,18 @@ def tile_list_nack_silu_backward_kernel(tc, tab_words, tab_scales, w1, w2_words,
             if a < LAST:
                 if a not in z_pairs:
                     z_pairs[a] = keep.tile([P, PACK // PAIR, S * PAIR], BF16, name=f"z_pairs{a}", align_bytes=64)
-                return z_pairs[a][:, w, PAIR * c0 : PAIR * c1].rearrange("p (c e) -> p c e", e=PAIR)
+                return z_pairs[a][:, w, PAIR * c0 : PAIR * c1]
             half = c0 // HALF
             if w == 0 and half == 0:
                 z_pairs[a, half] = placed("last_pairs", [P, PACK // PAIR, HALF * PAIR], BF16, SLICES - 1)
             elif w == 0:
                 z_pairs[a, half] = keep.tile([P, PACK // PAIR, HALF * PAIR], BF16, name="last_pairs1", tag="z_pairs0", align_bytes=64)
-            return z_pairs[a, half][:, w, :].rearrange("p (c e) -> p c e", e=PAIR)
+            return z_pairs[a, half][:, w, :]
 
         def finish_on_vector(u, half):
             cols = slice(half * HALF, (half + 1) * HALF)
             nc.vector.scalar_tensor_tensor(
-                out=pair_out(u, half * HALF, (half + 1) * HALF),
+                out=pair_out(u, half * HALF, (half + 1) * HALF).rearrange("p (c e) -> p c e", e=PAIR),
                 in0=neg_tanh[u][:, :, cols].rearrange("p e c -> p c e"),
                 scalar=1.0,
                 in1=scaled_h[u][:, :, cols].rearrange("p e c -> p c e"),
@@ -206,9 +207,9 @@ def tile_list_nack_silu_backward_kernel(tc, tab_words, tab_scales, w1, w2_words,
 
         def finish_on_gpsimd(u, c0, c1, factor):
             nc.gpsimd.tensor_tensor(
-                out=pair_out(u, c0, c1),
-                in0=factor.rearrange("p e c -> p c e"),
-                in1=scaled_h[u][:, :, c0:c1].rearrange("p e c -> p c e"),
+                out=pair_out(u, c0, c1).rearrange("p (c r e) -> p c e r", r=RUN, e=PAIR),
+                in0=factor.rearrange("p e (c r) -> p c e r", r=RUN),
+                in1=scaled_h[u][:, :, c0:c1].rearrange("p e (c r) -> p c e r", r=RUN),
                 op=ALU.mult,
             )
 

@@ -21,25 +21,31 @@ PACK = 4
 PASS = P * PACK
 QUADRANTS = 4
 HALF = 512
+PAIR = 2
 K_PASSES = K // PASS
 H_PASSES = H // PASS
 HALVES = S // HALF
 N_TILES = N // P
-LIST_COLS = HALF // 16
-LAST = H_PASSES - 1
-
 SLICES = H // P
-PAIR = 2
 PAIRS = SLICES // PAIR
+PASS_PAIRS = PACK // PAIR
+LIST_COLS = HALF // 16
+LAST_PASS = H_PASSES - 1
+LAST_PAIR = PAIRS - 1
+LAST_SLICE = SLICES - 1
+
 LOAD_BUFS = 4
-H_BANKS = 4
+H_BANKS = 6
 TANH_BUFS = 3
-SPLIT = 576
-ODD_SPLIT = T2 // 2 + 1
+LATE = 576
 RUN = 4
+ODD_SPLIT = T2 // 2 + 1
+
 KIB = 1024
+ROWS_END = 8 * KIB
 AREA_KIB = (8, 12, 12, 12, 8, 14, 8, 14, 6)
-ROW_AREAS = (0, 1, 2, 3, 4, 5, 6, 7, 0, 1, 3, 2, 8)
+ROW_AREA = (0, 1, 2, 3, 4, 5, 6, 7, 0, 1, 3, 2)
+ODD_AREA = 8
 
 
 def tile_list_nack_silu_backward_kernel(tc, tab_words, tab_scales, w1, w2_words, w2_scales, sT, wgo, offs, offs2, out):
@@ -77,6 +83,7 @@ def tile_list_nack_silu_backward_kernel(tc, tab_words, tab_scales, w1, w2_words,
         w1_codes = {}
         w1_planes = {}
         picked = {}
+        h = {}
         silu_neg = {}
         neg_tanh = {}
         scaled_h = {}
@@ -85,8 +92,8 @@ def tile_list_nack_silu_backward_kernel(tc, tab_words, tab_scales, w1, w2_words,
         z_codes = {}
         z_planes = {}
 
-        def placed(name, shape, dtype, i, start=0):
-            offset = KIB * sum(AREA_KIB[: ROW_AREAS[i]]) + start
+        def placed(name, shape, dtype, area, start=0):
+            offset = KIB * sum(AREA_KIB[:area]) + start
             return arena.tile(shape, dtype, name=name, offset=offset, align_bytes=64)
 
         def gather_table(g):
@@ -109,23 +116,23 @@ def tile_list_nack_silu_backward_kernel(tc, tab_words, tab_scales, w1, w2_words,
             )
 
         def quantize_w1(a):
-            if a < LAST:
+            if a < LAST_PASS:
                 w1_codes[a] = keep.tile([P, K_PASSES * PASS], U32, name="w1_codes", tag=("codes", "picked2")[a], align_bytes=64)
             else:
-                w1_codes[a] = placed("w1_codes_last", [P, K_PASSES * PASS], U32, 5, 10 * KIB)
+                w1_codes[a] = placed("w1_codes_last", [P, K_PASSES * PASS], U32, ROW_AREA[PACK * a - 3], ROWS_END + 2 * KIB)
             w1_planes[a] = keep.tile([P, K_PASSES * PASS], U8, name="w1_plane", tag=f"plane{a}", align_bytes=64)
             nc.vector.quantize_mx(out=w1_codes[a][:].bitcast(E4M3X4), scales=w1_planes[a][:], in_=grouped[a][:])
 
         def gather_s(i):
             a, t = divmod(i, PACK)
-            rows = placed(f"rows{i}", [P, T], F32, i)
+            rows = placed(f"rows{i}", [P, T], F32, ROW_AREA[i])
             nc.sync.dma_start(out=rows[:], in_=sT[a * PASS : (a + 1) * PASS, :].rearrange("(p t) n -> p t n", t=PACK)[:, t, :])
             if i % PAIR == 0 and i > PAIR:
-                picked[i] = placed(f"picked{i}", [P, S], F32, i - 1, 8 * KIB)
+                picked[i] = placed(f"picked{i}", [P, S], F32, ROW_AREA[i - 1], ROWS_END)
             elif i % PAIR == 0:
                 picked[i] = keep.tile([P, S], F32, name="picked", tag=f"picked{i}", align_bytes=64)
             else:
-                picked[i] = placed(f"picked{i}", [P, S], F32, SLICES, 2 * KIB * (i // PAIR % 2))
+                picked[i] = placed(f"picked{i}", [P, S], F32, ODD_AREA, 2 * KIB * (i // PAIR % 2))
             nc.vector.tensor_copy(picked[i][:], rows[:].indirect(idx[:]))
 
         def activations(i):
@@ -133,62 +140,71 @@ def tile_list_nack_silu_backward_kernel(tc, tab_words, tab_scales, w1, w2_words,
             if e == 0:
                 neg_tanh[u] = work.tile([P, PAIR, S], F32, name="neg_tanh", tag="tanh", align_bytes=64)
             s = picked[i][:]
-            if i < SLICES - 1:
+            if 0 < i < LAST_SLICE:
                 nc.scalar.activation(out=neg_tanh[u][:, e, :], in_=s, func=ACT.Tanh, scale=-0.5)
-            if e == 0:
+            if i == 0:
+                whole = placed("silu_whole", [P, S], F32, ROW_AREA[5], ROWS_END)
+                nc.scalar.activation(out=whole[:], in_=s, func=ACT.Silu, scale=-1.0)
+                nc.scalar.activation(out=neg_tanh[u][:, e, :], in_=s, func=ACT.Tanh, scale=-0.5)
+                for half in range(HALVES):
+                    silu_neg[i, half] = whole[:, half * HALF : (half + 1) * HALF]
+            elif e == 0:
                 nc.scalar.activation(out=s, in_=s, func=ACT.Silu, scale=-1.0)
                 for half in range(HALVES):
                     silu_neg[i, half] = s[:, half * HALF : (half + 1) * HALF]
-            elif i < SLICES - 1:
-                first = placed(f"silu_first{i}", [P, HALF], F32, SLICES, 4 * KIB * (1 - u % 2))
-                if i < SLICES - 3:
-                    second = placed(f"silu_second{i}", [P, HALF], F32, i + 2, 8 * KIB)
+            elif i < LAST_SLICE:
+                first = placed(f"silu_first{i}", [P, HALF], F32, ODD_AREA, 4 * KIB * (1 - u % 2))
+                if i + 3 < SLICES:
+                    second = placed(f"silu_second{i}", [P, HALF], F32, ROW_AREA[i + 2], ROWS_END)
                 else:
                     second = keep.tile([P, HALF], F32, name="silu_second", tag="picked0", align_bytes=64)
                 for half, tile in enumerate((first, second)):
                     silu_neg[i, half] = tile[:]
                     nc.scalar.activation(out=tile[:], in_=s[:, half * HALF : (half + 1) * HALF], func=ACT.Silu, scale=-1.0)
             else:
-                scaled_h[u] = placed("scaled_h_last", [P, PAIR, S], F32, i, 4 * KIB)
+                scaled_h[u] = placed("scaled_h_last", [P, PAIR, S], F32, ROW_AREA[i], 4 * KIB)
                 for half in range(HALVES):
                     silu_neg[i, half] = scaled_h[u][:, e, half * HALF : (half + 1) * HALF]
                 nc.scalar.activation(out=scaled_h[u][:, e, :], in_=s, func=ACT.Silu, scale=-1.0)
                 nc.scalar.activation(out=neg_tanh[u][:, e, :], in_=s, func=ACT.Tanh, scale=-0.5)
 
-        def first_product(i):
+        def first_product(i, half):
             a, t = divmod(i, PACK)
+            cols = slice(half * HALF, (half + 1) * HALF)
+            h[i, half] = h_psum.tile([P, HALF], F32, name="h")
+            for g in range(K_PASSES):
+                w_cols = slice(g * PASS + t * P, g * PASS + (t + 1) * P)
+                nc.tensor.matmul_mx(
+                    out=h[i, half][:],
+                    lhsT=w1_codes[a][:, w_cols].bitcast(E4M3X4),
+                    lhsT_scale=w1_planes[a][:, w_cols],
+                    rhs=v_words[g][:, cols].bitcast(E5M2X4),
+                    rhs_scale=v_planes[g][:, cols],
+                    start=(g == 0),
+                    stop=(g == K_PASSES - 1),
+                )
+
+        def scale_h(i):
             u, e = divmod(i, PAIR)
-            if e == 0 and u < PAIRS - 1:
-                scaled_h[u] = placed(f"scaled_h{u}", [P, PAIR, S], F32, i + PAIR)
+            if e == 0 and u < LAST_PAIR:
+                scaled_h[u] = placed(f"scaled_h{u}", [P, PAIR, S], F32, ROW_AREA[i + PAIR])
             for half in range(HALVES):
                 cols = slice(half * HALF, (half + 1) * HALF)
-                h = h_psum.tile([P, HALF], F32, name="h")
-                for g in range(K_PASSES):
-                    w_cols = slice(g * PASS + t * P, g * PASS + (t + 1) * P)
-                    nc.tensor.matmul_mx(
-                        out=h[:],
-                        lhsT=w1_codes[a][:, w_cols].bitcast(E4M3X4),
-                        lhsT_scale=w1_planes[a][:, w_cols],
-                        rhs=v_words[g][:, cols].bitcast(E5M2X4),
-                        rhs_scale=v_planes[g][:, cols],
-                        start=(g == 0),
-                        stop=(g == K_PASSES - 1),
-                    )
                 nc.vector.scalar_tensor_tensor(
-                    out=scaled_h[u][:, e, cols], in0=silu_neg[i, half], scalar=1.0, in1=h[:], op0=ALU.subtract, op1=ALU.mult
+                    out=scaled_h[u][:, e, cols], in0=silu_neg[i, half], scalar=1.0, in1=h[i, half][:], op0=ALU.subtract, op1=ALU.mult
                 )
 
         def pair_out(u, c0, c1):
-            a, w = divmod(u, PACK // PAIR)
-            if a < LAST:
+            a, w = divmod(u, PASS_PAIRS)
+            if a < LAST_PASS:
                 if a not in z_pairs:
-                    z_pairs[a] = keep.tile([P, PACK // PAIR, S * PAIR], BF16, name=f"z_pairs{a}", align_bytes=64)
+                    z_pairs[a] = keep.tile([P, PASS_PAIRS, S * PAIR], BF16, name=f"z_pairs{a}", align_bytes=64)
                 return z_pairs[a][:, w, PAIR * c0 : PAIR * c1]
             half = c0 // HALF
             if w == 0 and half == 0:
-                z_pairs[a, half] = placed("last_pairs", [P, PACK // PAIR, HALF * PAIR], BF16, SLICES - 1)
+                z_pairs[a, half] = placed("last_pairs", [P, PASS_PAIRS, HALF * PAIR], BF16, ROW_AREA[LAST_SLICE])
             elif w == 0:
-                z_pairs[a, half] = keep.tile([P, PACK // PAIR, HALF * PAIR], BF16, name="last_pairs1", tag="z_pairs0", align_bytes=64)
+                z_pairs[a, half] = keep.tile([P, PASS_PAIRS, HALF * PAIR], BF16, name="last_pairs1", tag="z_pairs0", align_bytes=64)
             return z_pairs[a, half][:, w, :]
 
         def finish_on_vector(u, half):
@@ -214,19 +230,21 @@ def tile_list_nack_silu_backward_kernel(tc, tab_words, tab_scales, w1, w2_words,
             )
 
         def join_pairs(a, half):
-            if half == 0 and a < LAST:
-                z_bf[a] = placed(f"z_bf{a}", [P, S * PACK], BF16, 5 + 2 * a, 2 * KIB)
+            if half == 0 and a < LAST_PASS:
+                z_bf[a] = placed(f"z_bf{a}", [P, S * PACK], BF16, ROW_AREA[5 + PAIR * a], 2 * KIB)
             elif half == 0:
                 z_bf[a] = keep.tile([P, S * PACK], BF16, name="z_bf", tag="grouped", align_bytes=64)
-            pairs = z_pairs[a][:, :, half * HALF * PAIR : (half + 1) * HALF * PAIR] if a < LAST else z_pairs[a, half][:]
+            pairs = z_pairs[a][:, :, half * HALF * PAIR : (half + 1) * HALF * PAIR] if a < LAST_PASS else z_pairs[a, half][:]
             nc.scalar.copy(
-                out=z_bf[a][:, half * HALF * PACK : (half + 1) * HALF * PACK].bitcast(U32).rearrange("p (c w) -> p c w", w=PACK // PAIR),
+                out=z_bf[a][:, half * HALF * PACK : (half + 1) * HALF * PACK].bitcast(U32).rearrange("p (c w) -> p c w", w=PASS_PAIRS),
                 in_=pairs.bitcast(U32).rearrange("p w c -> p c w"),
             )
 
         def z_tiles(a):
-            if a < LAST:
-                z_codes[a] = placed(f"z_codes{a}", [P, S], U32, (7, SLICES - 1)[a], (10, 8)[a] * KIB)
+            if a == 0:
+                z_codes[a] = placed("z_codes0", [P, S], U32, ROW_AREA[7], ROWS_END + 2 * KIB)
+            elif a < LAST_PASS:
+                z_codes[a] = placed("z_codes1", [P, S], U32, ROW_AREA[LAST_SLICE], ROWS_END)
             else:
                 z_codes[a] = keep.tile([P, S], U32, name="z_codes", tag="codes", align_bytes=64)
             z_planes[a] = keep.tile([P, S], U8, name="z_plane", tag=f"plane{a}", align_bytes=64)
@@ -247,7 +265,7 @@ def tile_list_nack_silu_backward_kernel(tc, tab_words, tab_scales, w1, w2_words,
                     rhs=z_codes[a][:, cols].bitcast(E4M3X4),
                     rhs_scale=z_planes[a][:, cols],
                     start=(a == 0),
-                    stop=(a == LAST),
+                    stop=(a == LAST_PASS),
                 )
             y_sb = work.tile([P, HALF], F32, name="y_sb", tag="tanh", align_bytes=64)
             nc.scalar.activation(out=y_sb[:], in_=y[:], func=ACT.Copy, scale=0.5)
@@ -267,54 +285,59 @@ def tile_list_nack_silu_backward_kernel(tc, tab_words, tab_scales, w1, w2_words,
             gather_table(g)
         for i in range(1, SLICES):
             a, t = divmod(i, PACK)
-            if a < LAST and t % PAIR == 1:
+            if a < LAST_PASS and t % PAIR == 1:
                 round_w1(t // PAIR, a + 1)
             gather_s(i)
             u = i // PAIR
-            if i % PAIR == 1 and PAIR < i < SLICES - 1:
-                shifted = placed(f"shifted{i}", [P, PAIR, SPLIT], F32, i)
-                nc.gpsimd.tensor_scalar(shifted[:], neg_tanh[u - 1][:, :, :SPLIT], 1.0, -1.0, ALU.mult, ALU.add)
-                finish_on_gpsimd(u - 1, 0, SPLIT, shifted[:])
-            if i == SLICES - 1:
+            if i % PAIR == 1 and PAIR < i < LAST_SLICE:
+                shifted = placed(f"shifted{i}", [P, PAIR, LATE], F32, ROW_AREA[i])
+                nc.gpsimd.tensor_scalar(shifted[:], neg_tanh[u - 1][:, :, :LATE], 1.0, -1.0, ALU.mult, ALU.add)
+                finish_on_gpsimd(u - 1, 0, LATE, shifted[:])
+            if i == LAST_SLICE:
                 finish_on_gpsimd(u - 1, 0, HALF, neg_tanh[u - 1][:, :, :HALF])
             activations(i)
-            if i % PAIR == 1 and i < SLICES - 1:
-                shift_on_scalar(u, SPLIT if u < PAIRS - 2 else 0)
+            if i % PAIR == 1 and i < LAST_SLICE:
+                shift_on_scalar(u, LATE if u < LAST_PAIR - 1 else 0)
             if i % PAIR == 0:
-                first_product(i - 2)
+                for j in (i - 1, i - 2):
+                    for half in reversed(range(HALVES)):
+                        first_product(j, half)
+                scale_h(i - 2)
                 if a > 0 and t == 0:
                     quantize_w1(a)
-                if i == SLICES - 2:
+                if i == SLICES - PAIR:
                     z_tiles(0)
                     quantize_z(0, 0, S)
-                first_product(i - 1)
-                c0 = SPLIT if u - 1 < PAIRS - 2 else HALF
+                scale_h(i - 1)
+                c0 = LATE if u - 1 < LAST_PAIR - 1 else HALF
                 finish_on_gpsimd(u - 1, c0, S, neg_tanh[u - 1][:, :, c0:])
-            if i in (SLICES - 4, SLICES - 2):
-                done = (i - SLICES + 4) // PAIR
+            if a == LAST_PASS and i % PAIR == 0:
                 for half in range(HALVES):
-                    join_pairs(done, half)
+                    join_pairs(t // PAIR, half)
+
         for j in range(SLICES - PAIR, SLICES):
-            first_product(j)
+            for half in range(HALVES):
+                first_product(j, half)
+            scale_h(j)
         for half in range(HALVES):
-            finish_on_vector(PAIRS - 1, half)
-        z_tiles(1)
-        z_tiles(LAST)
+            finish_on_vector(LAST_PAIR, half)
+        for a in range(1, H_PASSES):
+            z_tiles(a)
         for half in range(HALVES):
-            join_pairs(LAST, half)
+            join_pairs(LAST_PASS, half)
             for a in range(1, H_PASSES):
                 quantize_z(a, half * HALF, (half + 1) * HALF)
 
-        w2_codes = placed("w2_codes", [P, H_PASSES, N], I32, 6)
+        w2_codes = placed("w2_codes", [P, H_PASSES, N], I32, ROW_AREA[6])
         nc.sync.dma_start(out=w2_codes[:], in_=w2_words.rearrange("a p c i -> p a (c i)").bitcast(I32))
-        w2_planes = placed("w2_planes", [P, H_PASSES * N], U8, 6, 6 * KIB)
+        w2_planes = placed("w2_planes", [P, H_PASSES * N], U8, ROW_AREA[6], 4 * H_PASSES * N)
         nc.gpsimd.memset(w2_planes[:].bitcast(I32), 0)
         for q in range(QUADRANTS):
             nc.sync.dma_start(
                 out=w2_planes[32 * q : 32 * q + 4, :].bitcast(I32).rearrange("r (a n) -> r a n", a=H_PASSES),
                 in_=w2_scales[:, 4 * q : 4 * q + 4, :].bitcast(I32).rearrange("a r n -> r a n"),
             )
-        weights = placed("weights", [P, S], F32, 8)
+        weights = placed("weights", [P, S], F32, ROW_AREA[8])
         nc.sync.dma_start(out=weights[:], in_=wgo)
         idx2 = keep.tile([P, S // 16], U16, name="idx2")
         nc.sync.dma_start(idx2[:], offs2)

@@ -34,26 +34,30 @@ LAST_PASS = H_PASSES - 1
 LAST_PAIR = PAIRS - 1
 LAST_SLICE = SLICES - 1
 
-LOAD_BUFS = 4
 H_BANKS = 6
-TANH_BUFS = 3
-LATE = 576
-RUN = 4
+Y_BUFS = 3
+RUN = 2
 ODD_SPLIT = T2 // 2 + 1
+COPY_SCATTERS = 2
 
 KIB = 1024
-ROWS_END = 8 * KIB
-AREA_KIB = (8, 12, 12, 12, 8, 14, 8, 14, 6)
-ROW_AREA = (0, 1, 2, 3, 4, 5, 6, 7, 0, 1, 3, 2)
-ODD_AREA = 8
+AREA = 8 * KIB
+ROW_AREA = (0, 5, 6, 7, 8, 0, 2, 4, 5, 7, 9, 0)
+WORD_AREA = (1, 3)
+RAW_AREA = (2, 4, 9, 1, 3, 6)
+TANH_AT = 80 * KIB
+PICKED_AT = 104 * KIB
+CODES_AT = 132 * KIB
+HALVES_AT = 136 * KIB
+Z_AT = 142 * KIB
+YW_AT = 158 * KIB
 
 
 def tile_list_nack_silu_backward_kernel(tc, tab_words, tab_scales, w1, w2_words, w2_scales, sT, wgo, offs, offs2, out):
     nc = tc.nc
     with ExitStack() as ctx:
         keep = ctx.enter_context(tc.tile_pool(name="keep", bufs=1))
-        stream = ctx.enter_context(tc.tile_pool(name="stream", bufs=LOAD_BUFS))
-        work = ctx.enter_context(tc.tile_pool(name="work", bufs=TANH_BUFS))
+        work = ctx.enter_context(tc.tile_pool(name="work", bufs=Y_BUFS))
         arena = ctx.enter_context(tc.tile_pool(name="arena", bufs=1))
         h_psum = ctx.enter_context(tc.psum_pool(name="h_psum", bufs=H_BANKS))
         y_psum = ctx.enter_context(tc.psum_pool(name="y_psum", bufs=8 - H_BANKS))
@@ -82,27 +86,28 @@ def tile_list_nack_silu_backward_kernel(tc, tab_words, tab_scales, w1, w2_words,
         grouped = {}
         w1_codes = {}
         w1_planes = {}
+        rows = {}
         picked = {}
-        h = {}
         silu_neg = {}
         neg_tanh = {}
         scaled_h = {}
         z_bf = {}
-        z_pairs = {}
         z_codes = {}
         z_planes = {}
 
-        def placed(name, shape, dtype, area, start=0):
-            offset = KIB * sum(AREA_KIB[:area]) + start
+        def placed(name, shape, dtype, offset):
             return arena.tile(shape, dtype, name=name, offset=offset, align_bytes=64)
 
+        def cols_of(half):
+            return slice(half * HALF, (half + 1) * HALF)
+
         def gather_table(g):
-            words = stream.tile([P, T], I32, name="words", tag="load", align_bytes=64)
+            words = placed(f"words{g}", [P, T], I32, AREA * WORD_AREA[g])
             nc.sync.dma_start(out=words[:], in_=tab_words[g].rearrange("p t i -> p (t i)").bitcast(I32))
             nc.vector.tensor_copy(v_words[g][:], words[:].bitcast(U32).indirect(idx[:]))
 
         def round_w1(g, a):
-            raw = stream.tile([P, PACK, PASS], F32, name="raw", tag="load", align_bytes=64)
+            raw = placed(f"raw{a}{g}", [P, PACK, PASS], F32, AREA * RAW_AREA[K_PASSES * a + g])
             nc.sync.dma_start(
                 out=raw[:],
                 in_=w1[g * PASS : (g + 1) * PASS, a * PASS : (a + 1) * PASS].rearrange("(p j) c -> p j c", j=PACK),
@@ -116,66 +121,77 @@ def tile_list_nack_silu_backward_kernel(tc, tab_words, tab_scales, w1, w2_words,
             )
 
         def quantize_w1(a):
-            if a < LAST_PASS:
-                w1_codes[a] = keep.tile([P, K_PASSES * PASS], U32, name="w1_codes", tag=("codes", "picked2")[a], align_bytes=64)
+            if a == 0:
+                w1_codes[a] = keep.tile([P, K_PASSES * PASS], U32, name="w1_codes", align_bytes=64)
             else:
-                w1_codes[a] = placed("w1_codes_last", [P, K_PASSES * PASS], U32, ROW_AREA[PACK * a - 3], ROWS_END + 2 * KIB)
-            w1_planes[a] = keep.tile([P, K_PASSES * PASS], U8, name="w1_plane", tag=f"plane{a}", align_bytes=64)
+                w1_codes[a] = placed(f"w1_codes{a}", [P, K_PASSES * PASS], U32, (PICKED_AT, CODES_AT)[a - 1])
+            w1_planes[a] = keep.tile([P, K_PASSES * PASS], U8, name=f"w1_plane{a}", align_bytes=64)
             nc.vector.quantize_mx(out=w1_codes[a][:].bitcast(E4M3X4), scales=w1_planes[a][:], in_=grouped[a][:])
 
+        def load_rows(i):
+            a, t = divmod(i, PACK)
+            rows[i] = placed(f"rows{i}", [P, T], F32, AREA * ROW_AREA[i])
+            nc.sync.dma_start(out=rows[i][:], in_=sT[a * PASS : (a + 1) * PASS, :].rearrange("(p t) n -> p t n", t=PACK)[:, t, :])
+
         def gather_s(i):
-            a, t = divmod(i, PACK)
-            rows = placed(f"rows{i}", [P, T], F32, ROW_AREA[i])
-            nc.sync.dma_start(out=rows[:], in_=sT[a * PASS : (a + 1) * PASS, :].rearrange("(p t) n -> p t n", t=PACK)[:, t, :])
-            if i % PAIR == 0 and i > PAIR:
-                picked[i] = placed(f"picked{i}", [P, S], F32, ROW_AREA[i - 1], ROWS_END)
-            elif i % PAIR == 0:
-                picked[i] = keep.tile([P, S], F32, name="picked", tag=f"picked{i}", align_bytes=64)
-            else:
-                picked[i] = placed(f"picked{i}", [P, S], F32, ODD_AREA, 2 * KIB * (i // PAIR % 2))
-            nc.vector.tensor_copy(picked[i][:], rows[:].indirect(idx[:]))
+            load_rows(i)
+            slot = {7: 2, 8: 3, 11: 1}.get(i, i)
+            whole = placed(f"picked{i}", [P, S], F32, PICKED_AT + 4 * KIB * slot)
+            nc.vector.tensor_copy(whole[:], rows[i][:].indirect(idx[:]))
+            for half in range(HALVES):
+                picked[i, half] = whole[:, cols_of(half)]
 
-        def activations(i):
-            u, e = divmod(i, PAIR)
-            if e == 0:
-                neg_tanh[u] = work.tile([P, PAIR, S], F32, name="neg_tanh", tag="tanh", align_bytes=64)
-            s = picked[i][:]
-            if 0 < i < LAST_SLICE:
-                nc.scalar.activation(out=neg_tanh[u][:, e, :], in_=s, func=ACT.Tanh, scale=-0.5)
-            if i == 0:
-                whole = placed("silu_whole", [P, S], F32, ROW_AREA[5], ROWS_END)
-                nc.scalar.activation(out=whole[:], in_=s, func=ACT.Silu, scale=-1.0)
-                nc.scalar.activation(out=neg_tanh[u][:, e, :], in_=s, func=ACT.Tanh, scale=-0.5)
-                for half in range(HALVES):
-                    silu_neg[i, half] = whole[:, half * HALF : (half + 1) * HALF]
-            elif e == 0:
+        def gather_half(i, half):
+            if half == 0:
+                load_rows(i)
+            part = placed(f"picked{i}_{half}", [P, HALF], F32, HALVES_AT + 2 * KIB * (i - 9 + half))
+            nc.vector.tensor_copy(part[:], rows[i][:].indirect(idx[:, half * LIST_COLS : (half + 1) * LIST_COLS]))
+            picked[i, half] = part[:]
+
+        silu_at = {
+            0: PICKED_AT + 26 * KIB,
+            2: PICKED_AT + 20 * KIB,
+            3: PICKED_AT + 24 * KIB,
+            4: CODES_AT,
+            6: HALVES_AT,
+            7: HALVES_AT + 2 * KIB,
+            11: HALVES_AT + 4 * KIB,
+        }
+
+        def activations(i, half):
+            a, t = divmod(i, PACK)
+            if (a, half) not in neg_tanh:
+                slot = len(neg_tanh) % 3
+                neg_tanh[a, half] = placed(f"neg_tanh{a}{half}", [P, PACK, HALF], F32, TANH_AT + AREA * slot)
+            s = picked[i, half]
+            if half == 0 and i in silu_at:
+                apart = placed(f"silu{i}", [P, HALF], F32, silu_at[i])
+                silu_neg[i, half] = apart[:]
+                nc.scalar.activation(out=apart[:], in_=s, func=ACT.Silu, scale=-1.0)
+                nc.scalar.activation(out=neg_tanh[a, half][:, t, :], in_=s, func=ACT.Tanh, scale=-0.5)
+            else:
+                silu_neg[i, half] = s
+                nc.scalar.activation(out=neg_tanh[a, half][:, t, :], in_=s, func=ACT.Tanh, scale=-0.5)
                 nc.scalar.activation(out=s, in_=s, func=ACT.Silu, scale=-1.0)
-                for half in range(HALVES):
-                    silu_neg[i, half] = s[:, half * HALF : (half + 1) * HALF]
-            elif i < LAST_SLICE:
-                first = placed(f"silu_first{i}", [P, HALF], F32, ODD_AREA, 4 * KIB * (1 - u % 2))
-                if i + 3 < SLICES:
-                    second = placed(f"silu_second{i}", [P, HALF], F32, ROW_AREA[i + 2], ROWS_END)
-                else:
-                    second = keep.tile([P, HALF], F32, name="silu_second", tag="picked0", align_bytes=64)
-                for half, tile in enumerate((first, second)):
-                    silu_neg[i, half] = tile[:]
-                    nc.scalar.activation(out=tile[:], in_=s[:, half * HALF : (half + 1) * HALF], func=ACT.Silu, scale=-1.0)
-            else:
-                scaled_h[u] = placed("scaled_h_last", [P, PAIR, S], F32, ROW_AREA[i], 4 * KIB)
-                for half in range(HALVES):
-                    silu_neg[i, half] = scaled_h[u][:, e, half * HALF : (half + 1) * HALF]
-                nc.scalar.activation(out=scaled_h[u][:, e, :], in_=s, func=ACT.Silu, scale=-1.0)
-                nc.scalar.activation(out=neg_tanh[u][:, e, :], in_=s, func=ACT.Tanh, scale=-0.5)
 
-        def first_product(i, half):
+        def shift_on_scalar(a, half, t0, t1):
+            part = neg_tanh[a, half][:, t0:t1, :]
+            nc.scalar.activation(out=part, in_=part, func=ACT.Copy, bias=-1.0)
+
+        def shift_on_gpsimd(a, half, t0, t1):
+            part = neg_tanh[a, half][:, t0:t1, :]
+            nc.gpsimd.tensor_scalar(part, part, 1.0, -1.0, ALU.mult, ALU.add)
+
+        scaled_area = {(0, 0): 4, (0, 1): 6, (1, 0): 8, (2, 0): 11, (1, 1): 9, (2, 1): 10}
+
+        def scale_h(i, half):
             a, t = divmod(i, PACK)
-            cols = slice(half * HALF, (half + 1) * HALF)
-            h[i, half] = h_psum.tile([P, HALF], F32, name="h")
+            cols = cols_of(half)
+            h = h_psum.tile([P, HALF], F32, name="h")
             for g in range(K_PASSES):
                 w_cols = slice(g * PASS + t * P, g * PASS + (t + 1) * P)
                 nc.tensor.matmul_mx(
-                    out=h[i, half][:],
+                    out=h[:],
                     lhsT=w1_codes[a][:, w_cols].bitcast(E4M3X4),
                     lhsT_scale=w1_planes[a][:, w_cols],
                     rhs=v_words[g][:, cols].bitcast(E5M2X4),
@@ -183,99 +199,80 @@ def tile_list_nack_silu_backward_kernel(tc, tab_words, tab_scales, w1, w2_words,
                     start=(g == 0),
                     stop=(g == K_PASSES - 1),
                 )
-
-        def scale_h(i):
-            u, e = divmod(i, PAIR)
-            if e == 0 and u < LAST_PAIR:
-                scaled_h[u] = placed(f"scaled_h{u}", [P, PAIR, S], F32, ROW_AREA[i + PAIR])
-            for half in range(HALVES):
-                cols = slice(half * HALF, (half + 1) * HALF)
-                nc.vector.scalar_tensor_tensor(
-                    out=scaled_h[u][:, e, cols], in0=silu_neg[i, half], scalar=1.0, in1=h[i, half][:], op0=ALU.subtract, op1=ALU.mult
-                )
-
-        def pair_out(u, c0, c1):
-            a, w = divmod(u, PASS_PAIRS)
-            if a < LAST_PASS:
-                if a not in z_pairs:
-                    z_pairs[a] = keep.tile([P, PASS_PAIRS, S * PAIR], BF16, name=f"z_pairs{a}", align_bytes=64)
-                return z_pairs[a][:, w, PAIR * c0 : PAIR * c1]
-            half = c0 // HALF
-            if w == 0 and half == 0:
-                z_pairs[a, half] = placed("last_pairs", [P, PASS_PAIRS, HALF * PAIR], BF16, ROW_AREA[LAST_SLICE])
-            elif w == 0:
-                z_pairs[a, half] = keep.tile([P, PASS_PAIRS, HALF * PAIR], BF16, name="last_pairs1", tag="z_pairs0", align_bytes=64)
-            return z_pairs[a, half][:, w, :]
-
-        def finish_on_vector(u, half):
-            cols = slice(half * HALF, (half + 1) * HALF)
+            if t == 0:
+                scaled_h[a, half] = placed(f"scaled_h{a}{half}", [P, PACK, HALF], F32, AREA * ROW_AREA[scaled_area[a, half]])
             nc.vector.scalar_tensor_tensor(
-                out=pair_out(u, half * HALF, (half + 1) * HALF).rearrange("p (c e) -> p c e", e=PAIR),
-                in0=neg_tanh[u][:, :, cols].rearrange("p e c -> p c e"),
-                scalar=1.0,
-                in1=scaled_h[u][:, :, cols].rearrange("p e c -> p c e"),
-                op0=ALU.subtract,
-                op1=ALU.mult,
+                out=scaled_h[a, half][:, t, :], in0=silu_neg[i, half], scalar=1.0, in1=h[:], op0=ALU.subtract, op1=ALU.mult
             )
 
-        def shift_on_scalar(u, c0):
-            nc.scalar.activation(out=neg_tanh[u][:, :, c0:], in_=neg_tanh[u][:, :, c0:], func=ACT.Copy, bias=-1.0)
+        z_first = placed("z_first", [P, 2 * HALF * PACK], BF16, Z_AT)
 
-        def finish_on_gpsimd(u, c0, c1, factor):
+        def finish(a, half):
+            if half == 0 and a < LAST_PASS:
+                z_bf[a, half] = z_first[:, a * HALF * PACK : (a + 1) * HALF * PACK]
+            else:
+                start = {(2, 0): 8, (0, 1): 12, (1, 1): 8, (2, 1): 0}[a, half]
+                tile = placed(f"z_bf{a}{half}", [P, HALF * PACK], BF16, Z_AT + start * KIB)
+                z_bf[a, half] = tile[:]
             nc.gpsimd.tensor_tensor(
-                out=pair_out(u, c0, c1).rearrange("p (c r e) -> p c e r", r=RUN, e=PAIR),
-                in0=factor.rearrange("p e (c r) -> p c e r", r=RUN),
-                in1=scaled_h[u][:, :, c0:c1].rearrange("p e (c r) -> p c e r", r=RUN),
+                out=z_bf[a, half].rearrange("p (c r t) -> p c t r", r=RUN, t=PACK),
+                in0=neg_tanh[a, half][:].rearrange("p t (c r) -> p c t r", r=RUN),
+                in1=scaled_h[a, half][:].rearrange("p t (c r) -> p c t r", r=RUN),
                 op=ALU.mult,
             )
 
-        def join_pairs(a, half):
-            if half == 0 and a < LAST_PASS:
-                z_bf[a] = placed(f"z_bf{a}", [P, S * PACK], BF16, ROW_AREA[5 + PAIR * a], 2 * KIB)
-            elif half == 0:
-                z_bf[a] = keep.tile([P, S * PACK], BF16, name="z_bf", tag="grouped", align_bytes=64)
-            pairs = z_pairs[a][:, :, half * HALF * PAIR : (half + 1) * HALF * PAIR] if a < LAST_PASS else z_pairs[a, half][:]
-            nc.scalar.copy(
-                out=z_bf[a][:, half * HALF * PACK : (half + 1) * HALF * PACK].bitcast(U32).rearrange("p (c w) -> p c w", w=PASS_PAIRS),
-                in_=pairs.bitcast(U32).rearrange("p w c -> p c w"),
-            )
+        def quantize_first():
+            codes = placed("z_codes_first", [P, 2 * HALF], U32, PICKED_AT + 8 * KIB)
+            plane = keep.tile([P, 2 * HALF], U8, name="z_plane_first", align_bytes=64)
+            nc.vector.quantize_mx(out=codes[:].bitcast(E4M3X4), scales=plane[:], in_=z_first[:])
+            for a in range(LAST_PASS):
+                z_codes[a, 0] = codes[:, cols_of(a)]
+                z_planes[a, 0] = plane[:, cols_of(a)]
 
-        def z_tiles(a):
-            if a == 0:
-                z_codes[a] = placed("z_codes0", [P, S], U32, ROW_AREA[7], ROWS_END + 2 * KIB)
-            elif a < LAST_PASS:
-                z_codes[a] = placed("z_codes1", [P, S], U32, ROW_AREA[LAST_SLICE], ROWS_END)
-            else:
-                z_codes[a] = keep.tile([P, S], U32, name="z_codes", tag="codes", align_bytes=64)
-            z_planes[a] = keep.tile([P, S], U8, name="z_plane", tag=f"plane{a}", align_bytes=64)
-
-        def quantize_z(a, c0, c1):
-            nc.vector.quantize_mx(
-                out=z_codes[a][:, c0:c1].bitcast(E4M3X4), scales=z_planes[a][:, c0:c1], in_=z_bf[a][:, PACK * c0 : PACK * c1]
-            )
+        def quantize_z(a, half):
+            start = {(2, 0): PICKED_AT + 12 * KIB, (0, 1): YW_AT, (1, 1): YW_AT + 2 * KIB, (2, 1): YW_AT + 4 * KIB}[a, half]
+            codes = placed(f"z_codes{a}{half}", [P, HALF], U32, start)
+            plane = keep.tile([P, HALF], U8, name=f"z_plane{a}{half}", align_bytes=64)
+            nc.vector.quantize_mx(out=codes[:].bitcast(E4M3X4), scales=plane[:], in_=z_bf[a, half])
+            z_codes[a, half] = codes[:]
+            z_planes[a, half] = plane[:]
 
         def second_product(n, half):
-            cols = slice(half * HALF, (half + 1) * HALF)
             y = y_psum.tile([P, HALF], F32, name="y")
             for a in range(H_PASSES):
                 nc.tensor.matmul_mx(
                     out=y[:],
                     lhsT=w2_codes[:, a, n * P : (n + 1) * P].bitcast(E4M3X4),
                     lhsT_scale=w2_planes[:, a * N + n * P : a * N + (n + 1) * P],
-                    rhs=z_codes[a][:, cols].bitcast(E4M3X4),
-                    rhs_scale=z_planes[a][:, cols],
+                    rhs=z_codes[a, half].bitcast(E4M3X4),
+                    rhs_scale=z_planes[a, half],
                     start=(a == 0),
                     stop=(a == LAST_PASS),
                 )
-            y_sb = work.tile([P, HALF], F32, name="y_sb", tag="tanh", align_bytes=64)
+            return y
+
+        def places(n, half):
+            return pages[n][:].indirect(idx2[:, half * LIST_COLS : (half + 1) * LIST_COLS])
+
+        def weigh(n):
+            y = second_product(n, 0)
+            weighed = placed(f"weighed{n}", [P, HALF], F32, YW_AT + (1 + 3 * n) * KIB)
+            nc.vector.scalar_tensor_tensor(
+                out=weighed[:], in0=y[:], scalar=0.5, in1=weights[:, cols_of(0)], op0=ALU.mult, op1=ALU.mult
+            )
+            return weighed
+
+        def weigh_and_place(n, half):
+            y = second_product(n, half)
+            y_sb = work.tile([P, HALF], F32, name="y_sb", align_bytes=64)
             nc.scalar.activation(out=y_sb[:], in_=y[:], func=ACT.Copy, scale=0.5)
-            places = pages[n][:].indirect(idx2[:, half * LIST_COLS : (half + 1) * LIST_COLS])
-            nc.vector.tensor_tensor(places, y_sb[:], weights[:, cols], ALU.mult)
+            nc.vector.tensor_tensor(places(n, half), y_sb[:], weights[:, cols_of(half)], ALU.mult)
             if half == HALVES - 1:
                 nc.sync.dma_start(out=out[n * P : (n + 1) * P, :], in_=pages[n][:])
 
         gather_s(0)
-        activations(0)
+        for half in range(HALVES):
+            activations(0, half)
         for g in range(K_PASSES):
             nc.vector.tensor_copy(v_planes[g][:], tab_planes[:, g * T : (g + 1) * T].indirect(idx[:]))
         for g in range(K_PASSES):
@@ -283,65 +280,90 @@ def tile_list_nack_silu_backward_kernel(tc, tab_words, tab_scales, w1, w2_words,
             if g == K_PASSES - 1:
                 quantize_w1(0)
             gather_table(g)
-        for i in range(1, SLICES):
-            a, t = divmod(i, PACK)
-            if a < LAST_PASS and t % PAIR == 1:
-                round_w1(t // PAIR, a + 1)
+        for i in range(1, PACK):
             gather_s(i)
-            u = i // PAIR
-            if i % PAIR == 1 and PAIR < i < LAST_SLICE:
-                shifted = placed(f"shifted{i}", [P, PAIR, LATE], F32, ROW_AREA[i])
-                nc.gpsimd.tensor_scalar(shifted[:], neg_tanh[u - 1][:, :, :LATE], 1.0, -1.0, ALU.mult, ALU.add)
-                finish_on_gpsimd(u - 1, 0, LATE, shifted[:])
-            if i == LAST_SLICE:
-                finish_on_gpsimd(u - 1, 0, HALF, neg_tanh[u - 1][:, :, :HALF])
-            activations(i)
-            if i % PAIR == 1 and i < LAST_SLICE:
-                shift_on_scalar(u, LATE if u < LAST_PAIR - 1 else 0)
-            if i % PAIR == 0:
-                for j in (i - 1, i - 2):
-                    for half in reversed(range(HALVES)):
-                        first_product(j, half)
-                scale_h(i - 2)
-                if a > 0 and t == 0:
-                    quantize_w1(a)
-                if i == SLICES - PAIR:
-                    z_tiles(0)
-                    quantize_z(0, 0, S)
-                scale_h(i - 1)
-                c0 = LATE if u - 1 < LAST_PAIR - 1 else HALF
-                finish_on_gpsimd(u - 1, c0, S, neg_tanh[u - 1][:, :, c0:])
-            if a == LAST_PASS and i % PAIR == 0:
-                for half in range(HALVES):
-                    join_pairs(t // PAIR, half)
-
-        for j in range(SLICES - PAIR, SLICES):
             for half in range(HALVES):
-                first_product(j, half)
-            scale_h(j)
-        for half in range(HALVES):
-            finish_on_vector(LAST_PAIR, half)
-        for a in range(1, H_PASSES):
-            z_tiles(a)
-        for half in range(HALVES):
-            join_pairs(LAST_PASS, half)
-            for a in range(1, H_PASSES):
-                quantize_z(a, half * HALF, (half + 1) * HALF)
+                activations(i, half)
+                if i % 2 == 1:
+                    shift_on_gpsimd(0, half, i - 1, i + 1)
+        gather_s(4)
+        activations(4, 0)
+        for g in range(K_PASSES):
+            round_w1(g, 1)
+        for i in range(0, 4):
+            scale_h(i, 0)
+        finish(0, 0)
+        for i in (5, 6):
+            gather_s(i)
+            activations(i, 0)
+        for i in range(0, 4):
+            scale_h(i, 1)
+            if i == 1:
+                quantize_w1(1)
+        finish(0, 1)
+        for g in range(K_PASSES):
+            round_w1(g, 2)
+        gather_s(7)
+        activations(7, 0)
+        shift_on_scalar(1, 0, 0, PACK)
+        gather_s(8)
+        activations(8, 0)
+        for i in range(4, 8):
+            scale_h(i, 0)
+            if i == 5:
+                quantize_w1(2)
+        finish(1, 0)
+        activations(4, 1)
+        activations(5, 1)
+        for i in (9, 10):
+            gather_half(i, 0)
+            activations(i, 0)
+        shift_on_gpsimd(2, 0, 0, 3)
+        activations(6, 1)
+        gather_s(11)
+        activations(11, 0)
+        shift_on_gpsimd(2, 0, 3, 4)
+        for i in range(8, 12):
+            scale_h(i, 0)
+        finish(2, 0)
+        activations(7, 1)
+        shift_on_scalar(1, 1, 0, PACK)
+        activations(8, 1)
+        activations(11, 1)
+        for i in (9, 10):
+            gather_half(i, 1)
+            activations(i, 1)
+        shift_on_scalar(2, 1, 0, PACK)
 
-        w2_codes = placed("w2_codes", [P, H_PASSES, N], I32, ROW_AREA[6])
+        w2_codes = placed("w2_codes", [P, H_PASSES, N], I32, AREA * ROW_AREA[6])
         nc.sync.dma_start(out=w2_codes[:], in_=w2_words.rearrange("a p c i -> p a (c i)").bitcast(I32))
-        w2_planes = placed("w2_planes", [P, H_PASSES * N], U8, ROW_AREA[6], 4 * H_PASSES * N)
+        w2_planes = placed("w2_planes", [P, H_PASSES * N], U8, AREA * ROW_AREA[6] + 4 * H_PASSES * N)
         nc.gpsimd.memset(w2_planes[:].bitcast(I32), 0)
         for q in range(QUADRANTS):
             nc.sync.dma_start(
                 out=w2_planes[32 * q : 32 * q + 4, :].bitcast(I32).rearrange("r (a n) -> r a n", a=H_PASSES),
                 in_=w2_scales[:, 4 * q : 4 * q + 4, :].bitcast(I32).rearrange("a r n -> r a n"),
             )
-        weights = placed("weights", [P, S], F32, ROW_AREA[8])
+        weights = placed("weights", [P, S], F32, AREA * ROW_AREA[7])
         nc.sync.dma_start(out=weights[:], in_=wgo)
         idx2 = keep.tile([P, S // 16], U16, name="idx2")
         nc.sync.dma_start(idx2[:], offs2)
 
-        for half in range(HALVES):
-            for n in range(N_TILES):
-                second_product(n, half)
+        for i in range(4, 9):
+            scale_h(i, 1)
+        quantize_first()
+        quantize_z(2, 0)
+        finish(1, 1)
+        for i in range(9, 12):
+            scale_h(i, 1)
+        finish(2, 1)
+        weighed = [weigh(n) for n in range(COPY_SCATTERS)]
+        for n in range(COPY_SCATTERS):
+            nc.vector.tensor_copy(places(n, 0), weighed[n][:])
+        quantize_z(0, 1)
+        quantize_z(1, 1)
+        weigh_and_place(2, 0)
+        quantize_z(2, 1)
+        weigh_and_place(3, 0)
+        for n in range(N_TILES):
+            weigh_and_place(n, 1)

@@ -38,7 +38,6 @@ H_BANKS = 6
 Y_BUFS = 3
 RUN = 2
 ODD_SPLIT = T2 // 2 + 1
-COPY_SCATTERS = 2
 
 KIB = 1024
 AREA = 8 * KIB
@@ -48,9 +47,9 @@ RAW_AREA = (2, 4, 9, 1, 3, 6)
 TANH_AT = 80 * KIB
 PICKED_AT = 104 * KIB
 CODES_AT = 132 * KIB
-HALVES_AT = 136 * KIB
-Z_AT = 142 * KIB
-YW_AT = 158 * KIB
+NINTH_AT = 136 * KIB
+Z_AT = 140 * KIB
+TANH_LATE_AT = 160 * KIB
 
 
 def tile_list_nack_silu_backward_kernel(tc, tab_words, tab_scales, w1, w2_words, w2_scales, sT, wgo, offs, offs2, out):
@@ -135,8 +134,8 @@ def tile_list_nack_silu_backward_kernel(tc, tab_words, tab_scales, w1, w2_words,
 
         def gather_s(i):
             load_rows(i)
-            slot = {7: 2, 8: 3, 11: 1}.get(i, i)
-            whole = placed(f"picked{i}", [P, S], F32, PICKED_AT + 4 * KIB * slot)
+            slot = {7: 2, 8: 3}.get(i, i)
+            whole = placed(f"picked{i}", [P, S], F32, NINTH_AT if i == 9 else PICKED_AT + 4 * KIB * slot)
             nc.vector.tensor_copy(whole[:], rows[i][:].indirect(idx[:]))
             for half in range(HALVES):
                 picked[i, half] = whole[:, cols_of(half)]
@@ -144,7 +143,7 @@ def tile_list_nack_silu_backward_kernel(tc, tab_words, tab_scales, w1, w2_words,
         def gather_half(i, half):
             if half == 0:
                 load_rows(i)
-            part = placed(f"picked{i}_{half}", [P, HALF], F32, HALVES_AT + 2 * KIB * (i - 9 + half))
+            part = placed(f"picked{i}_{half}", [P, HALF], F32, PICKED_AT + KIB * (24 if i == 10 else 8 + 2 * half))
             nc.vector.tensor_copy(part[:], rows[i][:].indirect(idx[:, half * LIST_COLS : (half + 1) * LIST_COLS]))
             picked[i, half] = part[:]
 
@@ -153,16 +152,15 @@ def tile_list_nack_silu_backward_kernel(tc, tab_words, tab_scales, w1, w2_words,
             2: PICKED_AT + 20 * KIB,
             3: PICKED_AT + 24 * KIB,
             4: CODES_AT,
-            6: HALVES_AT,
-            7: HALVES_AT + 2 * KIB,
-            11: HALVES_AT + 4 * KIB,
+            6: NINTH_AT,
+            11: PICKED_AT + 10 * KIB,
         }
 
         def activations(i, half):
             a, t = divmod(i, PACK)
             if (a, half) not in neg_tanh:
-                slot = len(neg_tanh) % 3
-                neg_tanh[a, half] = placed(f"neg_tanh{a}{half}", [P, PACK, HALF], F32, TANH_AT + AREA * slot)
+                start = TANH_LATE_AT if (a, half) == (1, 1) else TANH_AT + AREA * {(0, 0): 0, (0, 1): 1, (1, 0): 2, (2, 0): 0, (2, 1): 1}[a, half]
+                neg_tanh[a, half] = placed(f"neg_tanh{a}{half}", [P, PACK, HALF], F32, start)
             s = picked[i, half]
             if half == 0 and i in silu_at:
                 apart = placed(f"silu{i}", [P, HALF], F32, silu_at[i])
@@ -182,7 +180,7 @@ def tile_list_nack_silu_backward_kernel(tc, tab_words, tab_scales, w1, w2_words,
             part = neg_tanh[a, half][:, t0:t1, :]
             nc.gpsimd.tensor_scalar(part, part, 1.0, -1.0, ALU.mult, ALU.add)
 
-        scaled_area = {(0, 0): 4, (0, 1): 6, (1, 0): 8, (2, 0): 11, (1, 1): 9, (2, 1): 10}
+        scaled_area = {(0, 0): 8, (0, 1): 2, (1, 0): 5, (1, 1): 7, (2, 0): 1, (2, 1): 9}
 
         def scale_h(i, half):
             a, t = divmod(i, PACK)
@@ -200,39 +198,38 @@ def tile_list_nack_silu_backward_kernel(tc, tab_words, tab_scales, w1, w2_words,
                     stop=(g == K_PASSES - 1),
                 )
             if t == 0:
-                scaled_h[a, half] = placed(f"scaled_h{a}{half}", [P, PACK, HALF], F32, AREA * ROW_AREA[scaled_area[a, half]])
+                scaled_h[a, half] = placed(f"scaled_h{a}{half}", [P, PACK, HALF], F32, AREA * scaled_area[a, half])
             nc.vector.scalar_tensor_tensor(
                 out=scaled_h[a, half][:, t, :], in0=silu_neg[i, half], scalar=1.0, in1=h[:], op0=ALU.subtract, op1=ALU.mult
             )
 
-        z_first = placed("z_first", [P, 2 * HALF * PACK], BF16, Z_AT)
+        z_first = [placed(f"z_first{half}", [P, 2 * HALF * PACK], BF16, Z_AT + AREA * half) for half in range(HALVES)]
 
-        def finish(a, half):
-            if half == 0 and a < LAST_PASS:
-                z_bf[a, half] = z_first[:, a * HALF * PACK : (a + 1) * HALF * PACK]
+        def finish(a, half, engine, run):
+            if a < LAST_PASS:
+                z_bf[a, half] = z_first[half][:, a * HALF * PACK : (a + 1) * HALF * PACK]
             else:
-                start = {(2, 0): 8, (0, 1): 12, (1, 1): 8, (2, 1): 0}[a, half]
-                tile = placed(f"z_bf{a}{half}", [P, HALF * PACK], BF16, Z_AT + start * KIB)
+                tile = placed(f"z_last{half}", [P, HALF * PACK], BF16, Z_AT + 2 * AREA * (1 - half))
                 z_bf[a, half] = tile[:]
-            nc.gpsimd.tensor_tensor(
-                out=z_bf[a, half].rearrange("p (c r t) -> p c t r", r=RUN, t=PACK),
-                in0=neg_tanh[a, half][:].rearrange("p t (c r) -> p c t r", r=RUN),
-                in1=scaled_h[a, half][:].rearrange("p t (c r) -> p c t r", r=RUN),
+            engine.tensor_tensor(
+                out=z_bf[a, half].rearrange("p (c r t) -> p c t r", r=run, t=PACK),
+                in0=neg_tanh[a, half][:].rearrange("p t (c r) -> p c t r", r=run),
+                in1=scaled_h[a, half][:].rearrange("p t (c r) -> p c t r", r=run),
                 op=ALU.mult,
             )
 
-        def quantize_first():
-            codes = placed("z_codes_first", [P, 2 * HALF], U32, PICKED_AT + 8 * KIB)
-            plane = keep.tile([P, 2 * HALF], U8, name="z_plane_first", align_bytes=64)
-            nc.vector.quantize_mx(out=codes[:].bitcast(E4M3X4), scales=plane[:], in_=z_first[:])
+        def quantize_first(half):
+            codes = placed(f"z_codes_first{half}", [P, 2 * HALF], U32, (PICKED_AT + 24 * KIB, Z_AT + 2 * AREA)[half])
+            plane = keep.tile([P, 2 * HALF], U8, name=f"z_plane_first{half}", align_bytes=64)
+            nc.vector.quantize_mx(out=codes[:].bitcast(E4M3X4), scales=plane[:], in_=z_first[half][:])
             for a in range(LAST_PASS):
-                z_codes[a, 0] = codes[:, cols_of(a)]
-                z_planes[a, 0] = plane[:, cols_of(a)]
+                z_codes[a, half] = codes[:, cols_of(a)]
+                z_planes[a, half] = plane[:, cols_of(a)]
 
-        def quantize_z(a, half):
-            start = {(2, 0): PICKED_AT + 12 * KIB, (0, 1): YW_AT, (1, 1): YW_AT + 2 * KIB, (2, 1): YW_AT + 4 * KIB}[a, half]
-            codes = placed(f"z_codes{a}{half}", [P, HALF], U32, start)
-            plane = keep.tile([P, HALF], U8, name=f"z_plane{a}{half}", align_bytes=64)
+        def quantize_last(half):
+            a = LAST_PASS
+            codes = placed(f"z_codes_last{half}", [P, HALF], U32, PICKED_AT + KIB * (10, 8)[half])
+            plane = keep.tile([P, HALF], U8, name=f"z_plane_last{half}", align_bytes=64)
             nc.vector.quantize_mx(out=codes[:].bitcast(E4M3X4), scales=plane[:], in_=z_bf[a, half])
             z_codes[a, half] = codes[:]
             z_planes[a, half] = plane[:]
@@ -253,14 +250,6 @@ def tile_list_nack_silu_backward_kernel(tc, tab_words, tab_scales, w1, w2_words,
 
         def places(n, half):
             return pages[n][:].indirect(idx2[:, half * LIST_COLS : (half + 1) * LIST_COLS])
-
-        def weigh(n):
-            y = second_product(n, 0)
-            weighed = placed(f"weighed{n}", [P, HALF], F32, YW_AT + (1 + 3 * n) * KIB)
-            nc.vector.scalar_tensor_tensor(
-                out=weighed[:], in0=y[:], scalar=0.5, in1=weights[:, cols_of(0)], op0=ALU.mult, op1=ALU.mult
-            )
-            return weighed
 
         def weigh_and_place(n, half):
             y = second_product(n, half)
@@ -292,7 +281,7 @@ def tile_list_nack_silu_backward_kernel(tc, tab_words, tab_scales, w1, w2_words,
             round_w1(g, 1)
         for i in range(0, 4):
             scale_h(i, 0)
-        finish(0, 0)
+        finish(0, 0, nc.gpsimd, RUN)
         for i in (5, 6):
             gather_s(i)
             activations(i, 0)
@@ -300,37 +289,42 @@ def tile_list_nack_silu_backward_kernel(tc, tab_words, tab_scales, w1, w2_words,
             scale_h(i, 1)
             if i == 1:
                 quantize_w1(1)
-        finish(0, 1)
+        shift_on_gpsimd(1, 0, 0, 3)
+        finish(0, 1, nc.gpsimd, RUN)
         for g in range(K_PASSES):
             round_w1(g, 2)
+        activations(4, 1)
+        shift_on_gpsimd(1, 1, 0, 1)
         gather_s(7)
         activations(7, 0)
-        shift_on_scalar(1, 0, 0, PACK)
+        shift_on_scalar(1, 0, 3, 4)
         gather_s(8)
         activations(8, 0)
+        shift_on_gpsimd(2, 0, 0, 1)
         for i in range(4, 8):
             scale_h(i, 0)
             if i == 5:
                 quantize_w1(2)
-        finish(1, 0)
-        activations(4, 1)
-        activations(5, 1)
-        for i in (9, 10):
+        finish(1, 0, nc.gpsimd, RUN)
+        for i in range(5, 8):
+            activations(i, 1)
+        shift_on_scalar(1, 1, 1, PACK)
+        gather_s(9)
+        activations(9, 0)
+        for i in range(4, 8):
+            scale_h(i, 1)
+        finish(1, 1, nc.gpsimd, RUN)
+        shift_on_scalar(2, 0, 1, 2)
+        for i in (10, 11):
             gather_half(i, 0)
             activations(i, 0)
-        shift_on_gpsimd(2, 0, 0, 3)
-        activations(6, 1)
-        gather_s(11)
-        activations(11, 0)
-        shift_on_gpsimd(2, 0, 3, 4)
+        shift_on_scalar(2, 0, 2, 4)
         for i in range(8, 12):
             scale_h(i, 0)
-        finish(2, 0)
-        activations(7, 1)
-        shift_on_scalar(1, 1, 0, PACK)
+        finish(2, 0, nc.gpsimd, RUN)
         activations(8, 1)
-        activations(11, 1)
-        for i in (9, 10):
+        activations(9, 1)
+        for i in (10, 11):
             gather_half(i, 1)
             activations(i, 1)
         shift_on_scalar(2, 1, 0, PACK)
@@ -349,21 +343,15 @@ def tile_list_nack_silu_backward_kernel(tc, tab_words, tab_scales, w1, w2_words,
         idx2 = keep.tile([P, S // 16], U16, name="idx2")
         nc.sync.dma_start(idx2[:], offs2)
 
-        for i in range(4, 9):
+        for i in range(8, 12):
             scale_h(i, 1)
-        quantize_first()
-        quantize_z(2, 0)
-        finish(1, 1)
-        for i in range(9, 12):
-            scale_h(i, 1)
-        finish(2, 1)
-        weighed = [weigh(n) for n in range(COPY_SCATTERS)]
-        for n in range(COPY_SCATTERS):
-            nc.vector.tensor_copy(places(n, 0), weighed[n][:])
-        quantize_z(0, 1)
-        quantize_z(1, 1)
-        weigh_and_place(2, 0)
-        quantize_z(2, 1)
-        weigh_and_place(3, 0)
+        quantize_first(0)
+        quantize_last(0)
+        finish(2, 1, nc.vector, 4)
+        quantize_first(1)
+        weigh_and_place(0, 0)
+        quantize_last(1)
+        for n in range(1, N_TILES):
+            weigh_and_place(n, 0)
         for n in range(N_TILES):
             weigh_and_place(n, 1)

@@ -36,7 +36,8 @@ LAST_SLICE = SLICES - 1
 
 H_BANKS = 6
 Y_BUFS = 3
-RUN = 2
+SHARED = HALF // 2
+RUN = 4
 ODD_SPLIT = T2 // 2 + 1
 
 KIB = 1024
@@ -91,6 +92,7 @@ def tile_list_nack_silu_backward_kernel(tc, tab_words, tab_scales, w1, w2_words,
         neg_tanh = {}
         scaled_h = {}
         z_bf = {}
+        z_last = {}
         z_codes = {}
         z_planes = {}
 
@@ -123,7 +125,7 @@ def tile_list_nack_silu_backward_kernel(tc, tab_words, tab_scales, w1, w2_words,
             if a == 0:
                 w1_codes[a] = keep.tile([P, K_PASSES * PASS], U32, name="w1_codes", align_bytes=64)
             else:
-                w1_codes[a] = placed(f"w1_codes{a}", [P, K_PASSES * PASS], U32, (PICKED_AT, CODES_AT)[a - 1])
+                w1_codes[a] = placed(f"w1_codes{a}", [P, K_PASSES * PASS], U32, (PICKED_AT + 4 * KIB, CODES_AT)[a - 1])
             w1_planes[a] = keep.tile([P, K_PASSES * PASS], U8, name=f"w1_plane{a}", align_bytes=64)
             nc.vector.quantize_mx(out=w1_codes[a][:].bitcast(E4M3X4), scales=w1_planes[a][:], in_=grouped[a][:])
 
@@ -151,7 +153,7 @@ def tile_list_nack_silu_backward_kernel(tc, tab_words, tab_scales, w1, w2_words,
             0: PICKED_AT + 26 * KIB,
             2: PICKED_AT + 20 * KIB,
             3: PICKED_AT + 24 * KIB,
-            4: CODES_AT,
+            5: CODES_AT,
             6: NINTH_AT,
             11: PICKED_AT + 10 * KIB,
         }
@@ -205,21 +207,24 @@ def tile_list_nack_silu_backward_kernel(tc, tab_words, tab_scales, w1, w2_words,
 
         z_first = [placed(f"z_first{half}", [P, 2 * HALF * PACK], BF16, Z_AT + AREA * half) for half in range(HALVES)]
 
-        def finish(a, half, engine, run):
+        def finish(a, half, engine, c0=0, c1=HALF):
             if a < LAST_PASS:
                 z_bf[a, half] = z_first[half][:, a * HALF * PACK : (a + 1) * HALF * PACK]
+                z = z_bf[a, half]
             else:
-                tile = placed(f"z_last{half}", [P, HALF * PACK], BF16, Z_AT + 2 * AREA * (1 - half))
-                z_bf[a, half] = tile[:]
+                start = PICKED_AT + 24 * KIB if c0 > 0 else Z_AT + 2 * AREA * (1 - half)
+                tile = placed(f"z_last{half}_{c0}", [P, (c1 - c0) * PACK], BF16, start)
+                z = tile[:]
+                z_last.setdefault(half, []).append((c0, c1, z))
             engine.tensor_tensor(
-                out=z_bf[a, half].rearrange("p (c r t) -> p c t r", r=run, t=PACK),
-                in0=neg_tanh[a, half][:].rearrange("p t (c r) -> p c t r", r=run),
-                in1=scaled_h[a, half][:].rearrange("p t (c r) -> p c t r", r=run),
+                out=z.rearrange("p (c r t) -> p c t r", r=RUN, t=PACK),
+                in0=neg_tanh[a, half][:, :, c0:c1].rearrange("p t (c r) -> p c t r", r=RUN),
+                in1=scaled_h[a, half][:, :, c0:c1].rearrange("p t (c r) -> p c t r", r=RUN),
                 op=ALU.mult,
             )
 
         def quantize_first(half):
-            codes = placed(f"z_codes_first{half}", [P, 2 * HALF], U32, (PICKED_AT + 24 * KIB, Z_AT + 2 * AREA)[half])
+            codes = placed(f"z_codes_first{half}", [P, 2 * HALF], U32, (PICKED_AT + 10 * KIB, Z_AT + 2 * AREA)[half])
             plane = keep.tile([P, 2 * HALF], U8, name=f"z_plane_first{half}", align_bytes=64)
             nc.vector.quantize_mx(out=codes[:].bitcast(E4M3X4), scales=plane[:], in_=z_first[half][:])
             for a in range(LAST_PASS):
@@ -228,9 +233,10 @@ def tile_list_nack_silu_backward_kernel(tc, tab_words, tab_scales, w1, w2_words,
 
         def quantize_last(half):
             a = LAST_PASS
-            codes = placed(f"z_codes_last{half}", [P, HALF], U32, PICKED_AT + KIB * (10, 8)[half])
+            codes = placed(f"z_codes_last{half}", [P, HALF], U32, (Z_AT + 4 * KIB, PICKED_AT + 8 * KIB)[half])
             plane = keep.tile([P, HALF], U8, name=f"z_plane_last{half}", align_bytes=64)
-            nc.vector.quantize_mx(out=codes[:].bitcast(E4M3X4), scales=plane[:], in_=z_bf[a, half])
+            for c0, c1, z in reversed(z_last[half]):
+                nc.vector.quantize_mx(out=codes[:, c0:c1].bitcast(E4M3X4), scales=plane[:, c0:c1], in_=z)
             z_codes[a, half] = codes[:]
             z_planes[a, half] = plane[:]
 
@@ -281,31 +287,30 @@ def tile_list_nack_silu_backward_kernel(tc, tab_words, tab_scales, w1, w2_words,
             round_w1(g, 1)
         for i in range(0, 4):
             scale_h(i, 0)
-        finish(0, 0, nc.gpsimd, RUN)
+        finish(0, 0, nc.gpsimd)
         for i in (5, 6):
             gather_s(i)
             activations(i, 0)
+        shift_on_gpsimd(1, 0, 0, 2)
         for i in range(0, 4):
             scale_h(i, 1)
-            if i == 1:
+            if i == 2:
                 quantize_w1(1)
-        shift_on_gpsimd(1, 0, 0, 3)
-        finish(0, 1, nc.gpsimd, RUN)
+        finish(0, 1, nc.gpsimd)
         for g in range(K_PASSES):
             round_w1(g, 2)
         activations(4, 1)
         shift_on_gpsimd(1, 1, 0, 1)
         gather_s(7)
         activations(7, 0)
-        shift_on_scalar(1, 0, 3, 4)
+        shift_on_scalar(1, 0, 2, 4)
         gather_s(8)
         activations(8, 0)
-        shift_on_gpsimd(2, 0, 0, 1)
         for i in range(4, 8):
             scale_h(i, 0)
-            if i == 5:
+            if i == 6:
                 quantize_w1(2)
-        finish(1, 0, nc.gpsimd, RUN)
+        finish(1, 0, nc.gpsimd)
         for i in range(5, 8):
             activations(i, 1)
         shift_on_scalar(1, 1, 1, PACK)
@@ -313,15 +318,15 @@ def tile_list_nack_silu_backward_kernel(tc, tab_words, tab_scales, w1, w2_words,
         activations(9, 0)
         for i in range(4, 8):
             scale_h(i, 1)
-        finish(1, 1, nc.gpsimd, RUN)
-        shift_on_scalar(2, 0, 1, 2)
+        finish(1, 1, nc.gpsimd)
+        shift_on_scalar(2, 0, 0, 2)
         for i in (10, 11):
             gather_half(i, 0)
             activations(i, 0)
         shift_on_scalar(2, 0, 2, 4)
         for i in range(8, 12):
             scale_h(i, 0)
-        finish(2, 0, nc.gpsimd, RUN)
+        finish(2, 0, nc.gpsimd, 0, SHARED)
         activations(8, 1)
         activations(9, 1)
         for i in (10, 11):
@@ -345,9 +350,10 @@ def tile_list_nack_silu_backward_kernel(tc, tab_words, tab_scales, w1, w2_words,
 
         for i in range(8, 12):
             scale_h(i, 1)
+        finish(2, 0, nc.vector, SHARED, HALF)
         quantize_first(0)
         quantize_last(0)
-        finish(2, 1, nc.vector, 4)
+        finish(2, 1, nc.vector)
         quantize_first(1)
         weigh_and_place(0, 0)
         quantize_last(1)

@@ -21,100 +21,115 @@ PACK = 4
 PASS = P * PACK
 QUADRANTS = 4
 HALF = 512
-PAIR = 2
+GROUP = HALF // PACK
 K_PASSES = K // PASS
 H_PASSES = H // PASS
 HALVES = S // HALF
+GROUPS = S // GROUP
 N_TILES = N // P
-SLICES = H // P
-PAIRS = SLICES // PAIR
-PASS_PAIRS = PACK // PAIR
 LIST_COLS = HALF // 16
-LAST_PASS = H_PASSES - 1
-LAST_PAIR = PAIRS - 1
-LAST_SLICE = SLICES - 1
-
-H_BANKS = 6
-Y_BUFS = 3
-SHARED = HALF // 2
 RUN = 4
 ODD_SPLIT = T2 // 2 + 1
+BANKS = 8
+BANK_BYTES = 2048
+EARLY_GROUPS = 2
+LAST = H_PASSES - 1
 
 KIB = 1024
 AREA = 8 * KIB
-ROW_AREA = (0, 5, 6, 7, 8, 0, 2, 4, 5, 7, 9, 0)
-WORD_AREA = (1, 3)
-RAW_AREA = (2, 4, 9, 1, 3, 6)
-TANH_AT = 80 * KIB
-PICKED_AT = 104 * KIB
-CODES_AT = 132 * KIB
-NINTH_AT = 136 * KIB
-Z_AT = 140 * KIB
-TANH_LATE_AT = 160 * KIB
+FACTORS_AT = 0
+RING_AT = 96 * KIB
+V_AT = RING_AT + 7 * AREA
+CODES_AT = V_AT + 2 * AREA
+
+
+def ring(n):
+    return RING_AT + n * AREA
+
+
+ROW_AT = (ring(0), ring(1), V_AT, V_AT + AREA, ring(3), ring(6), ring(1), ring(2), ring(3), ring(5), ring(6), ring(0))
+WORD_AT = (ring(4), CODES_AT)
+RAW_AT = {(0, 0): ring(2), (0, 1): ring(5), (2, 0): ring(0), (2, 1): ring(4), (1, 0): ring(1), (1, 1): ring(2)}
+W1_CODES_AT = (CODES_AT, CODES_AT + 4 * KIB, ring(6))
+Z_AT = {
+    (0, 0): ring(3),
+    (0, 1): ring(3) + 4 * KIB,
+    (2, 0): ring(5) + 4 * KIB,
+    (2, 1): ring(6) + 4 * KIB,
+    (1, 0): ring(0),
+    (1, 1): ring(0) + 4 * KIB,
+}
 
 
 def tile_list_nack_silu_backward_kernel(tc, tab_words, tab_scales, w1, w2_words, w2_scales, sT, wgo, offs, offs2, out):
     nc = tc.nc
     with ExitStack() as ctx:
         keep = ctx.enter_context(tc.tile_pool(name="keep", bufs=1))
-        work = ctx.enter_context(tc.tile_pool(name="work", bufs=Y_BUFS))
         arena = ctx.enter_context(tc.tile_pool(name="arena", bufs=1))
-        h_psum = ctx.enter_context(tc.psum_pool(name="h_psum", bufs=H_BANKS))
-        y_psum = ctx.enter_context(tc.psum_pool(name="y_psum", bufs=8 - H_BANKS))
+        psum = ctx.enter_context(tc.psum_pool(name="psum", bufs=1))
+
+        def placed(name, shape, dtype, offset):
+            return arena.tile(shape, dtype, name=name, offset=offset, align_bytes=64)
+
+        banks_taken = []
+
+        def next_bank():
+            n = len(banks_taken)
+            banks_taken.append(n)
+            return psum.tile([P, HALF], F32, name=f"bank{n}", offset=BANK_BYTES * (n % BANKS))
+
+        def cols_of(half):
+            return slice(half * HALF, (half + 1) * HALF)
 
         idx = keep.tile([P, S // 16], U16, name="idx")
         nc.sync.dma_start(idx[:], offs)
 
         tab_planes = keep.tile([P, K_PASSES * T], U8, name="tab_planes", align_bytes=64)
-        v_planes = [keep.tile([P, S], U8, name=f"v_plane{g}", align_bytes=64) for g in range(K_PASSES)]
         nc.gpsimd.memset(tab_planes[:].bitcast(I32), 0)
 
         pages = [keep.tile([P, T2], F32, name=f"page{n}") for n in range(N_TILES)]
-        for page in pages[: N_TILES // 2]:
+        for page in pages[1:]:
             nc.gpsimd.memset(page[:], 0.0)
-        for page in pages[N_TILES // 2 :]:
-            nc.vector.memset(page[:, :ODD_SPLIT], 0.0)
-            nc.vector.memset(page[:, ODD_SPLIT:], 0.0)
+        nc.vector.memset(pages[0][:, :ODD_SPLIT], 0.0)
+        nc.vector.memset(pages[0][:, ODD_SPLIT:], 0.0)
 
-        v_words = [keep.tile([P, S], U32, name=f"v_words{g}", align_bytes=64) for g in range(K_PASSES)]
-        for q in range(QUADRANTS):
-            nc.sync.dma_start(
-                out=tab_planes[32 * q : 32 * q + 4, :].bitcast(I32).rearrange("r (g n) -> r g n", g=K_PASSES),
-                in_=tab_scales[:, 4 * q : 4 * q + 4, :].bitcast(I32).rearrange("g r n -> r g n"),
-            )
-
+        rows = {}
+        factors = {}
+        last = {}
         grouped = {}
         w1_codes = {}
         w1_planes = {}
-        rows = {}
-        picked = {}
-        silu_neg = {}
-        neg_tanh = {}
-        scaled_h = {}
+        v_words = {}
+        v_planes = {}
         z_bf = {}
-        z_last = {}
         z_codes = {}
         z_planes = {}
 
-        def placed(name, shape, dtype, offset):
-            return arena.tile(shape, dtype, name=name, offset=offset, align_bytes=64)
+        def load_scales():
+            for q in range(QUADRANTS):
+                nc.sync.dma_start(
+                    out=tab_planes[32 * q : 32 * q + 4, :].bitcast(I32).rearrange("r (g n) -> r g n", g=K_PASSES),
+                    in_=tab_scales[:, 4 * q : 4 * q + 4, :].bitcast(I32).rearrange("g r n -> r g n"),
+                )
 
-        def cols_of(half):
-            return slice(half * HALF, (half + 1) * HALF)
+        def gather_plane(g):
+            v_planes[g] = keep.tile([P, S], U8, name=f"v_plane{g}", align_bytes=64)
+            nc.vector.tensor_copy(v_planes[g][:], tab_planes[:, g * T : (g + 1) * T].indirect(idx[:]))
 
-        def gather_table(g):
-            words = placed(f"words{g}", [P, T], I32, AREA * WORD_AREA[g])
+        def gather_words(g):
+            words = placed(f"words{g}", [P, T], I32, WORD_AT[g])
             nc.sync.dma_start(out=words[:], in_=tab_words[g].rearrange("p t i -> p (t i)").bitcast(I32))
+            v_words[g] = placed(f"v_words{g}", [P, S], U32, V_AT + g * AREA)
             nc.vector.tensor_copy(v_words[g][:], words[:].bitcast(U32).indirect(idx[:]))
 
-        def round_w1(g, a):
-            raw = placed(f"raw{a}{g}", [P, PACK, PASS], F32, AREA * RAW_AREA[K_PASSES * a + g])
+        def round_w1(a, g):
+            raw = placed(f"raw{a}{g}", [P, PACK, PASS], F32, RAW_AT[a, g])
             nc.sync.dma_start(
                 out=raw[:],
                 in_=w1[g * PASS : (g + 1) * PASS, a * PASS : (a + 1) * PASS].rearrange("(p j) c -> p j c", j=PACK),
             )
             if g == 0:
-                grouped[a] = keep.tile([P, K_PASSES * PACK * PASS], BF16, name="grouped", tag="grouped", align_bytes=64)
+                grouped[a] = keep.tile([P, K_PASSES * PACK * PASS], BF16, name="grouped", tag="grouped", bufs=2, align_bytes=64)
             nc.scalar.activation(
                 out=grouped[a][:, g * PACK * PASS : (g + 1) * PACK * PASS].rearrange("p (t m j) -> p m j t", t=PACK, j=PACK),
                 in_=raw[:].rearrange("p j (m t) -> p m j t", t=PACK),
@@ -122,76 +137,59 @@ def tile_list_nack_silu_backward_kernel(tc, tab_words, tab_scales, w1, w2_words,
             )
 
         def quantize_w1(a):
-            if a == 0:
-                w1_codes[a] = keep.tile([P, K_PASSES * PASS], U32, name="w1_codes", align_bytes=64)
-            else:
-                w1_codes[a] = placed(f"w1_codes{a}", [P, K_PASSES * PASS], U32, (PICKED_AT + 4 * KIB, CODES_AT)[a - 1])
+            w1_codes[a] = placed(f"w1_codes{a}", [P, K_PASSES * PASS], U32, W1_CODES_AT[a])
             w1_planes[a] = keep.tile([P, K_PASSES * PASS], U8, name=f"w1_plane{a}", align_bytes=64)
             nc.vector.quantize_mx(out=w1_codes[a][:].bitcast(E4M3X4), scales=w1_planes[a][:], in_=grouped[a][:])
 
-        def load_rows(i):
+        def gather_s(i, half=None):
             a, t = divmod(i, PACK)
-            rows[i] = placed(f"rows{i}", [P, T], F32, AREA * ROW_AREA[i])
-            nc.sync.dma_start(out=rows[i][:], in_=sT[a * PASS : (a + 1) * PASS, :].rearrange("(p t) n -> p t n", t=PACK)[:, t, :])
-
-        def gather_s(i):
-            load_rows(i)
-            slot = {7: 2, 8: 3}.get(i, i)
-            whole = placed(f"picked{i}", [P, S], F32, NINTH_AT if i == 9 else PICKED_AT + 4 * KIB * slot)
-            nc.vector.tensor_copy(whole[:], rows[i][:].indirect(idx[:]))
-            for half in range(HALVES):
-                picked[i, half] = whole[:, cols_of(half)]
-
-        def gather_half(i, half):
-            if half == 0:
-                load_rows(i)
-            part = placed(f"picked{i}_{half}", [P, HALF], F32, PICKED_AT + KIB * (24 if i == 10 else 8 + 2 * half))
-            nc.vector.tensor_copy(part[:], rows[i][:].indirect(idx[:, half * LIST_COLS : (half + 1) * LIST_COLS]))
-            picked[i, half] = part[:]
-
-        silu_at = {
-            0: PICKED_AT + 26 * KIB,
-            2: PICKED_AT + 20 * KIB,
-            3: PICKED_AT + 24 * KIB,
-            5: CODES_AT,
-            6: NINTH_AT,
-            11: PICKED_AT + 10 * KIB,
-        }
-
-        def activations(i, half):
-            a, t = divmod(i, PACK)
-            if (a, half) not in neg_tanh:
-                start = TANH_LATE_AT if (a, half) == (1, 1) else TANH_AT + AREA * {(0, 0): 0, (0, 1): 1, (1, 0): 2, (2, 0): 0, (2, 1): 1}[a, half]
-                neg_tanh[a, half] = placed(f"neg_tanh{a}{half}", [P, PACK, HALF], F32, start)
-            s = picked[i, half]
-            if half == 0 and i in silu_at:
-                apart = placed(f"silu{i}", [P, HALF], F32, silu_at[i])
-                silu_neg[i, half] = apart[:]
-                nc.scalar.activation(out=apart[:], in_=s, func=ACT.Silu, scale=-1.0)
-                nc.scalar.activation(out=neg_tanh[a, half][:, t, :], in_=s, func=ACT.Tanh, scale=-0.5)
+            if i not in rows:
+                rows[i] = placed(f"rows{i}", [P, T], F32, ROW_AT[i])
+                nc.sync.dma_start(out=rows[i][:], in_=sT[a * PASS : (a + 1) * PASS, :].rearrange("(p t) n -> p t n", t=PACK)[:, t, :])
+            if a not in factors:
+                factors[a] = placed(f"factors{a}", [P, PACK, 2, S], F32, FACTORS_AT + a * 4 * AREA)
+            if half is None:
+                nc.vector.tensor_copy(factors[a][:, t, 1, :], rows[i][:].indirect(idx[:]))
             else:
-                silu_neg[i, half] = s
-                nc.scalar.activation(out=neg_tanh[a, half][:, t, :], in_=s, func=ACT.Tanh, scale=-0.5)
-                nc.scalar.activation(out=s, in_=s, func=ACT.Silu, scale=-1.0)
+                offsets = idx[:, half * LIST_COLS : (half + 1) * LIST_COLS]
+                nc.vector.tensor_copy(factors[a][:, t, 1, cols_of(half)], rows[i][:].indirect(offsets))
 
-        def shift_on_scalar(a, half, t0, t1):
-            part = neg_tanh[a, half][:, t0:t1, :]
-            nc.scalar.activation(out=part, in_=part, func=ACT.Copy, bias=-1.0)
+        def gather_last(t):
+            a = LAST
+            i = PACK * a + t
+            rows[i] = placed(f"rows{i}", [P, T], F32, ROW_AT[i])
+            nc.sync.dma_start(out=rows[i][:], in_=sT[a * PASS : (a + 1) * PASS, :].rearrange("(p t) n -> p t n", t=PACK)[:, t, :])
+            for half in range(HALVES):
+                if t == 0:
+                    last[half] = placed(f"last{half}", [P, PACK, 2, HALF], F32, FACTORS_AT + (a * 4 + half * 2) * AREA)
+                offsets = idx[:, half * LIST_COLS : (half + 1) * LIST_COLS]
+                nc.vector.tensor_copy(last[half][:, t, 1, :], rows[i][:].indirect(offsets))
+                s = last[half][:, t, 1, :]
+                nc.scalar.activation(out=last[half][:, t, 0, :], in_=s, func=ACT.Silu, scale=-1.0)
+                nc.scalar.activation(out=s, in_=s, func=ACT.Tanh, scale=-0.5)
 
-        def shift_on_gpsimd(a, half, t0, t1):
-            part = neg_tanh[a, half][:, t0:t1, :]
-            nc.gpsimd.tensor_scalar(part, part, 1.0, -1.0, ALU.mult, ALU.add)
-
-        scaled_area = {(0, 0): 8, (0, 1): 2, (1, 0): 5, (1, 1): 7, (2, 0): 1, (2, 1): 9}
-
-        def scale_h(i, half):
+        def activations(i, cols=slice(0, S)):
             a, t = divmod(i, PACK)
-            cols = cols_of(half)
-            h = h_psum.tile([P, HALF], F32, name="h")
+            s = factors[a][:, t, 1, cols]
+            nc.scalar.activation(out=factors[a][:, t, 0, cols], in_=s, func=ACT.Silu, scale=-1.0)
+            nc.scalar.activation(out=s, in_=s, func=ACT.Tanh, scale=-0.5)
+
+        def shift(part, engine):
+            if engine is nc.scalar:
+                nc.scalar.activation(out=part, in_=part, func=ACT.Copy, bias=-1.0)
+            else:
+                nc.gpsimd.tensor_scalar(part, part, 1.0, -1.0, ALU.mult, ALU.add)
+
+        def derivative(i, engine, cols=slice(0, S)):
+            a, t = divmod(i, PACK)
+            shift(factors[a][:, t, :, cols], engine)
+            nc.gpsimd.tensor_tensor(factors[a][:, t, 0, cols], factors[a][:, t, 0, cols], factors[a][:, t, 1, cols], ALU.mult)
+
+        def first_product(h, a, t, cols):
             for g in range(K_PASSES):
                 w_cols = slice(g * PASS + t * P, g * PASS + (t + 1) * P)
                 nc.tensor.matmul_mx(
-                    out=h[:],
+                    out=h,
                     lhsT=w1_codes[a][:, w_cols].bitcast(E4M3X4),
                     lhsT_scale=w1_planes[a][:, w_cols],
                     rhs=v_words[g][:, cols].bitcast(E5M2X4),
@@ -199,165 +197,147 @@ def tile_list_nack_silu_backward_kernel(tc, tab_words, tab_scales, w1, w2_words,
                     start=(g == 0),
                     stop=(g == K_PASSES - 1),
                 )
-            if t == 0:
-                scaled_h[a, half] = placed(f"scaled_h{a}{half}", [P, PACK, HALF], F32, AREA * scaled_area[a, half])
-            nc.vector.scalar_tensor_tensor(
-                out=scaled_h[a, half][:, t, :], in0=silu_neg[i, half], scalar=1.0, in1=h[:], op0=ALU.subtract, op1=ALU.mult
-            )
 
-        z_first = [placed(f"z_first{half}", [P, 2 * HALF * PACK], BF16, Z_AT + AREA * half) for half in range(HALVES)]
+        def z_tile(a, half):
+            if (a, half) not in z_bf:
+                z_bf[a, half] = placed(f"z{a}{half}", [P, HALF * PACK], BF16, Z_AT[a, half])
+            return z_bf[a, half]
 
-        def finish(a, half, engine, c0=0, c1=HALF):
-            if a < LAST_PASS:
-                z_bf[a, half] = z_first[half][:, a * HALF * PACK : (a + 1) * HALF * PACK]
-                z = z_bf[a, half]
-            else:
-                start = PICKED_AT + 24 * KIB if c0 > 0 else Z_AT + 2 * AREA * (1 - half)
-                tile = placed(f"z_last{half}_{c0}", [P, (c1 - c0) * PACK], BF16, start)
-                z = tile[:]
-                z_last.setdefault(half, []).append((c0, c1, z))
-            engine.tensor_tensor(
-                out=z.rearrange("p (c r t) -> p c t r", r=RUN, t=PACK),
-                in0=neg_tanh[a, half][:, :, c0:c1].rearrange("p t (c r) -> p c t r", r=RUN),
-                in1=scaled_h[a, half][:, :, c0:c1].rearrange("p t (c r) -> p c t r", r=RUN),
+        def interleaved(a, half, c0, c1):
+            return z_tile(a, half)[:, c0 * PACK : c1 * PACK].rearrange("p (c r t) -> p c t r", r=RUN, t=PACK)
+
+        def in_runs(part):
+            return part.rearrange("p t (c r) -> p c t r", r=RUN)
+
+        def z_group(a, group):
+            cols = slice(group * GROUP, (group + 1) * GROUP)
+            half, c0 = divmod(group * GROUP, HALF)
+            h = next_bank()
+            for t in range(PACK):
+                first_product(h[:, t * GROUP : (t + 1) * GROUP], a, t, cols)
+            nc.vector.tensor_tensor(
+                out=interleaved(a, half, c0, c0 + GROUP),
+                in0=in_runs(h[:].rearrange("p (t c) -> p t c", t=PACK)),
+                in1=in_runs(factors[a][:, :, 0, cols]),
                 op=ALU.mult,
             )
 
-        def quantize_first(half):
-            codes = placed(f"z_codes_first{half}", [P, 2 * HALF], U32, (PICKED_AT + 10 * KIB, Z_AT + 2 * AREA)[half])
-            plane = keep.tile([P, 2 * HALF], U8, name=f"z_plane_first{half}", align_bytes=64)
-            nc.vector.quantize_mx(out=codes[:].bitcast(E4M3X4), scales=plane[:], in_=z_first[half][:])
-            for a in range(LAST_PASS):
-                z_codes[a, half] = codes[:, cols_of(a)]
-                z_planes[a, half] = plane[:, cols_of(a)]
+        def scale_h(i, half):
+            a, t = divmod(i, PACK)
+            h = next_bank()
+            first_product(h[:], a, t, cols_of(half))
+            part = last[half][:, t, 0, :]
+            nc.vector.scalar_tensor_tensor(out=part, in0=part, scalar=1.0, in1=h[:], op0=ALU.subtract, op1=ALU.mult)
 
-        def quantize_last(half):
-            a = LAST_PASS
-            codes = placed(f"z_codes_last{half}", [P, HALF], U32, (Z_AT + 4 * KIB, PICKED_AT + 8 * KIB)[half])
-            plane = keep.tile([P, HALF], U8, name=f"z_plane_last{half}", align_bytes=64)
-            for c0, c1, z in reversed(z_last[half]):
-                nc.vector.quantize_mx(out=codes[:, c0:c1].bitcast(E4M3X4), scales=plane[:, c0:c1], in_=z)
-            z_codes[a, half] = codes[:]
-            z_planes[a, half] = plane[:]
+        def finish(a, group, count):
+            half, c0 = divmod(group * GROUP, HALF)
+            nc.gpsimd.tensor_tensor(
+                out=interleaved(a, half, c0, c0 + count * GROUP),
+                in0=in_runs(last[half][:, :, 1, c0 : c0 + count * GROUP]),
+                in1=in_runs(last[half][:, :, 0, c0 : c0 + count * GROUP]),
+                op=ALU.mult,
+            )
 
-        def second_product(n, half):
-            y = y_psum.tile([P, HALF], F32, name="y")
-            for a in range(H_PASSES):
+        def quantize_z(a, half):
+            codes = placed(f"z_codes{a}{half}", [P, HALF], U32, FACTORS_AT + 4 * AREA + 2 * KIB * (HALVES * a + half))
+            plane = keep.tile([P, HALF], U8, name=f"z_plane{a}{half}", align_bytes=64)
+            nc.vector.quantize_mx(out=codes[:].bitcast(E4M3X4), scales=plane[:], in_=z_bf[a, half][:])
+            z_codes[a, half] = codes
+            z_planes[a, half] = plane
+
+        z_order = ((0, 2, 1), (0, 1, 2))
+
+        def weigh_and_place(n, half):
+            y = next_bank()
+            for k, a in enumerate(z_order[half]):
                 nc.tensor.matmul_mx(
                     out=y[:],
                     lhsT=w2_codes[:, a, n * P : (n + 1) * P].bitcast(E4M3X4),
                     lhsT_scale=w2_planes[:, a * N + n * P : a * N + (n + 1) * P],
-                    rhs=z_codes[a, half].bitcast(E4M3X4),
-                    rhs_scale=z_planes[a, half],
-                    start=(a == 0),
-                    stop=(a == LAST_PASS),
+                    rhs=z_codes[a, half][:].bitcast(E4M3X4),
+                    rhs_scale=z_planes[a, half][:],
+                    start=(k == 0),
+                    stop=(k == H_PASSES - 1),
                 )
-            return y
-
-        def places(n, half):
-            return pages[n][:].indirect(idx2[:, half * LIST_COLS : (half + 1) * LIST_COLS])
-
-        def weigh_and_place(n, half):
-            y = second_product(n, half)
-            y_sb = work.tile([P, HALF], F32, name="y_sb", align_bytes=64)
+            y_sb = placed(f"y_sb{n}{half}", [P, HALF], F32, FACTORS_AT + 2 * KIB * (N_TILES * half + n))
             nc.scalar.activation(out=y_sb[:], in_=y[:], func=ACT.Copy, scale=0.5)
-            nc.vector.tensor_tensor(places(n, half), y_sb[:], weights[:, cols_of(half)], ALU.mult)
+            places = pages[n][:].indirect(idx2[:, half * LIST_COLS : (half + 1) * LIST_COLS])
+            nc.vector.tensor_tensor(places, y_sb[:], weights[:, cols_of(half)], ALU.mult)
             if half == HALVES - 1:
                 nc.sync.dma_start(out=out[n * P : (n + 1) * P, :], in_=pages[n][:])
 
-        gather_s(0)
-        for half in range(HALVES):
-            activations(0, half)
-        for g in range(K_PASSES):
-            nc.vector.tensor_copy(v_planes[g][:], tab_planes[:, g * T : (g + 1) * T].indirect(idx[:]))
-        for g in range(K_PASSES):
-            round_w1(g, 0)
-            if g == K_PASSES - 1:
-                quantize_w1(0)
-            gather_table(g)
-        for i in range(1, PACK):
+        def slice_ahead(i, engine=nc.gpsimd):
             gather_s(i)
-            for half in range(HALVES):
-                activations(i, half)
-                if i % 2 == 1:
-                    shift_on_gpsimd(0, half, i - 1, i + 1)
-        gather_s(4)
-        activations(4, 0)
-        for g in range(K_PASSES):
-            round_w1(g, 1)
-        for i in range(0, 4):
-            scale_h(i, 0)
-        finish(0, 0, nc.gpsimd)
-        for i in (5, 6):
-            gather_s(i)
-            activations(i, 0)
-        shift_on_gpsimd(1, 0, 0, 2)
-        for i in range(0, 4):
-            scale_h(i, 1)
-            if i == 2:
-                quantize_w1(1)
-        finish(0, 1, nc.gpsimd)
-        for g in range(K_PASSES):
-            round_w1(g, 2)
-        activations(4, 1)
-        shift_on_gpsimd(1, 1, 0, 1)
-        gather_s(7)
-        activations(7, 0)
-        shift_on_scalar(1, 0, 2, 4)
-        gather_s(8)
-        activations(8, 0)
-        for i in range(4, 8):
-            scale_h(i, 0)
-            if i == 6:
-                quantize_w1(2)
-        finish(1, 0, nc.gpsimd)
-        for i in range(5, 8):
-            activations(i, 1)
-        shift_on_scalar(1, 1, 1, PACK)
-        gather_s(9)
-        activations(9, 0)
-        for i in range(4, 8):
-            scale_h(i, 1)
-        finish(1, 1, nc.gpsimd)
-        shift_on_scalar(2, 0, 0, 2)
-        for i in (10, 11):
-            gather_half(i, 0)
-            activations(i, 0)
-        shift_on_scalar(2, 0, 2, 4)
-        for i in range(8, 12):
-            scale_h(i, 0)
-        finish(2, 0, nc.gpsimd, 0, SHARED)
-        activations(8, 1)
-        activations(9, 1)
-        for i in (10, 11):
-            gather_half(i, 1)
-            activations(i, 1)
-        shift_on_scalar(2, 1, 0, PACK)
+            activations(i)
+            derivative(i, engine)
 
-        w2_codes = placed("w2_codes", [P, H_PASSES, N], I32, AREA * ROW_AREA[6])
+        for half in range(HALVES):
+            gather_s(0, half)
+            activations(0, cols_of(half))
+            derivative(0, (nc.gpsimd, nc.scalar)[half], cols_of(half))
+        slice_ahead(1)
+        gather_s(2)
+        activations(2)
+        load_scales()
+        for g in range(K_PASSES):
+            gather_plane(g)
+        round_w1(0, 0)
+        derivative(2, nc.scalar)
+        slice_ahead(3)
+        slice_ahead(4)
+        gather_words(0)
+        round_w1(0, 1)
+        gather_s(5)
+        activations(5)
+        gather_words(1)
+        quantize_w1(0)
+        round_w1(2, 0)
+        for half in range(HALVES):
+            derivative(5, (nc.gpsimd, nc.scalar)[half], cols_of(half))
+        slice_ahead(6)
+        slice_ahead(7)
+        gather_last(0)
+        for group in range(EARLY_GROUPS):
+            z_group(0, group)
+        round_w1(2, 1)
+        gather_last(1)
+        gather_last(2)
+        quantize_w1(2)
+        shift(last[0][:, : PACK - 1, 1, :], nc.gpsimd)
+        gather_last(3)
+        shift(last[0][:, PACK - 1, 1, :], nc.gpsimd)
+        for g in range(K_PASSES):
+            round_w1(1, g)
+        shift(last[1][:, :, 1, :], nc.scalar)
+
+        w2_codes = placed("w2_codes", [P, H_PASSES, N], I32, ring(4))
         nc.sync.dma_start(out=w2_codes[:], in_=w2_words.rearrange("a p c i -> p a (c i)").bitcast(I32))
-        w2_planes = placed("w2_planes", [P, H_PASSES * N], U8, AREA * ROW_AREA[6] + 4 * H_PASSES * N)
+        w2_planes = placed("w2_planes", [P, H_PASSES * N], U8, ring(4) + 4 * H_PASSES * N)
         nc.gpsimd.memset(w2_planes[:].bitcast(I32), 0)
         for q in range(QUADRANTS):
             nc.sync.dma_start(
                 out=w2_planes[32 * q : 32 * q + 4, :].bitcast(I32).rearrange("r (a n) -> r a n", a=H_PASSES),
                 in_=w2_scales[:, 4 * q : 4 * q + 4, :].bitcast(I32).rearrange("a r n -> r a n"),
             )
-        weights = placed("weights", [P, S], F32, AREA * ROW_AREA[7])
+        weights = placed("weights", [P, S], F32, ring(5))
         nc.sync.dma_start(out=weights[:], in_=wgo)
         idx2 = keep.tile([P, S // 16], U16, name="idx2")
         nc.sync.dma_start(idx2[:], offs2)
 
-        for i in range(8, 12):
-            scale_h(i, 1)
-        finish(2, 0, nc.vector, SHARED, HALF)
-        quantize_first(0)
-        quantize_last(0)
-        finish(2, 1, nc.vector)
-        quantize_first(1)
-        weigh_and_place(0, 0)
-        quantize_last(1)
-        for n in range(1, N_TILES):
-            weigh_and_place(n, 0)
-        for n in range(N_TILES):
-            weigh_and_place(n, 1)
+        for half in range(HALVES):
+            for i in range(8, 12):
+                scale_h(i, half)
+            for group in range(PACK * half, PACK * (half + 1), 2):
+                finish(2, group, 2)
+        for group in range(EARLY_GROUPS, GROUPS):
+            if group == GROUPS - 2:
+                quantize_w1(1)
+            z_group(0, group)
+        for group in range(GROUPS):
+            z_group(1, group)
+        for half in range(HALVES):
+            for a in z_order[half]:
+                quantize_z(a, half)
+        for half in range(HALVES):
+            for n in range(N_TILES):
+                weigh_and_place(n, half)

@@ -33,6 +33,7 @@ ODD_SPLIT = T2 // 2 + 1
 BANKS = 8
 BANK_BYTES = 2048
 EARLY_GROUPS = 2
+TURN = 3
 LAST = H_PASSES - 1
 
 KIB = 1024
@@ -40,7 +41,11 @@ AREA = 8 * KIB
 FACTORS_AT = 0
 RING_AT = 96 * KIB
 V_AT = RING_AT + 7 * AREA
-CODES_AT = V_AT + 2 * AREA
+PLANES_AT = V_AT + 2 * AREA
+GROUPED_AT = PLANES_AT + 4 * KIB
+CODES_AT = GROUPED_AT + 2 * AREA
+MID_AT = FACTORS_AT + 4 * AREA
+DERIV_AT = PLANES_AT - 4 * KIB
 
 
 def ring(n):
@@ -50,14 +55,16 @@ def ring(n):
 ROW_AT = (ring(0), ring(1), V_AT, V_AT + AREA, ring(3), ring(6), ring(1), ring(2), ring(3), ring(5), ring(6), ring(0))
 WORD_AT = (ring(4), CODES_AT)
 RAW_AT = {(0, 0): ring(2), (0, 1): ring(5), (2, 0): ring(0), (2, 1): ring(4), (1, 0): ring(1), (1, 1): ring(2)}
+GROUPED = (GROUPED_AT, MID_AT, GROUPED_AT + AREA)
 W1_CODES_AT = (CODES_AT, CODES_AT + 4 * KIB, ring(6))
 Z_AT = {
     (0, 0): ring(3),
-    (0, 1): ring(3) + 4 * KIB,
-    (2, 0): ring(5) + 4 * KIB,
-    (2, 1): ring(6) + 4 * KIB,
-    (1, 0): ring(0),
-    (1, 1): ring(0) + 4 * KIB,
+    (0, 2): ring(0),
+    (0, 4): ring(0) + 2 * KIB,
+    (2, 0): ring(4),
+    (2, 4): ring(4) + 4 * KIB,
+    (1, 0): ring(3) + 4 * KIB,
+    (1, 4): V_AT + 4 * KIB,
 }
 
 
@@ -73,10 +80,9 @@ def tile_list_nack_silu_backward_kernel(tc, tab_words, tab_scales, w1, w2_words,
 
         banks_taken = []
 
-        def next_bank():
-            n = len(banks_taken)
-            banks_taken.append(n)
-            return psum.tile([P, HALF], F32, name=f"bank{n}", offset=BANK_BYTES * (n % BANKS))
+        def take_bank(bank):
+            banks_taken.append(bank)
+            return psum.tile([P, HALF], F32, name=f"bank{len(banks_taken)}", offset=BANK_BYTES * bank)
 
         def cols_of(half):
             return slice(half * HALF, (half + 1) * HALF)
@@ -84,7 +90,7 @@ def tile_list_nack_silu_backward_kernel(tc, tab_words, tab_scales, w1, w2_words,
         idx = keep.tile([P, S // 16], U16, name="idx")
         nc.sync.dma_start(idx[:], offs)
 
-        tab_planes = keep.tile([P, K_PASSES * T], U8, name="tab_planes", align_bytes=64)
+        tab_planes = placed("tab_planes", [P, K_PASSES * T], U8, PLANES_AT)
         nc.gpsimd.memset(tab_planes[:].bitcast(I32), 0)
 
         pages = [keep.tile([P, T2], F32, name=f"page{n}") for n in range(N_TILES)]
@@ -96,6 +102,8 @@ def tile_list_nack_silu_backward_kernel(tc, tab_words, tab_scales, w1, w2_words,
         rows = {}
         factors = {}
         last = {}
+        neg_tanh = {}
+        derivs = {}
         grouped = {}
         w1_codes = {}
         w1_planes = {}
@@ -129,7 +137,7 @@ def tile_list_nack_silu_backward_kernel(tc, tab_words, tab_scales, w1, w2_words,
                 in_=w1[g * PASS : (g + 1) * PASS, a * PASS : (a + 1) * PASS].rearrange("(p j) c -> p j c", j=PACK),
             )
             if g == 0:
-                grouped[a] = keep.tile([P, K_PASSES * PACK * PASS], BF16, name="grouped", tag="grouped", bufs=2, align_bytes=64)
+                grouped[a] = placed(f"grouped{a}", [P, K_PASSES * PACK * PASS], BF16, GROUPED[a])
             nc.scalar.activation(
                 out=grouped[a][:, g * PACK * PASS : (g + 1) * PACK * PASS].rearrange("p (t m j) -> p m j t", t=PACK, j=PACK),
                 in_=raw[:].rearrange("p j (m t) -> p m j t", t=PACK),
@@ -154,19 +162,22 @@ def tile_list_nack_silu_backward_kernel(tc, tab_words, tab_scales, w1, w2_words,
                 offsets = idx[:, half * LIST_COLS : (half + 1) * LIST_COLS]
                 nc.vector.tensor_copy(factors[a][:, t, 1, cols_of(half)], rows[i][:].indirect(offsets))
 
-        def gather_last(t):
+        def gather_last(t, half):
             a = LAST
             i = PACK * a + t
-            rows[i] = placed(f"rows{i}", [P, T], F32, ROW_AT[i])
-            nc.sync.dma_start(out=rows[i][:], in_=sT[a * PASS : (a + 1) * PASS, :].rearrange("(p t) n -> p t n", t=PACK)[:, t, :])
-            for half in range(HALVES):
-                if t == 0:
-                    last[half] = placed(f"last{half}", [P, PACK, 2, HALF], F32, FACTORS_AT + (a * 4 + half * 2) * AREA)
-                offsets = idx[:, half * LIST_COLS : (half + 1) * LIST_COLS]
-                nc.vector.tensor_copy(last[half][:, t, 1, :], rows[i][:].indirect(offsets))
-                s = last[half][:, t, 1, :]
-                nc.scalar.activation(out=last[half][:, t, 0, :], in_=s, func=ACT.Silu, scale=-1.0)
-                nc.scalar.activation(out=s, in_=s, func=ACT.Tanh, scale=-0.5)
+            if half == 0:
+                rows[i] = placed(f"rows{i}", [P, T], F32, ROW_AT[i])
+                nc.sync.dma_start(out=rows[i][:], in_=sT[a * PASS : (a + 1) * PASS, :].rearrange("(p t) n -> p t n", t=PACK)[:, t, :])
+            if t == 0:
+                last[half] = placed(f"last{half}", [P, PACK, 2, HALF], F32, FACTORS_AT + (a * 4 + half * 2) * AREA)
+            offsets = idx[:, half * LIST_COLS : (half + 1) * LIST_COLS]
+            s = last[half][:, t, 1, :]
+            neg_tanh[t, half] = s
+            if (t, half) == (PACK - 1, HALVES - 1):
+                neg_tanh[t, half] = placed("neg_tanh", [P, HALF], F32, Z_AT[LAST, 0])[:]
+            nc.vector.tensor_copy(s, rows[i][:].indirect(offsets))
+            nc.scalar.activation(out=last[half][:, t, 0, :], in_=s, func=ACT.Silu, scale=-1.0)
+            nc.scalar.activation(out=neg_tanh[t, half], in_=s, func=ACT.Tanh, scale=-0.5)
 
         def activations(i, cols=slice(0, S)):
             a, t = divmod(i, PACK)
@@ -180,10 +191,16 @@ def tile_list_nack_silu_backward_kernel(tc, tab_words, tab_scales, w1, w2_words,
             else:
                 nc.gpsimd.tensor_scalar(part, part, 1.0, -1.0, ALU.mult, ALU.add)
 
+        def product(i, cols=slice(0, S)):
+            a, t = divmod(i, PACK)
+            if a not in derivs:
+                derivs[a] = factors[a][:, :, 0, :] if a == 0 else placed("derivs", [P, PACK, S], F32, DERIV_AT)[:]
+            nc.gpsimd.tensor_tensor(derivs[a][:, t, cols], factors[a][:, t, 0, cols], factors[a][:, t, 1, cols], ALU.mult)
+
         def derivative(i, engine, cols=slice(0, S)):
             a, t = divmod(i, PACK)
             shift(factors[a][:, t, :, cols], engine)
-            nc.gpsimd.tensor_tensor(factors[a][:, t, 0, cols], factors[a][:, t, 0, cols], factors[a][:, t, 1, cols], ALU.mult)
+            product(i, cols)
 
         def first_product(h, a, t, cols):
             for g in range(K_PASSES):
@@ -198,57 +215,55 @@ def tile_list_nack_silu_backward_kernel(tc, tab_words, tab_scales, w1, w2_words,
                     stop=(g == K_PASSES - 1),
                 )
 
-        def z_tile(a, half):
-            if (a, half) not in z_bf:
-                z_bf[a, half] = placed(f"z{a}{half}", [P, HALF * PACK], BF16, Z_AT[a, half])
-            return z_bf[a, half]
-
-        def interleaved(a, half, c0, c1):
-            return z_tile(a, half)[:, c0 * PACK : c1 * PACK].rearrange("p (c r t) -> p c t r", r=RUN, t=PACK)
+        def interleaved(a, group, count):
+            first = max(g for b, g in Z_AT if b == a and g <= group)
+            if (a, first) not in z_bf:
+                end = min([g for b, g in Z_AT if b == a and g > first] + [GROUPS])
+                z_bf[a, first] = placed(f"z{a}{first}", [P, (end - first) * HALF], BF16, Z_AT[a, first])
+            part = z_bf[a, first][:, (group - first) * HALF : (group - first + count) * HALF]
+            return part.rearrange("p (c r t) -> p c t r", r=RUN, t=PACK)
 
         def in_runs(part):
             return part.rearrange("p t (c r) -> p c t r", r=RUN)
 
-        def z_group(a, group):
+        def z_group(a, group, bank):
             cols = slice(group * GROUP, (group + 1) * GROUP)
-            half, c0 = divmod(group * GROUP, HALF)
-            h = next_bank()
+            h = take_bank(bank)
             for t in range(PACK):
                 first_product(h[:, t * GROUP : (t + 1) * GROUP], a, t, cols)
             nc.vector.tensor_tensor(
-                out=interleaved(a, half, c0, c0 + GROUP),
+                out=interleaved(a, group, 1),
                 in0=in_runs(h[:].rearrange("p (t c) -> p t c", t=PACK)),
-                in1=in_runs(factors[a][:, :, 0, cols]),
+                in1=in_runs(derivs[a][:, :, cols]),
                 op=ALU.mult,
             )
 
         def scale_h(i, half):
             a, t = divmod(i, PACK)
-            h = next_bank()
+            h = take_bank(PACK + t)
             first_product(h[:], a, t, cols_of(half))
             part = last[half][:, t, 0, :]
             nc.vector.scalar_tensor_tensor(out=part, in0=part, scalar=1.0, in1=h[:], op0=ALU.subtract, op1=ALU.mult)
 
-        def finish(a, group, count):
-            half, c0 = divmod(group * GROUP, HALF)
-            nc.gpsimd.tensor_tensor(
-                out=interleaved(a, half, c0, c0 + count * GROUP),
-                in0=in_runs(last[half][:, :, 1, c0 : c0 + count * GROUP]),
-                in1=in_runs(last[half][:, :, 0, c0 : c0 + count * GROUP]),
-                op=ALU.mult,
-            )
+        def finish(half, shifted, z):
+            nc.gpsimd.tensor_tensor(z, last[half][:, :, 0, :], shifted, ALU.mult)
+            nc.scalar.activation(out=interleaved(LAST, PACK * half, PACK), in_=in_runs(z), func=ACT.Copy)
 
         def quantize_z(a, half):
-            codes = placed(f"z_codes{a}{half}", [P, HALF], U32, FACTORS_AT + 4 * AREA + 2 * KIB * (HALVES * a + half))
+            codes = placed(f"z_codes{a}{half}", [P, HALF], U32, DERIV_AT + 2 * KIB * (HALVES * a + half))
             plane = keep.tile([P, HALF], U8, name=f"z_plane{a}{half}", align_bytes=64)
-            nc.vector.quantize_mx(out=codes[:].bitcast(E4M3X4), scales=plane[:], in_=z_bf[a, half][:])
+            for (b, first), z in z_bf.items():
+                if b == a and first // PACK == half:
+                    c0 = first % PACK * GROUP
+                    cols = slice(c0, c0 + z.shape[1] // PACK)
+                    nc.vector.quantize_mx(out=codes[:, cols].bitcast(E4M3X4), scales=plane[:, cols], in_=z[:])
             z_codes[a, half] = codes
             z_planes[a, half] = plane
 
         z_order = ((0, 2, 1), (0, 1, 2))
 
         def weigh_and_place(n, half):
-            y = next_bank()
+            y = take_bank(PACK)
             for k, a in enumerate(z_order[half]):
                 nc.tensor.matmul_mx(
                     out=y[:],
@@ -284,57 +299,70 @@ def tile_list_nack_silu_backward_kernel(tc, tab_words, tab_scales, w1, w2_words,
         round_w1(0, 0)
         derivative(2, nc.scalar)
         slice_ahead(3)
-        slice_ahead(4)
+        gather_s(4)
+        activations(4)
+        shift(factors[1][:, 0, :, :], nc.gpsimd)
         gather_words(0)
         round_w1(0, 1)
         gather_s(5)
         activations(5)
         gather_words(1)
         quantize_w1(0)
+        product(4)
         round_w1(2, 0)
         for half in range(HALVES):
             derivative(5, (nc.gpsimd, nc.scalar)[half], cols_of(half))
         slice_ahead(6)
-        slice_ahead(7)
-        gather_last(0)
+        gather_s(7)
+        activations(7)
+        for kind in range(2):
+            shift(factors[1][:, 3, kind, :], nc.gpsimd)
+        product(7)
+        for half in range(HALVES):
+            gather_last(0, half)
         for group in range(EARLY_GROUPS):
-            z_group(0, group)
+            z_group(0, group, BANKS - EARLY_GROUPS + group)
         round_w1(2, 1)
-        gather_last(1)
-        gather_last(2)
+        for t in (1, 2):
+            for half in range(HALVES):
+                gather_last(t, half)
         quantize_w1(2)
-        shift(last[0][:, : PACK - 1, 1, :], nc.gpsimd)
-        gather_last(3)
-        shift(last[0][:, PACK - 1, 1, :], nc.gpsimd)
+        shift(last[0][:, :3, 1, :], nc.gpsimd)
+        for half in range(HALVES):
+            gather_last(3, half)
+        shift(last[0][:, 3, 1, :], nc.gpsimd)
         for g in range(K_PASSES):
             round_w1(1, g)
-        shift(last[1][:, :, 1, :], nc.scalar)
+        shifted = placed("shifted", [P, PACK, HALF], F32, RAW_AT[1, 1])
+        nc.scalar.activation(out=shifted[:, :3, :], in_=last[1][:, :3, 1, :], func=ACT.Copy, bias=-1.0)
+        nc.scalar.activation(out=shifted[:, 3, :], in_=neg_tanh[3, 1], func=ACT.Copy, bias=-1.0)
 
-        w2_codes = placed("w2_codes", [P, H_PASSES, N], I32, ring(4))
+        w2_codes = placed("w2_codes", [P, H_PASSES, N], I32, ring(5))
         nc.sync.dma_start(out=w2_codes[:], in_=w2_words.rearrange("a p c i -> p a (c i)").bitcast(I32))
-        w2_planes = placed("w2_planes", [P, H_PASSES * N], U8, ring(4) + 4 * H_PASSES * N)
+        w2_planes = placed("w2_planes", [P, H_PASSES * N], U8, ring(5) + 4 * H_PASSES * N)
         nc.gpsimd.memset(w2_planes[:].bitcast(I32), 0)
         for q in range(QUADRANTS):
             nc.sync.dma_start(
                 out=w2_planes[32 * q : 32 * q + 4, :].bitcast(I32).rearrange("r (a n) -> r a n", a=H_PASSES),
                 in_=w2_scales[:, 4 * q : 4 * q + 4, :].bitcast(I32).rearrange("a r n -> r a n"),
             )
-        weights = placed("weights", [P, S], F32, ring(5))
+        weights = placed("weights", [P, S], F32, ring(6) + 4 * KIB)
         nc.sync.dma_start(out=weights[:], in_=wgo)
         idx2 = keep.tile([P, S // 16], U16, name="idx2")
         nc.sync.dma_start(idx2[:], offs2)
 
-        for half in range(HALVES):
-            for i in range(8, 12):
-                scale_h(i, half)
-            for group in range(PACK * half, PACK * (half + 1), 2):
-                finish(2, group, 2)
+        for i in range(8, 12):
+            scale_h(i, 0)
+        finish(0, last[0][:, :, 1, :], last[0][:, :, 0, :])
+        for i in range(8, 12):
+            scale_h(i, 1)
         for group in range(EARLY_GROUPS, GROUPS):
             if group == GROUPS - 2:
                 quantize_w1(1)
-            z_group(0, group)
+                finish(1, shifted[:], placed("z_last", [P, PACK, HALF], F32, GROUPED[1])[:])
+            z_group(0, group, (group - EARLY_GROUPS) % PACK)
         for group in range(GROUPS):
-            z_group(1, group)
+            z_group(1, group, (4, 5, 6, 7, 2, 3, 0, 1)[group])
         for half in range(HALVES):
             for a in z_order[half]:
                 quantize_z(a, half)

@@ -32,8 +32,6 @@ RUN = 4
 ODD_SPLIT = T2 // 2 + 1
 BANKS = 8
 BANK_BYTES = 2048
-EARLY_GROUPS = 2
-TURN = 3
 LAST = H_PASSES - 1
 
 KIB = 1024
@@ -52,18 +50,18 @@ def ring(n):
     return RING_AT + n * AREA
 
 
-ROW_AT = (ring(0), ring(1), V_AT, V_AT + AREA, ring(3), ring(6), ring(1), ring(2), ring(3), ring(5), ring(6), ring(0))
+ROW_AT = (ring(0), ring(1), V_AT, V_AT + AREA, ring(3), ring(6), ring(0), ring(1), ring(2), ring(4), ring(5), ring(0))
 WORD_AT = (ring(4), CODES_AT)
-RAW_AT = {(0, 0): ring(2), (0, 1): ring(5), (2, 0): ring(0), (2, 1): ring(4), (1, 0): ring(1), (1, 1): ring(2)}
-GROUPED = (GROUPED_AT, MID_AT, GROUPED_AT + AREA)
-W1_CODES_AT = (CODES_AT, CODES_AT + 4 * KIB, ring(6))
+RAW_AT = {(2, 0): ring(2), (2, 1): ring(5), (0, 0): ring(3), (0, 1): ring(6), (1, 0): ring(1), (1, 1): ring(2)}
+GROUPED = (GROUPED_AT + AREA, MID_AT, GROUPED_AT)
+W1_CODES_AT = (ring(0) + 4 * KIB, ring(3), CODES_AT)
+SCALED_AT = {(0, 0): ring(5), (0, 1): ring(5) + 4 * KIB, (1, 0): ring(0), (1, 1): CODES_AT + 4 * KIB}
 Z_AT = {
-    (0, 0): ring(3),
-    (0, 2): ring(0),
-    (0, 4): ring(0) + 2 * KIB,
-    (2, 0): ring(4),
-    (2, 4): ring(4) + 4 * KIB,
-    (1, 0): ring(3) + 4 * KIB,
+    (0, 0): ring(3) + 4 * KIB,
+    (0, 4): ring(6),
+    (2, 0): MID_AT + AREA,
+    (2, 4): ring(1) + 4 * KIB,
+    (1, 0): ring(6) + 4 * KIB,
     (1, 4): V_AT + 4 * KIB,
 }
 
@@ -104,6 +102,7 @@ def tile_list_nack_silu_backward_kernel(tc, tab_words, tab_scales, w1, w2_words,
         last = {}
         neg_tanh = {}
         derivs = {}
+        scaled = {}
         grouped = {}
         w1_codes = {}
         w1_planes = {}
@@ -238,16 +237,21 @@ def tile_list_nack_silu_backward_kernel(tc, tab_words, tab_scales, w1, w2_words,
                 op=ALU.mult,
             )
 
-        def scale_h(i, half):
-            a, t = divmod(i, PACK)
-            h = take_bank(PACK + t)
-            first_product(h[:], a, t, cols_of(half))
-            part = last[half][:, t, 0, :]
-            nc.vector.scalar_tensor_tensor(out=part, in0=part, scalar=1.0, in1=h[:], op0=ALU.subtract, op1=ALU.mult)
+        def scale_h(t, half, bank):
+            h = take_bank(bank)
+            first_product(h[:], LAST, t, cols_of(half))
+            pair, u = divmod(t, 2)
+            if u == 0:
+                scaled[pair, half] = placed(f"scaled{pair}{half}", [P, 2, HALF], F32, SCALED_AT[pair, half])
+            nc.vector.scalar_tensor_tensor(
+                out=scaled[pair, half][:, u, :], in0=last[half][:, t, 0, :], scalar=1.0, in1=h[:], op0=ALU.subtract, op1=ALU.mult
+            )
 
-        def finish(half, shifted, z):
-            nc.gpsimd.tensor_tensor(z, last[half][:, :, 0, :], shifted, ALU.mult)
-            nc.scalar.activation(out=interleaved(LAST, PACK * half, PACK), in_=in_runs(z), func=ACT.Copy)
+        def finish(half, shifted, at):
+            z = placed(f"z_float{half}", [P, PACK, HALF], F32, at)
+            for pair in range(2):
+                nc.gpsimd.tensor_tensor(z[:, 2 * pair : 2 * pair + 2, :], scaled[pair, half][:], shifted[:, 2 * pair : 2 * pair + 2, :], ALU.mult)
+            nc.scalar.activation(out=interleaved(LAST, PACK * half, PACK), in_=in_runs(z[:]), func=ACT.Copy)
 
         def quantize_z(a, half):
             codes = placed(f"z_codes{a}{half}", [P, HALF], U32, DERIV_AT + 2 * KIB * (HALVES * a + half))
@@ -296,37 +300,35 @@ def tile_list_nack_silu_backward_kernel(tc, tab_words, tab_scales, w1, w2_words,
         load_scales()
         for g in range(K_PASSES):
             gather_plane(g)
-        round_w1(0, 0)
+        round_w1(LAST, 0)
         derivative(2, nc.scalar)
         slice_ahead(3)
         gather_s(4)
         activations(4)
         shift(factors[1][:, 0, :, :], nc.gpsimd)
         gather_words(0)
-        round_w1(0, 1)
+        round_w1(LAST, 1)
         gather_s(5)
         activations(5)
         gather_words(1)
-        quantize_w1(0)
+        quantize_w1(LAST)
         product(4)
-        round_w1(2, 0)
         for half in range(HALVES):
             derivative(5, (nc.gpsimd, nc.scalar)[half], cols_of(half))
         slice_ahead(6)
         gather_s(7)
         activations(7)
-        for kind in range(2):
-            shift(factors[1][:, 3, kind, :], nc.gpsimd)
-        product(7)
+        derivative(7, nc.gpsimd)
         for half in range(HALVES):
             gather_last(0, half)
-        for group in range(EARLY_GROUPS):
-            z_group(0, group, BANKS - EARLY_GROUPS + group)
-        round_w1(2, 1)
+        round_w1(0, 0)
         for t in (1, 2):
             for half in range(HALVES):
                 gather_last(t, half)
-        quantize_w1(2)
+        for half in range(HALVES):
+            for t in range(2):
+                scale_h(t, half, 2 * half + t)
+        round_w1(0, 1)
         shift(last[0][:, :3, 1, :], nc.gpsimd)
         for half in range(HALVES):
             gather_last(3, half)
@@ -337,32 +339,33 @@ def tile_list_nack_silu_backward_kernel(tc, tab_words, tab_scales, w1, w2_words,
         nc.scalar.activation(out=shifted[:, :3, :], in_=last[1][:, :3, 1, :], func=ACT.Copy, bias=-1.0)
         nc.scalar.activation(out=shifted[:, 3, :], in_=neg_tanh[3, 1], func=ACT.Copy, bias=-1.0)
 
-        w2_codes = placed("w2_codes", [P, H_PASSES, N], I32, ring(5))
+        w2_codes = placed("w2_codes", [P, H_PASSES, N], I32, ring(4))
         nc.sync.dma_start(out=w2_codes[:], in_=w2_words.rearrange("a p c i -> p a (c i)").bitcast(I32))
-        w2_planes = placed("w2_planes", [P, H_PASSES * N], U8, ring(5) + 4 * H_PASSES * N)
+        w2_planes = placed("w2_planes", [P, H_PASSES * N], U8, ring(4) + 4 * H_PASSES * N)
         nc.gpsimd.memset(w2_planes[:].bitcast(I32), 0)
         for q in range(QUADRANTS):
             nc.sync.dma_start(
                 out=w2_planes[32 * q : 32 * q + 4, :].bitcast(I32).rearrange("r (a n) -> r a n", a=H_PASSES),
                 in_=w2_scales[:, 4 * q : 4 * q + 4, :].bitcast(I32).rearrange("a r n -> r a n"),
             )
-        weights = placed("weights", [P, S], F32, ring(6) + 4 * KIB)
+        weights = placed("weights", [P, S], F32, ring(1))
         nc.sync.dma_start(out=weights[:], in_=wgo)
         idx2 = keep.tile([P, S // 16], U16, name="idx2")
         nc.sync.dma_start(idx2[:], offs2)
 
-        for i in range(8, 12):
-            scale_h(i, 0)
-        finish(0, last[0][:, :, 1, :], last[0][:, :, 0, :])
-        for i in range(8, 12):
-            scale_h(i, 1)
-        for group in range(EARLY_GROUPS, GROUPS):
+        for t in (2, 3):
+            scale_h(t, 0, 2 + t)
+        quantize_w1(0)
+        finish(0, last[0][:, :, 1, :], GROUPED[0])
+        for t in (2, 3):
+            scale_h(t, 1, 2 + t)
+        for group in range(GROUPS):
             if group == GROUPS - 2:
                 quantize_w1(1)
-                finish(1, shifted[:], placed("z_last", [P, PACK, HALF], F32, GROUPED[1])[:])
-            z_group(0, group, (group - EARLY_GROUPS) % PACK)
+                finish(1, shifted[:], GROUPED[1])
+            z_group(0, group, (6, 7, 0, 1, 2, 3, 2, 3)[group])
         for group in range(GROUPS):
-            z_group(1, group, (4, 5, 6, 7, 2, 3, 0, 1)[group])
+            z_group(1, group, (PACK + group) % BANKS)
         for half in range(HALVES):
             for a in z_order[half]:
                 quantize_z(a, half)

@@ -50,14 +50,14 @@ def ring(n):
     return RING_AT + n * AREA
 
 
-ROW_AT = (ring(0), ring(1), V_AT, V_AT + AREA, ring(3), ring(6), ring(0), ring(1), ring(2), ring(4), ring(5), ring(0))
-WORD_AT = (ring(4), CODES_AT)
-RAW_AT = {(2, 0): ring(2), (2, 1): ring(5), (0, 0): ring(3), (0, 1): ring(6), (1, 0): ring(1), (1, 1): ring(2)}
+ROW_AT = (ring(0), ring(1), V_AT, V_AT + AREA, ring(3), ring(6), ring(0), ring(1), ring(4), ring(3), ring(5), ring(0))
+WORD_AT = (CODES_AT + 2 * KIB, CODES_AT - 6 * KIB)
+RAW_AT = {(2, 0): ring(2), (2, 1): ring(5), (0, 0): ring(2), (0, 1): ring(6), (1, 0): ring(1), (1, 1): ring(4)}
 GROUPED = (GROUPED_AT + AREA, MID_AT, GROUPED_AT)
-W1_CODES_AT = (ring(0) + 4 * KIB, ring(3), CODES_AT)
+W1_CODES_AT = {(0, 0): ring(0) + 4 * KIB, (1, 0): ring(2), (2, 0): CODES_AT + 2 * KIB, (2, 1): CODES_AT}
 SCALED_AT = {(0, 0): ring(5), (0, 1): ring(5) + 4 * KIB, (1, 0): ring(0), (1, 1): CODES_AT + 4 * KIB}
 Z_AT = {
-    (0, 0): ring(3) + 4 * KIB,
+    (0, 0): ring(2) + 4 * KIB,
     (0, 4): ring(6),
     (2, 0): MID_AT + AREA,
     (2, 4): ring(1) + 4 * KIB,
@@ -88,8 +88,10 @@ def tile_list_nack_silu_backward_kernel(tc, tab_words, tab_scales, w1, w2_words,
         idx = keep.tile([P, S // 16], U16, name="idx")
         nc.sync.dma_start(idx[:], offs)
 
-        tab_planes = placed("tab_planes", [P, K_PASSES * T], U8, PLANES_AT)
+        tab_planes = placed("tab_planes", [P, T], U8, PLANES_AT)
         nc.gpsimd.memset(tab_planes[:].bitcast(I32), 0)
+        v_planes = [keep.tile([P, S], U8, name=f"v_plane{g}", align_bytes=64) for g in range(K_PASSES)]
+        nc.gpsimd.memset(v_planes[1][:].bitcast(I32), 0)
 
         pages = [keep.tile([P, T2], F32, name=f"page{n}") for n in range(N_TILES)]
         for page in pages[1:]:
@@ -107,21 +109,24 @@ def tile_list_nack_silu_backward_kernel(tc, tab_words, tab_scales, w1, w2_words,
         w1_codes = {}
         w1_planes = {}
         v_words = {}
-        v_planes = {}
         z_bf = {}
         z_codes = {}
         z_planes = {}
 
-        def load_scales():
-            for q in range(QUADRANTS):
+        def gather_planes():
+            for q in (0, 2, 1, 3):
                 nc.sync.dma_start(
-                    out=tab_planes[32 * q : 32 * q + 4, :].bitcast(I32).rearrange("r (g n) -> r g n", g=K_PASSES),
-                    in_=tab_scales[:, 4 * q : 4 * q + 4, :].bitcast(I32).rearrange("g r n -> r g n"),
+                    out=tab_planes[32 * q : 32 * q + 4 * K_PASSES, :].bitcast(I32),
+                    in_=tab_scales[:, 4 * q : 4 * q + 4, :].bitcast(I32),
                 )
+            nc.vector.tensor_copy(v_planes[0][:], tab_planes[:].indirect(idx[:]))
 
-        def gather_plane(g):
-            v_planes[g] = keep.tile([P, S], U8, name=f"v_plane{g}", align_bytes=64)
-            nc.vector.tensor_copy(v_planes[g][:], tab_planes[:, g * T : (g + 1) * T].indirect(idx[:]))
+        def move_plane():
+            for q in (0, 2, 1, 3):
+                nc.sync.dma_start(
+                    out=v_planes[1][32 * q : 32 * q + 4, :].bitcast(I32),
+                    in_=v_planes[0][32 * q + 4 : 32 * q + 8, :].bitcast(I32),
+                )
 
         def gather_words(g):
             words = placed(f"words{g}", [P, T], I32, WORD_AT[g])
@@ -143,10 +148,16 @@ def tile_list_nack_silu_backward_kernel(tc, tab_words, tab_scales, w1, w2_words,
                 func=ACT.Copy,
             )
 
-        def quantize_w1(a):
-            w1_codes[a] = placed(f"w1_codes{a}", [P, K_PASSES * PASS], U32, W1_CODES_AT[a])
-            w1_planes[a] = keep.tile([P, K_PASSES * PASS], U8, name=f"w1_plane{a}", align_bytes=64)
-            nc.vector.quantize_mx(out=w1_codes[a][:].bitcast(E4M3X4), scales=w1_planes[a][:], in_=grouped[a][:])
+        def quantize_w1(a, passes=range(K_PASSES)):
+            cols = slice(passes.start * PASS, passes.stop * PASS)
+            codes = placed(f"w1_codes{a}{passes.start}", [P, len(passes) * PASS], U32, W1_CODES_AT[a, passes.start])
+            if passes.start == 0:
+                w1_planes[a] = keep.tile([P, K_PASSES * PASS], U8, name=f"w1_plane{a}", align_bytes=64)
+            nc.vector.quantize_mx(
+                out=codes[:].bitcast(E4M3X4), scales=w1_planes[a][:, cols], in_=grouped[a][:, PACK * cols.start : PACK * cols.stop]
+            )
+            for g in passes:
+                w1_codes[a, g] = codes[:, (g - passes.start) * PASS : (g - passes.start + 1) * PASS]
 
         def gather_s(i, half=None):
             a, t = divmod(i, PACK)
@@ -206,7 +217,7 @@ def tile_list_nack_silu_backward_kernel(tc, tab_words, tab_scales, w1, w2_words,
                 w_cols = slice(g * PASS + t * P, g * PASS + (t + 1) * P)
                 nc.tensor.matmul_mx(
                     out=h,
-                    lhsT=w1_codes[a][:, w_cols].bitcast(E4M3X4),
+                    lhsT=w1_codes[a, g][:, t * P : (t + 1) * P].bitcast(E4M3X4),
                     lhsT_scale=w1_planes[a][:, w_cols],
                     rhs=v_words[g][:, cols].bitcast(E5M2X4),
                     rhs_scale=v_planes[g][:, cols],
@@ -297,9 +308,7 @@ def tile_list_nack_silu_backward_kernel(tc, tab_words, tab_scales, w1, w2_words,
         slice_ahead(1)
         gather_s(2)
         activations(2)
-        load_scales()
-        for g in range(K_PASSES):
-            gather_plane(g)
+        gather_planes()
         round_w1(LAST, 0)
         derivative(2, nc.scalar)
         slice_ahead(3)
@@ -307,15 +316,17 @@ def tile_list_nack_silu_backward_kernel(tc, tab_words, tab_scales, w1, w2_words,
         activations(4)
         shift(factors[1][:, 0, :, :], nc.gpsimd)
         gather_words(0)
+        quantize_w1(LAST, range(0, 1))
         round_w1(LAST, 1)
         gather_s(5)
         activations(5)
         gather_words(1)
-        quantize_w1(LAST)
+        quantize_w1(LAST, range(1, 2))
         product(4)
         for half in range(HALVES):
             derivative(5, (nc.gpsimd, nc.scalar)[half], cols_of(half))
         slice_ahead(6)
+        move_plane()
         gather_s(7)
         activations(7)
         derivative(7, nc.gpsimd)
@@ -339,9 +350,9 @@ def tile_list_nack_silu_backward_kernel(tc, tab_words, tab_scales, w1, w2_words,
         nc.scalar.activation(out=shifted[:, :3, :], in_=last[1][:, :3, 1, :], func=ACT.Copy, bias=-1.0)
         nc.scalar.activation(out=shifted[:, 3, :], in_=neg_tanh[3, 1], func=ACT.Copy, bias=-1.0)
 
-        w2_codes = placed("w2_codes", [P, H_PASSES, N], I32, ring(4))
+        w2_codes = placed("w2_codes", [P, H_PASSES, N], I32, ring(3))
         nc.sync.dma_start(out=w2_codes[:], in_=w2_words.rearrange("a p c i -> p a (c i)").bitcast(I32))
-        w2_planes = placed("w2_planes", [P, H_PASSES * N], U8, ring(4) + 4 * H_PASSES * N)
+        w2_planes = placed("w2_planes", [P, H_PASSES * N], U8, ring(3) + 4 * H_PASSES * N)
         nc.gpsimd.memset(w2_planes[:].bitcast(I32), 0)
         for q in range(QUADRANTS):
             nc.sync.dma_start(

@@ -28,21 +28,23 @@ HALVES = S // HALF
 GROUPS = S // GROUP
 N_TILES = N // P
 LIST_COLS = HALF // 16
+LAST = H_PASSES - 1
 RUN = 4
 ODD_SPLIT = T2 // 2 + 1
 BANKS = 8
 BANK_BYTES = 2048
-LAST = H_PASSES - 1
+QUADRANT_TURN = (0, 2, 1, 3)
 
 KIB = 1024
 AREA = 8 * KIB
 FACTORS_AT = 0
-RING_AT = 96 * KIB
+MID_AT = FACTORS_AT + 4 * AREA
+LAST_AT = FACTORS_AT + 8 * AREA
+RING_AT = FACTORS_AT + 12 * AREA
 V_AT = RING_AT + 7 * AREA
 PLANES_AT = V_AT + 2 * AREA
-GROUPED_AT = PLANES_AT + 4 * KIB
-CODES_AT = GROUPED_AT + 2 * AREA
-MID_AT = FACTORS_AT + 4 * AREA
+ROUNDED_AT = PLANES_AT + 4 * KIB
+CODES_AT = ROUNDED_AT + 2 * AREA
 DERIV_AT = PLANES_AT - 4 * KIB
 
 
@@ -52,18 +54,23 @@ def ring(n):
 
 ROW_AT = (ring(0), ring(1), V_AT, V_AT + AREA, ring(3), ring(6), ring(0), ring(1), ring(4), ring(3), ring(5), ring(0))
 WORD_AT = (CODES_AT + 2 * KIB, CODES_AT - 6 * KIB)
-RAW_AT = {(2, 0): ring(2), (2, 1): ring(5), (0, 0): ring(2), (0, 1): ring(6), (1, 0): ring(1), (1, 1): ring(4)}
-GROUPED = (GROUPED_AT + AREA, MID_AT, GROUPED_AT)
+RAW_AT = {(2, 0): ring(2), (2, 1): ring(5), (0, 0): ring(2), (0, 1): ring(6), (1, 0): ring(1), (1, 1): ring(3)}
+ROUNDED = (ROUNDED_AT + AREA, MID_AT, ROUNDED_AT)
 W1_CODES_AT = {(0, 0): ring(0) + 4 * KIB, (1, 0): ring(2), (2, 0): CODES_AT + 2 * KIB, (2, 1): CODES_AT}
-SCALED_AT = {(0, 0): ring(5), (0, 1): ring(5) + 4 * KIB, (1, 0): ring(0), (1, 1): CODES_AT + 4 * KIB}
+SCALED_AT = {(0, 0): ring(4), (0, 1): ring(4) + 2 * KIB, (1, 0): ring(5) + 2 * KIB, (1, 1): ring(5) - 4 * KIB}
+EARLY_TANH_AT = CODES_AT + 4 * KIB
 Z_AT = {
     (0, 0): ring(2) + 4 * KIB,
-    (0, 4): ring(6),
-    (2, 0): MID_AT + AREA,
-    (2, 4): ring(1) + 4 * KIB,
+    (0, 1): ring(6),
     (1, 0): ring(6) + 4 * KIB,
-    (1, 4): V_AT + 4 * KIB,
+    (1, 1): V_AT + 4 * KIB,
+    (2, 0): LAST_AT + 2 * AREA,
+    (2, 1): ring(1) + 4 * KIB,
 }
+W2_AT = MID_AT + 12 * KIB
+FIRST_BANKS = (6, 7, 0, 1, 2, 3, 2, 3)
+Y_BANK = 4
+Z_ORDER = ((0, 2, 1), (0, 1, 2))
 
 
 def tile_list_nack_silu_backward_kernel(tc, tab_words, tab_scales, w1, w2_words, w2_scales, sT, wgo, offs, offs2, out):
@@ -102,10 +109,9 @@ def tile_list_nack_silu_backward_kernel(tc, tab_words, tab_scales, w1, w2_words,
         rows = {}
         factors = {}
         last = {}
-        neg_tanh = {}
         derivs = {}
         scaled = {}
-        grouped = {}
+        rounded = {}
         w1_codes = {}
         w1_planes = {}
         v_words = {}
@@ -114,7 +120,7 @@ def tile_list_nack_silu_backward_kernel(tc, tab_words, tab_scales, w1, w2_words,
         z_planes = {}
 
         def gather_planes():
-            for q in (0, 2, 1, 3):
+            for q in QUADRANT_TURN:
                 nc.sync.dma_start(
                     out=tab_planes[32 * q : 32 * q + 4 * K_PASSES, :].bitcast(I32),
                     in_=tab_scales[:, 4 * q : 4 * q + 4, :].bitcast(I32),
@@ -122,7 +128,7 @@ def tile_list_nack_silu_backward_kernel(tc, tab_words, tab_scales, w1, w2_words,
             nc.vector.tensor_copy(v_planes[0][:], tab_planes[:].indirect(idx[:]))
 
         def move_plane():
-            for q in (0, 2, 1, 3):
+            for q in QUADRANT_TURN:
                 nc.sync.dma_start(
                     out=v_planes[1][32 * q : 32 * q + 4, :].bitcast(I32),
                     in_=v_planes[0][32 * q + 4 : 32 * q + 8, :].bitcast(I32),
@@ -141,59 +147,54 @@ def tile_list_nack_silu_backward_kernel(tc, tab_words, tab_scales, w1, w2_words,
                 in_=w1[g * PASS : (g + 1) * PASS, a * PASS : (a + 1) * PASS].rearrange("(p j) c -> p j c", j=PACK),
             )
             if g == 0:
-                grouped[a] = placed(f"grouped{a}", [P, K_PASSES * PACK * PASS], BF16, GROUPED[a])
+                rounded[a] = placed(f"rounded{a}", [P, K_PASSES * PACK * PASS], BF16, ROUNDED[a])
             nc.scalar.activation(
-                out=grouped[a][:, g * PACK * PASS : (g + 1) * PACK * PASS].rearrange("p (t m j) -> p m j t", t=PACK, j=PACK),
+                out=rounded[a][:, g * PACK * PASS : (g + 1) * PACK * PASS].rearrange("p (t m j) -> p m j t", t=PACK, j=PACK),
                 in_=raw[:].rearrange("p j (m t) -> p m j t", t=PACK),
                 func=ACT.Copy,
             )
 
-        def quantize_w1(a, passes=range(K_PASSES)):
+        def quantize_w1(a, passes):
             cols = slice(passes.start * PASS, passes.stop * PASS)
             codes = placed(f"w1_codes{a}{passes.start}", [P, len(passes) * PASS], U32, W1_CODES_AT[a, passes.start])
             if passes.start == 0:
                 w1_planes[a] = keep.tile([P, K_PASSES * PASS], U8, name=f"w1_plane{a}", align_bytes=64)
             nc.vector.quantize_mx(
-                out=codes[:].bitcast(E4M3X4), scales=w1_planes[a][:, cols], in_=grouped[a][:, PACK * cols.start : PACK * cols.stop]
+                out=codes[:].bitcast(E4M3X4), scales=w1_planes[a][:, cols], in_=rounded[a][:, PACK * cols.start : PACK * cols.stop]
             )
             for g in passes:
                 w1_codes[a, g] = codes[:, (g - passes.start) * PASS : (g - passes.start + 1) * PASS]
 
-        def gather_s(i, half=None):
+        def load_rows(i):
+            a, t = divmod(i, PACK)
+            rows[i] = placed(f"rows{i}", [P, T], F32, ROW_AT[i])
+            nc.sync.dma_start(out=rows[i][:], in_=sT[a * PASS : (a + 1) * PASS, :].rearrange("(p t) n -> p t n", t=PACK)[:, t, :])
+
+        def entries(offsets, half):
+            return offsets[:, half * LIST_COLS : (half + 1) * LIST_COLS]
+
+        def activate(i, offsets, cols):
             a, t = divmod(i, PACK)
             if i not in rows:
-                rows[i] = placed(f"rows{i}", [P, T], F32, ROW_AT[i])
-                nc.sync.dma_start(out=rows[i][:], in_=sT[a * PASS : (a + 1) * PASS, :].rearrange("(p t) n -> p t n", t=PACK)[:, t, :])
+                load_rows(i)
             if a not in factors:
                 factors[a] = placed(f"factors{a}", [P, PACK, 2, S], F32, FACTORS_AT + a * 4 * AREA)
-            if half is None:
-                nc.vector.tensor_copy(factors[a][:, t, 1, :], rows[i][:].indirect(idx[:]))
-            else:
-                offsets = idx[:, half * LIST_COLS : (half + 1) * LIST_COLS]
-                nc.vector.tensor_copy(factors[a][:, t, 1, cols_of(half)], rows[i][:].indirect(offsets))
-
-        def gather_last(t, half):
-            a = LAST
-            i = PACK * a + t
-            if half == 0:
-                rows[i] = placed(f"rows{i}", [P, T], F32, ROW_AT[i])
-                nc.sync.dma_start(out=rows[i][:], in_=sT[a * PASS : (a + 1) * PASS, :].rearrange("(p t) n -> p t n", t=PACK)[:, t, :])
-            if t == 0:
-                last[half] = placed(f"last{half}", [P, PACK, 2, HALF], F32, FACTORS_AT + (a * 4 + half * 2) * AREA)
-            offsets = idx[:, half * LIST_COLS : (half + 1) * LIST_COLS]
-            s = last[half][:, t, 1, :]
-            neg_tanh[t, half] = s
-            if (t, half) == (PACK - 1, HALVES - 1):
-                neg_tanh[t, half] = placed("neg_tanh", [P, HALF], F32, Z_AT[LAST, 0])[:]
-            nc.vector.tensor_copy(s, rows[i][:].indirect(offsets))
-            nc.scalar.activation(out=last[half][:, t, 0, :], in_=s, func=ACT.Silu, scale=-1.0)
-            nc.scalar.activation(out=neg_tanh[t, half], in_=s, func=ACT.Tanh, scale=-0.5)
-
-        def activations(i, cols=slice(0, S)):
-            a, t = divmod(i, PACK)
             s = factors[a][:, t, 1, cols]
+            nc.vector.tensor_copy(s, rows[i][:].indirect(offsets))
             nc.scalar.activation(out=factors[a][:, t, 0, cols], in_=s, func=ACT.Silu, scale=-1.0)
             nc.scalar.activation(out=s, in_=s, func=ACT.Tanh, scale=-0.5)
+
+        def activate_last(t, half):
+            i = PACK * LAST + t
+            if half == 0:
+                load_rows(i)
+            if t == 0:
+                last[half] = placed(f"last{half}", [P, PACK, 2, HALF], F32, LAST_AT + half * 2 * AREA)
+            s = last[half][:, t, 1, :]
+            nc.vector.tensor_copy(s, rows[i][:].indirect(entries(idx, half)))
+            nc.scalar.activation(out=last[half][:, t, 0, :], in_=s, func=ACT.Silu, scale=-1.0)
+            if half == 0:
+                nc.scalar.activation(out=s, in_=s, func=ACT.Tanh, scale=-0.5)
 
         def shift(part, engine):
             if engine is nc.scalar:
@@ -201,13 +202,13 @@ def tile_list_nack_silu_backward_kernel(tc, tab_words, tab_scales, w1, w2_words,
             else:
                 nc.gpsimd.tensor_scalar(part, part, 1.0, -1.0, ALU.mult, ALU.add)
 
-        def product(i, cols=slice(0, S)):
+        def product(i, cols):
             a, t = divmod(i, PACK)
             if a not in derivs:
                 derivs[a] = factors[a][:, :, 0, :] if a == 0 else placed("derivs", [P, PACK, S], F32, DERIV_AT)[:]
             nc.gpsimd.tensor_tensor(derivs[a][:, t, cols], factors[a][:, t, 0, cols], factors[a][:, t, 1, cols], ALU.mult)
 
-        def derivative(i, engine, cols=slice(0, S)):
+        def derivative(i, engine, cols):
             a, t = divmod(i, PACK)
             shift(factors[a][:, t, :, cols], engine)
             product(i, cols)
@@ -226,11 +227,10 @@ def tile_list_nack_silu_backward_kernel(tc, tab_words, tab_scales, w1, w2_words,
                 )
 
         def interleaved(a, group, count):
-            first = max(g for b, g in Z_AT if b == a and g <= group)
-            if (a, first) not in z_bf:
-                end = min([g for b, g in Z_AT if b == a and g > first] + [GROUPS])
-                z_bf[a, first] = placed(f"z{a}{first}", [P, (end - first) * HALF], BF16, Z_AT[a, first])
-            part = z_bf[a, first][:, (group - first) * HALF : (group - first + count) * HALF]
+            half, first = divmod(group, PACK)
+            if (a, half) not in z_bf:
+                z_bf[a, half] = placed(f"z{a}{half}", [P, HALF * PACK], BF16, Z_AT[a, half])
+            part = z_bf[a, half][:, first * GROUP * PACK : (first + count) * GROUP * PACK]
             return part.rearrange("p (c r t) -> p c t r", r=RUN, t=PACK)
 
         def in_runs(part):
@@ -251,35 +251,32 @@ def tile_list_nack_silu_backward_kernel(tc, tab_words, tab_scales, w1, w2_words,
         def scale_h(t, half, bank):
             h = take_bank(bank)
             first_product(h[:], LAST, t, cols_of(half))
-            pair, u = divmod(t, 2)
-            if u == 0:
-                scaled[pair, half] = placed(f"scaled{pair}{half}", [P, 2, HALF], F32, SCALED_AT[pair, half])
+            if t < 2:
+                scaled[t, half] = placed(f"scaled{t}{half}", [P, (1, PACK - 1)[t], HALF], F32, SCALED_AT[t, half])
+            part = scaled[0, half][:, 0, :] if t == 0 else scaled[1, half][:, t - 1, :]
             nc.vector.scalar_tensor_tensor(
-                out=scaled[pair, half][:, u, :], in0=last[half][:, t, 0, :], scalar=1.0, in1=h[:], op0=ALU.subtract, op1=ALU.mult
+                out=part, in0=last[half][:, t, 0, :], scalar=1.0, in1=h[:], op0=ALU.subtract, op1=ALU.mult
             )
 
-        def finish(half, shifted, at):
+        def finish(half, first, rest, at):
             z = placed(f"z_float{half}", [P, PACK, HALF], F32, at)
-            for pair in range(2):
-                nc.gpsimd.tensor_tensor(z[:, 2 * pair : 2 * pair + 2, :], scaled[pair, half][:], shifted[:, 2 * pair : 2 * pair + 2, :], ALU.mult)
+            nc.gpsimd.tensor_tensor(z[:, :1, :], scaled[0, half][:], first, ALU.mult)
+            nc.gpsimd.tensor_tensor(z[:, 1:, :], scaled[1, half][:], rest, ALU.mult)
+            return z
+
+        def interleave(half, z):
             nc.scalar.activation(out=interleaved(LAST, PACK * half, PACK), in_=in_runs(z[:]), func=ACT.Copy)
 
         def quantize_z(a, half):
             codes = placed(f"z_codes{a}{half}", [P, HALF], U32, DERIV_AT + 2 * KIB * (HALVES * a + half))
             plane = keep.tile([P, HALF], U8, name=f"z_plane{a}{half}", align_bytes=64)
-            for (b, first), z in z_bf.items():
-                if b == a and first // PACK == half:
-                    c0 = first % PACK * GROUP
-                    cols = slice(c0, c0 + z.shape[1] // PACK)
-                    nc.vector.quantize_mx(out=codes[:, cols].bitcast(E4M3X4), scales=plane[:, cols], in_=z[:])
+            nc.vector.quantize_mx(out=codes[:].bitcast(E4M3X4), scales=plane[:], in_=z_bf[a, half][:])
             z_codes[a, half] = codes
             z_planes[a, half] = plane
 
-        z_order = ((0, 2, 1), (0, 1, 2))
-
         def weigh_and_place(n, half):
-            y = take_bank(PACK)
-            for k, a in enumerate(z_order[half]):
+            y = take_bank(Y_BANK)
+            for k, a in enumerate(Z_ORDER[half]):
                 nc.tensor.matmul_mx(
                     out=y[:],
                     lhsT=w2_codes[:, a, n * P : (n + 1) * P].bitcast(E4M3X4),
@@ -291,94 +288,96 @@ def tile_list_nack_silu_backward_kernel(tc, tab_words, tab_scales, w1, w2_words,
                 )
             y_sb = placed(f"y_sb{n}{half}", [P, HALF], F32, FACTORS_AT + 2 * KIB * (N_TILES * half + n))
             nc.scalar.activation(out=y_sb[:], in_=y[:], func=ACT.Copy, scale=0.5)
-            places = pages[n][:].indirect(idx2[:, half * LIST_COLS : (half + 1) * LIST_COLS])
+            places = pages[n][:].indirect(entries(idx2, half))
             nc.vector.tensor_tensor(places, y_sb[:], weights[:, cols_of(half)], ALU.mult)
             if half == HALVES - 1:
                 nc.sync.dma_start(out=out[n * P : (n + 1) * P, :], in_=pages[n][:])
 
-        def slice_ahead(i, engine=nc.gpsimd):
-            gather_s(i)
-            activations(i)
-            derivative(i, engine)
+        whole = slice(0, S)
+        by_half = (nc.gpsimd, nc.scalar)
 
         for half in range(HALVES):
-            gather_s(0, half)
-            activations(0, cols_of(half))
-            derivative(0, (nc.gpsimd, nc.scalar)[half], cols_of(half))
-        slice_ahead(1)
-        gather_s(2)
-        activations(2)
+            activate(0, entries(idx, half), cols_of(half))
+            derivative(0, by_half[half], cols_of(half))
+        activate(1, idx[:], whole)
+        derivative(1, nc.gpsimd, whole)
+        activate(2, idx[:], whole)
         gather_planes()
         round_w1(LAST, 0)
-        derivative(2, nc.scalar)
-        slice_ahead(3)
-        gather_s(4)
-        activations(4)
+        derivative(2, nc.scalar, whole)
+        activate(3, idx[:], whole)
+        derivative(3, nc.gpsimd, whole)
+        activate(4, idx[:], whole)
         shift(factors[1][:, 0, :, :], nc.gpsimd)
         gather_words(0)
         quantize_w1(LAST, range(0, 1))
         round_w1(LAST, 1)
-        gather_s(5)
-        activations(5)
+        activate(5, idx[:], whole)
         gather_words(1)
         quantize_w1(LAST, range(1, 2))
-        product(4)
+        product(4, whole)
         for half in range(HALVES):
-            derivative(5, (nc.gpsimd, nc.scalar)[half], cols_of(half))
-        slice_ahead(6)
+            derivative(5, by_half[half], cols_of(half))
+        activate(6, idx[:], whole)
+        derivative(6, nc.gpsimd, whole)
         move_plane()
-        gather_s(7)
-        activations(7)
-        derivative(7, nc.gpsimd)
+        activate(7, idx[:], whole)
+        derivative(7, nc.gpsimd, whole)
+
         for half in range(HALVES):
-            gather_last(0, half)
+            activate_last(0, half)
+        early_tanh = placed("early_tanh", [P, 1, HALF], F32, EARLY_TANH_AT)
+        nc.scalar.activation(out=early_tanh[:, 0, :], in_=last[1][:, 0, 1, :], func=ACT.Tanh, scale=-0.5)
+        for half in range(HALVES):
+            scale_h(0, half, half)
         round_w1(0, 0)
         for t in (1, 2):
             for half in range(HALVES):
-                gather_last(t, half)
+                activate_last(t, half)
         for half in range(HALVES):
-            for t in range(2):
-                scale_h(t, half, 2 * half + t)
+            scale_h(1, half, 2 + half)
+        scale_h(2, 0, 4)
         round_w1(0, 1)
-        shift(last[0][:, :3, 1, :], nc.gpsimd)
-        for half in range(HALVES):
-            gather_last(3, half)
-        shift(last[0][:, 3, 1, :], nc.gpsimd)
+        shift(early_tanh[:], nc.gpsimd)
+        shift(last[0][:, : PACK - 1, 1, :], nc.gpsimd)
+        activate_last(PACK - 1, 0)
+        shift(last[0][:, PACK - 1, 1, :], nc.scalar)
+        activate_last(PACK - 1, 1)
         for g in range(K_PASSES):
             round_w1(1, g)
-        shifted = placed("shifted", [P, PACK, HALF], F32, RAW_AT[1, 1])
-        nc.scalar.activation(out=shifted[:, :3, :], in_=last[1][:, :3, 1, :], func=ACT.Copy, bias=-1.0)
-        nc.scalar.activation(out=shifted[:, 3, :], in_=neg_tanh[3, 1], func=ACT.Copy, bias=-1.0)
+        late_tanh = placed("late_tanh", [P, PACK - 1, HALF], F32, RAW_AT[1, 1])
+        nc.scalar.activation(out=late_tanh[:], in_=last[1][:, 1:, 1, :], func=ACT.Tanh, scale=-0.5)
+        shift(late_tanh[:], nc.scalar)
 
-        w2_codes = placed("w2_codes", [P, H_PASSES, N], I32, ring(3))
+        w2_codes = placed("w2_codes", [P, H_PASSES, N], I32, W2_AT)
         nc.sync.dma_start(out=w2_codes[:], in_=w2_words.rearrange("a p c i -> p a (c i)").bitcast(I32))
-        w2_planes = placed("w2_planes", [P, H_PASSES * N], U8, ring(3) + 4 * H_PASSES * N)
+        w2_planes = placed("w2_planes", [P, H_PASSES * N], U8, W2_AT + 4 * H_PASSES * N)
         nc.gpsimd.memset(w2_planes[:].bitcast(I32), 0)
         for q in range(QUADRANTS):
             nc.sync.dma_start(
                 out=w2_planes[32 * q : 32 * q + 4, :].bitcast(I32).rearrange("r (a n) -> r a n", a=H_PASSES),
                 in_=w2_scales[:, 4 * q : 4 * q + 4, :].bitcast(I32).rearrange("a r n -> r a n"),
             )
-        weights = placed("weights", [P, S], F32, ring(1))
+        weights = placed("weights", [P, S], F32, RAW_AT[1, 0])
         nc.sync.dma_start(out=weights[:], in_=wgo)
         idx2 = keep.tile([P, S // 16], U16, name="idx2")
         nc.sync.dma_start(idx2[:], offs2)
 
-        for t in (2, 3):
-            scale_h(t, 0, 2 + t)
-        quantize_w1(0)
-        finish(0, last[0][:, :, 1, :], GROUPED[0])
-        for t in (2, 3):
-            scale_h(t, 1, 2 + t)
+        scale_h(3, 0, 5)
+        quantize_w1(0, range(K_PASSES))
+        z_float = finish(0, last[0][:, :1, 1, :], last[0][:, 1:, 1, :], ROUNDED[0])
+        scale_h(3, 1, 4)
+        scale_h(2, 1, 5)
+        interleave(0, z_float)
         for group in range(GROUPS):
             if group == GROUPS - 2:
-                quantize_w1(1)
-                finish(1, shifted[:], GROUPED[1])
-            z_group(0, group, (6, 7, 0, 1, 2, 3, 2, 3)[group])
+                quantize_w1(1, range(K_PASSES))
+                interleave(1, finish(1, early_tanh[:], late_tanh[:], ROUNDED[1]))
+            z_group(0, group, FIRST_BANKS[group])
         for group in range(GROUPS):
             z_group(1, group, (PACK + group) % BANKS)
         for half in range(HALVES):
-            for a in z_order[half]:
+            for a in Z_ORDER[half]:
                 quantize_z(a, half)
         for half in range(HALVES):
             for n in range(N_TILES):

@@ -328,6 +328,8 @@ def tile_list_nack_silu_backward_kernel(tc, tab_words, tab_scales, w1, w2_words,
             activate_last(0, half)
         early_tanh = placed("early_tanh", [P, 1, HALF], F32, EARLY_TANH_AT)
         nc.scalar.activation(out=early_tanh[:, 0, :], in_=last[1][:, 0, 1, :], func=ACT.Tanh, scale=-0.5)
+        shift(early_tanh[:], nc.scalar)
+        shift(last[0][:, 0, 1, :], nc.scalar)
         for half in range(HALVES):
             scale_h(0, half, half)
         round_w1(0, 0)
@@ -338,8 +340,7 @@ def tile_list_nack_silu_backward_kernel(tc, tab_words, tab_scales, w1, w2_words,
             scale_h(1, half, 2 + half)
         scale_h(2, 0, 4)
         round_w1(0, 1)
-        shift(early_tanh[:], nc.gpsimd)
-        shift(last[0][:, : PACK - 1, 1, :], nc.gpsimd)
+        shift(last[0][:, 1 : PACK - 1, 1, :], nc.gpsimd)
         activate_last(PACK - 1, 0)
         shift(last[0][:, PACK - 1, 1, :], nc.scalar)
         activate_last(PACK - 1, 1)

from contextlib import ExitStack

import concourse.mybir as mybir

K, H, N, T, S, T2 = 1024, 1536, 512, 2048, 1024, 2048
FLOPS = 2 * K * H * S + 2 * H * N * S

F32 = mybir.dt.float32
BF16 = mybir.dt.bfloat16
I32 = mybir.dt.int32
U32 = mybir.dt.uint32
U16 = mybir.dt.uint16
U8 = mybir.dt.uint8
E4M3X4 = mybir.dt.float8_e4m3fn_x4
E5M2X4 = mybir.dt.float8_e5m2_x4
ACT = mybir.ActivationFunctionType
ALU = mybir.AluOpType

P = 128
PACK = 4
PASS = P * PACK
QUADRANTS = 4
HALF = 512
GROUP = HALF // PACK
K_PASSES = K // PASS
H_PASSES = H // PASS
HALVES = S // HALF
GROUPS = S // GROUP
N_TILES = N // P
LIST_COLS = HALF // 16
LAST = H_PASSES - 1
RUN = 4
ODD_SPLIT = T2 // 2 + 1
BANKS = 8
BANK_BYTES = 2048
QUADRANT_TURN = (0, 2, 1, 3)

KIB = 1024
AREA = 8 * KIB
FACTORS_AT = 0
MID_AT = FACTORS_AT + 4 * AREA
LAST_AT = FACTORS_AT + 8 * AREA
RING_AT = FACTORS_AT + 12 * AREA
V_AT = RING_AT + 7 * AREA
PLANES_AT = V_AT + 2 * AREA
ROUNDED_AT = PLANES_AT + 4 * KIB
CODES_AT = ROUNDED_AT + 2 * AREA
DERIV_AT = PLANES_AT - 4 * KIB


def ring(n):
    return RING_AT + n * AREA


ROW_AT = (ring(0), ring(1), V_AT, V_AT + AREA, ring(3), ring(6), ring(0), ring(1), ring(4), ring(3), ring(5), ring(0))
WORD_AT = (CODES_AT + 2 * KIB, CODES_AT - 6 * KIB)
RAW_AT = {(2, 0): ring(2), (2, 1): ring(5), (0, 0): ring(2), (0, 1): ring(6), (1, 0): ring(1), (1, 1): ring(3)}
ROUNDED = (ROUNDED_AT + AREA, MID_AT, ROUNDED_AT)
W1_CODES_AT = {(0, 0): ring(0) + 4 * KIB, (1, 0): ring(2), (2, 0): CODES_AT + 2 * KIB, (2, 1): CODES_AT}
SCALED_AT = {(0, 0): ring(4), (0, 1): ring(4) + 2 * KIB, (1, 0): ring(5) + 2 * KIB, (1, 1): ring(5) - 4 * KIB}
EARLY_TANH_AT = CODES_AT + 4 * KIB
Z_AT = {
    (0, 0): ring(2) + 4 * KIB,
    (0, 1): ring(6),
    (1, 0): ring(6) + 4 * KIB,
    (1, 1): V_AT + 4 * KIB,
    (2, 0): LAST_AT + 2 * AREA,
    (2, 1): ring(1) + 4 * KIB,
}
W2_AT = MID_AT + 12 * KIB
FIRST_BANKS = (6, 7, 0, 1, 2, 3, 2, 3)
Y_BANK = 4
Z_ORDER = ((0, 2, 1), (0, 1, 2))


def tile_list_nack_silu_backward_kernel(tc, tab_words, tab_scales, w1, w2_words, w2_scales, sT, wgo, offs, offs2, out):
    nc = tc.nc
    with ExitStack() as ctx:
        keep = ctx.enter_context(tc.tile_pool(name="keep", bufs=1))
        arena = ctx.enter_context(tc.tile_pool(name="arena", bufs=1))
        psum = ctx.enter_context(tc.psum_pool(name="psum", bufs=1))

        def placed(name, shape, dtype, offset):
            return arena.tile(shape, dtype, name=name, offset=offset, align_bytes=64)

        banks_taken = []

        def take_bank(bank):
            banks_taken.append(bank)
            return psum.tile([P, HALF], F32, name=f"bank{len(banks_taken)}", offset=BANK_BYTES * bank)

        def cols_of(half):
            return slice(half * HALF, (half + 1) * HALF)

        idx = keep.tile([P, S // 16], U16, name="idx")
        nc.sync.dma_start(idx[:], offs)

        tab_planes = placed("tab_planes", [P, T], U8, PLANES_AT)
        nc.gpsimd.memset(tab_planes[:].bitcast(I32), 0)
        v_planes = [keep.tile([P, S], U8, name=f"v_plane{g}", align_bytes=64) for g in range(K_PASSES)]
        nc.gpsimd.memset(v_planes[1][:].bitcast(I32), 0)

        pages = [keep.tile([P, T2], F32, name=f"page{n}") for n in range(N_TILES)]
        for page in pages[1:]:
            nc.gpsimd.memset(page[:], 0.0)
        nc.vector.memset(pages[0][:, :ODD_SPLIT], 0.0)
        nc.vector.memset(pages[0][:, ODD_SPLIT:], 0.0)

        rows = {}
        factors = {}
        last = {}
        derivs = {}
        scaled = {}
        rounded = {}
        w1_codes = {}
        w1_planes = {}
        v_words = {}
        z_bf = {}
        z_codes = {}
        z_planes = {}

        def gather_planes():
            for q in QUADRANT_TURN:
                nc.sync.dma_start(
                    out=tab_planes[32 * q : 32 * q + 4 * K_PASSES, :].bitcast(I32),
                    in_=tab_scales[:, 4 * q : 4 * q + 4, :].bitcast(I32),
                )
            nc.vector.tensor_copy(v_planes[0][:], tab_planes[:].indirect(idx[:]))

        def move_plane():
            for q in QUADRANT_TURN:
                nc.sync.dma_start(
                    out=v_planes[1][32 * q : 32 * q + 4, :].bitcast(I32),
                    in_=v_planes[0][32 * q + 4 : 32 * q + 8, :].bitcast(I32),
                )

        def gather_words(g):
            words = placed(f"words{g}", [P, T], I32, WORD_AT[g])
            nc.sync.dma_start(out=words[:], in_=tab_words[g].rearrange("p t i -> p (t i)").bitcast(I32))
            v_words[g] = placed(f"v_words{g}", [P, S], U32, V_AT + g * AREA)
            nc.vector.tensor_copy(v_words[g][:], words[:].bitcast(U32).indirect(idx[:]))

        def round_w1(a, g):
            raw = placed(f"raw{a}{g}", [P, PACK, PASS], F32, RAW_AT[a, g])
            nc.sync.dma_start(
                out=raw[:],
                in_=w1[g * PASS : (g + 1) * PASS, a * PASS : (a + 1) * PASS].rearrange("(p j) c -> p j c", j=PACK),
            )
            if g == 0:
                rounded[a] = placed(f"rounded{a}", [P, K_PASSES * PACK * PASS], BF16, ROUNDED[a])
            nc.scalar.activation(
                out=rounded[a][:, g * PACK * PASS : (g + 1) * PACK * PASS].rearrange("p (t m j) -> p m j t", t=PACK, j=PACK),
                in_=raw[:].rearrange("p j (m t) -> p m j t", t=PACK),
                func=ACT.Copy,
            )

        def quantize_w1(a, passes):
            cols = slice(passes.start * PASS, passes.stop * PASS)
            codes = placed(f"w1_codes{a}{passes.start}", [P, len(passes) * PASS], U32, W1_CODES_AT[a, passes.start])
            if passes.start == 0:
                w1_planes[a] = keep.tile([P, K_PASSES * PASS], U8, name=f"w1_plane{a}", align_bytes=64)
            nc.vector.quantize_mx(
                out=codes[:].bitcast(E4M3X4), scales=w1_planes[a][:, cols], in_=rounded[a][:, PACK * cols.start : PACK * cols.stop]
            )
            for g in passes:
                w1_codes[a, g] = codes[:, (g - passes.start) * PASS : (g - passes.start + 1) * PASS]

        def load_rows(i):
            a, t = divmod(i, PACK)
            rows[i] = placed(f"rows{i}", [P, T], F32, ROW_AT[i])
            nc.sync.dma_start(out=rows[i][:], in_=sT[a * PASS : (a + 1) * PASS, :].rearrange("(p t) n -> p t n", t=PACK)[:, t, :])

        def entries(offsets, half):
            return offsets[:, half * LIST_COLS : (half + 1) * LIST_COLS]

        def activate(i, offsets, cols):
            a, t = divmod(i, PACK)
            if i not in rows:
                load_rows(i)
            if a not in factors:
                factors[a] = placed(f"factors{a}", [P, PACK, 2, S], F32, FACTORS_AT + a * 4 * AREA)
            s = factors[a][:, t, 1, cols]
            nc.vector.tensor_copy(s, rows[i][:].indirect(offsets))
            nc.scalar.activation(out=factors[a][:, t, 0, cols], in_=s, func=ACT.Silu, scale=-1.0)
            nc.scalar.activation(out=s, in_=s, func=ACT.Tanh, scale=-0.5)

        def activate_last(t, half):
            i = PACK * LAST + t
            if half == 0:
                load_rows(i)
            if t == 0:
                last[half] = placed(f"last{half}", [P, PACK, 2, HALF], F32, LAST_AT + half * 2 * AREA)
            s = last[half][:, t, 1, :]
            nc.vector.tensor_copy(s, rows[i][:].indirect(entries(idx, half)))
            nc.scalar.activation(out=last[half][:, t, 0, :], in_=s, func=ACT.Silu, scale=-1.0)
            if half == 0:
                nc.scalar.activation(out=s, in_=s, func=ACT.Tanh, scale=-0.5)

        def shift(part, engine):
            if engine is nc.scalar:
                nc.scalar.activation(out=part, in_=part, func=ACT.Copy, bias=-1.0)
            else:
                nc.gpsimd.tensor_scalar(part, part, 1.0, -1.0, ALU.mult, ALU.add)

        def product(i, cols):
            a, t = divmod(i, PACK)
            if a not in derivs:
                derivs[a] = factors[a][:, :, 0, :] if a == 0 else placed("derivs", [P, PACK, S], F32, DERIV_AT)[:]
            nc.gpsimd.tensor_tensor(derivs[a][:, t, cols], factors[a][:, t, 0, cols], factors[a][:, t, 1, cols], ALU.mult)

        def derivative(i, engine, cols):
            a, t = divmod(i, PACK)
            shift(factors[a][:, t, :, cols], engine)
            product(i, cols)

        def first_product(h, a, t, cols):
            for g in range(K_PASSES):
                w_cols = slice(g * PASS + t * P, g * PASS + (t + 1) * P)
                nc.tensor.matmul_mx(
                    out=h,
                    lhsT=w1_codes[a, g][:, t * P : (t + 1) * P].bitcast(E4M3X4),
                    lhsT_scale=w1_planes[a][:, w_cols],
                    rhs=v_words[g][:, cols].bitcast(E5M2X4),
                    rhs_scale=v_planes[g][:, cols],
                    start=(g == 0),
                    stop=(g == K_PASSES - 1),
                )

        def interleaved(a, group, count):
            half, first = divmod(group, PACK)
            if (a, half) not in z_bf:
                z_bf[a, half] = placed(f"z{a}{half}", [P, HALF * PACK], BF16, Z_AT[a, half])
            part = z_bf[a, half][:, first * GROUP * PACK : (first + count) * GROUP * PACK]
            return part.rearrange("p (c r t) -> p c t r", r=RUN, t=PACK)

        def in_runs(part):
            return part.rearrange("p t (c r) -> p c t r", r=RUN)

        def z_group(a, group, bank):
            cols = slice(group * GROUP, (group + 1) * GROUP)
            h = take_bank(bank)
            for t in range(PACK):
                first_product(h[:, t * GROUP : (t + 1) * GROUP], a, t, cols)
            nc.vector.tensor_tensor(
                out=interleaved(a, group, 1),
                in0=in_runs(h[:].rearrange("p (t c) -> p t c", t=PACK)),
                in1=in_runs(derivs[a][:, :, cols]),
                op=ALU.mult,
            )

        def scale_h(t, half, bank):
            h = take_bank(bank)
            first_product(h[:], LAST, t, cols_of(half))
            if t < 2:
                scaled[t, half] = placed(f"scaled{t}{half}", [P, (1, PACK - 1)[t], HALF], F32, SCALED_AT[t, half])
            part = scaled[0, half][:, 0, :] if t == 0 else scaled[1, half][:, t - 1, :]
            nc.vector.scalar_tensor_tensor(
                out=part, in0=last[half][:, t, 0, :], scalar=1.0, in1=h[:], op0=ALU.subtract, op1=ALU.mult
            )

        def finish(half, first, rest, at):
            z = placed(f"z_float{half}", [P, PACK, HALF], F32, at)
            nc.gpsimd.tensor_tensor(z[:, :1, :], scaled[0, half][:], first, ALU.mult)
            nc.gpsimd.tensor_tensor(z[:, 1:, :], scaled[1, half][:], rest, ALU.mult)
            return z

        def interleave(half, z):
            nc.scalar.activation(out=interleaved(LAST, PACK * half, PACK), in_=in_runs(z[:]), func=ACT.Copy)

        def quantize_z(a, half):
            codes = placed(f"z_codes{a}{half}", [P, HALF], U32, DERIV_AT + 2 * KIB * (HALVES * a + half))
            plane = keep.tile([P, HALF], U8, name=f"z_plane{a}{half}", align_bytes=64)
            nc.vector.quantize_mx(out=codes[:].bitcast(E4M3X4), scales=plane[:], in_=z_bf[a, half][:])
            z_codes[a, half] = codes
            z_planes[a, half] = plane

        def weigh_and_place(n, half):
            y = take_bank(Y_BANK)
            for k, a in enumerate(Z_ORDER[half]):
                nc.tensor.matmul_mx(
                    out=y[:],
                    lhsT=w2_codes[:, a, n * P : (n + 1) * P].bitcast(E4M3X4),
                    lhsT_scale=w2_planes[:, a * N + n * P : a * N + (n + 1) * P],
                    rhs=z_codes[a, half][:].bitcast(E4M3X4),
                    rhs_scale=z_planes[a, half][:],
                    start=(k == 0),
                    stop=(k == H_PASSES - 1),
                )
            y_sb = placed(f"y_sb{n}{half}", [P, HALF], F32, FACTORS_AT + 2 * KIB * (N_TILES * half + n))
            nc.scalar.activation(out=y_sb[:], in_=y[:], func=ACT.Copy, scale=0.5)
            places = pages[n][:].indirect(entries(idx2, half))
            nc.vector.tensor_tensor(places, y_sb[:], weights[:, cols_of(half)], ALU.mult)
            if half == HALVES - 1:
                nc.sync.dma_start(out=out[n * P : (n + 1) * P, :], in_=pages[n][:])

        whole = slice(0, S)
        by_half = (nc.gpsimd, nc.scalar)

        for half in range(HALVES):
            activate(0, entries(idx, half), cols_of(half))
            derivative(0, by_half[half], cols_of(half))
        activate(1, idx[:], whole)
        derivative(1, nc.gpsimd, whole)
        activate(2, idx[:], whole)
        gather_planes()
        round_w1(LAST, 0)
        derivative(2, nc.scalar, whole)
        activate(3, idx[:], whole)
        derivative(3, nc.gpsimd, whole)
        activate(4, idx[:], whole)
        shift(factors[1][:, 0, :, :], nc.gpsimd)
        gather_words(0)
        quantize_w1(LAST, range(0, 1))
        round_w1(LAST, 1)
        activate(5, idx[:], whole)
        gather_words(1)
        quantize_w1(LAST, range(1, 2))
        product(4, whole)
        for half in range(HALVES):
            derivative(5, by_half[half], cols_of(half))
        activate(6, idx[:], whole)
        derivative(6, nc.gpsimd, whole)
        move_plane()
        activate(7, idx[:], whole)
        derivative(7, nc.gpsimd, whole)

        for half in range(HALVES):
            activate_last(0, half)
        early_tanh = placed("early_tanh", [P, 1, HALF], F32, EARLY_TANH_AT)
        nc.scalar.activation(out=early_tanh[:, 0, :], in_=last[1][:, 0, 1, :], func=ACT.Tanh, scale=-0.5)
        shift(early_tanh[:], nc.scalar)
        shift(last[0][:, 0, 1, :], nc.scalar)
        for half in range(HALVES):
            scale_h(0, half, half)
        round_w1(0, 0)
        for t in (1, 2):
            for half in range(HALVES):
                activate_last(t, half)
        for half in range(HALVES):
            scale_h(1, half, 2 + half)
        scale_h(2, 0, 4)
        round_w1(0, 1)
        shift(last[0][:, 1 : PACK - 1, 1, :], nc.gpsimd)
        activate_last(PACK - 1, 0)
        shift(last[0][:, PACK - 1, 1, :], nc.scalar)
        activate_last(PACK - 1, 1)
        for g in range(K_PASSES):
            round_w1(1, g)
        late_tanh = placed("late_tanh", [P, PACK - 1, HALF], F32, RAW_AT[1, 1])
        nc.scalar.activation(out=late_tanh[:], in_=last[1][:, 1:, 1, :], func=ACT.Tanh, scale=-0.5)
        shift(late_tanh[:], nc.scalar)

        w2_codes = placed("w2_codes", [P, H_PASSES, N], I32, W2_AT)
        nc.sync.dma_start(out=w2_codes[:], in_=w2_words.rearrange("a p c i -> p a (c i)").bitcast(I32))
        w2_planes = placed("w2_planes", [P, H_PASSES * N], U8, W2_AT + 4 * H_PASSES * N)
        nc.gpsimd.memset(w2_planes[:].bitcast(I32), 0)
        for q in range(QUADRANTS):
            nc.sync.dma_start(
                out=w2_planes[32 * q : 32 * q + 4, :].bitcast(I32).rearrange("r (a n) -> r a n", a=H_PASSES),
                in_=w2_scales[:, 4 * q : 4 * q + 4, :].bitcast(I32).rearrange("a r n -> r a n"),
            )
        weights = placed("weights", [P, S], F32, RAW_AT[1, 0])
        nc.sync.dma_start(out=weights[:], in_=wgo)
        idx2 = keep.tile([P, S // 16], U16, name="idx2")
        nc.sync.dma_start(idx2[:], offs2)

        scale_h(3, 0, 5)
        quantize_w1(0, range(K_PASSES))
        z_float = finish(0, last[0][:, :1, 1, :], last[0][:, 1:, 1, :], ROUNDED[0])
        scale_h(3, 1, 4)
        scale_h(2, 1, 5)
        interleave(0, z_float)
        for group in range(GROUPS):
            if group == GROUPS - 2:
                quantize_w1(1, range(K_PASSES))
                interleave(1, finish(1, early_tanh[:], late_tanh[:], ROUNDED[1]))
            z_group(0, group, FIRST_BANKS[group])
        for group in range(GROUPS):
            z_group(1, group, (PACK + group) % BANKS)
        for half in range(HALVES):
            for a in Z_ORDER[half]:
                quantize_z(a, half)
        for half in range(HALVES):
            for n in range(N_TILES):
                weigh_and_place(n, half)
